import numpy as np
import ml_dtypes


def mxq(x, axis, fmt="e4m3"):
    dtype, down = {"e4m3": (ml_dtypes.float8_e4m3fn, 7), "e5m2": (ml_dtypes.float8_e5m2, 14)}[fmt]
    v = np.moveaxis(np.asarray(x, np.float32).astype(ml_dtypes.bfloat16).astype(np.float64), axis, -1)
    blocks = v.reshape(v.shape[:-1] + (-1, 32))
    amax = np.abs(blocks).max(-1, keepdims=True)
    byte = np.maximum(np.where(amax > 0, np.frexp(amax)[1] - 1 + 127, 0) - down, 1)
    scale = np.exp2(byte - 127.0)
    codes = (blocks / scale).astype(np.float32).astype(dtype).astype(np.float64)
    return np.moveaxis((codes * scale).reshape(v.shape), -1, axis)


WIDE = False


def mx_kscale(k):
    if not WIDE:
        return np.ones(k)
    levels = np.array([18, -18])
    if k % 512:
        return np.exp2(np.random.permutation(np.resize(levels, k // 32))).repeat(32)
    a = np.empty((k // 512, 16))
    for p in range(k // 512):
        a[p, :8] = np.random.permutation(np.resize(levels, 8))
        for g in range(8):
            far = levels[np.abs(levels - a[p, g]) >= 10]
            a[p, g + 8] = far[np.random.randint(len(far))]
    return np.exp2(a.ravel()).repeat(32)


def f64(x):
    return np.asarray(x).astype(np.float64)


def striped(idx):
    return np.tile(np.asarray(idx).reshape(-1, 16).T, (8, 1)).astype(np.uint16)


def unstriped(offs):
    return offs[:16].T.reshape(-1).astype(np.int64)


B, N, T, D, R = 1, 512, 2048, 512, 1024


def setup_inputs():
    n = np.random.standard_normal
    idx = np.random.permutation(T)[:B * N]
    s = mx_kscale(D)[:, None]
    z = mx_kscale(R)[:, None]
    u = np.ones(T)
    u[idx] = mx_kscale(B * N)
    r = np.random.uniform(0.5, 2.0, T) * u
    x = n((B, D, R))
    return {
        "xT": (x * s).astype(np.float32),
        "wT": (n((D, T)) * (1.00 / np.sqrt(D)) / s / r).astype(np.float32),
        "y": np.random.randint(0, 2, (B, R, N)).astype(np.float32),
        "wt": (np.random.uniform(0.5, 1.5, (B, R, 1)) * 1.0 / np.sqrt(R) * z).astype(np.float32),
        "ts": np.tile(r, (128, 1)).astype(np.float32),
        "kb": np.tile(0.5 * n(T), (128, 1)).astype(np.float32),
        "xm": (x.transpose(0, 2, 1) / z).astype(np.float32),
        "offs": striped(idx),
    }


def reference(xT, wT, y, wt, ts, kb, xm, offs):
    idx = unstriped(offs)
    pick = lambda x: x[:, idx].reshape(x.shape[0], B, N).transpose(1, 0, 2)
    w = pick(f64(wT))
    a = mxq(f64(xT), 1, "e4m3").transpose(0, 2, 1) @ mxq(w, 1, "e4m3")
    ts_ = pick(f64(ts))[:, :1, :]
    a = a * ts_
    a = a + pick(f64(kb))[:, :1, :]
    g = f64(wt) * (1.0 / (1.0 + np.exp(-a)) - f64(y))
    g = g * ts_
    dw = mxq(f64(xm), 1, "e4m3").transpose(0, 2, 1) @ mxq(g, 1, "e5m2")
    gw = np.zeros((D, T))
    gw[:, idx] = dw.transpose(1, 0, 2).reshape(D, B * N)
    gx = mxq(g, 2, "e5m2") @ mxq(w, 2, "e4m3").transpose(0, 2, 1)
    return gw, gx

@@ -1,0 +1,295 @@
+from contextlib import ExitStack
+
+import concourse.mybir as mybir
+from concourse.masks import make_identity
+
+N, T, D, R = 512, 2048, 512, 1024
+FLOPS = 3 * 2 * R * D * N
+
+F32 = mybir.dt.float32
+BF16 = mybir.dt.bfloat16
+U32 = mybir.dt.uint32
+U16 = mybir.dt.uint16
+U8 = mybir.dt.uint8
+E4M3 = mybir.dt.float8_e4m3fn_x4
+E5M2 = mybir.dt.float8_e5m2_x4
+ACT = mybir.ActivationFunctionType
+ALU = mybir.AluOpType
+
+P = 128
+PACK = 4
+K_PASS = P * PACK
+HALVES = R // K_PASS
+BLOCKS = N // P
+
+
+def tile_attend_gnce_wx_ts_kb_kernel(tc, xT, wT, y, wt, ts, kb, xm, offs, out_0, out_1):
+    nc = tc.nc
+    with ExitStack() as ctx:
+        keep = ctx.enter_context(tc.tile_pool(name="keep", bufs=1))
+        ring = ctx.enter_context(tc.tile_pool(name="ring", bufs=3))
+        psum = ctx.enter_context(tc.psum_pool(name="psum", bufs=1))
+
+        def bank(tag, bufs):
+            return psum.tile([P, K_PASS], F32, name=tag, tag=tag, bufs=bufs)
+
+        def mx_tiles(name, width):
+            codes = keep.tile([P, width], U32, name=name + "_codes", align_bytes=64)
+            scales = keep.tile([P, width], U8, name=name + "_scales", align_bytes=64)
+            return codes, scales
+
+        def quantize(mx, cols, grouped, fmt):
+            nc.vector.quantize_mx(out=mx[0][:, cols].bitcast(fmt), scales=mx[1][:, cols], in_=grouped)
+
+        def matmul(out, lhs, lhs_cols, lhs_fmt, rhs, rhs_fmt, start, stop):
+            nc.tensor.matmul_mx(
+                out=out,
+                lhsT=lhs[0][:, lhs_cols].bitcast(lhs_fmt),
+                lhsT_scale=lhs[1][:, lhs_cols],
+                rhs=rhs[0][:].bitcast(rhs_fmt),
+                rhs_scale=rhs[1][:],
+                start=start,
+                stop=stop,
+            )
+
+        def interleave(copy, grouped, raw):
+            copy(
+                out=grouped[:].rearrange("p (c i) j -> p c j i", i=4),
+                in_=raw[:].rearrange("p j (c i) -> p c j i", i=4),
+            )
+
+        offsets = keep.tile([P, N // 16], U16, name="offsets")
+        nc.sync.dma_start(offsets[:], offs)
+
+        ts_table = keep.tile([P, T], F32, name="ts_table")
+        kb_table = keep.tile([P, T], F32, name="kb_table")
+        nc.vector.memset(ts_table[:], 0.0)
+        nc.vector.memset(kb_table[:], 0.0)
+        wt_rows = keep.tile([P, HALVES, PACK], F32, name="wt_rows")
+        nc.scalar.dma_start(out=wt_rows[:], in_=wt[0].rearrange("(g p j) o -> p g (j o)", g=HALVES, j=PACK))
+        nc.scalar.dma_start(out=ts_table[0:1, :], in_=ts[0:1, :])
+        nc.scalar.dma_start(out=kb_table[0:1, :], in_=kb[0:1, :])
+
+        x_raw = [keep.tile([P, PACK, K_PASS], F32, name=f"x_raw{g}") for g in range(HALVES)]
+        y_raw = [keep.tile([P, PACK, N], F32, name=f"y_raw{g}") for g in range(HALVES)]
+        xm_raw = [keep.tile([P, PACK, D], F32, name=f"xm_raw{g}") for g in range(HALVES)]
+        w_table = [keep.tile([P, T], F32, name=f"w_table{j}") for j in range(PACK)]
+        x_hbm = xT[0].rearrange("(p j) (g r) -> g p j r", j=PACK, g=HALVES)
+        y_hbm = y[0].rearrange("(g p j) i -> g p j i", j=PACK, g=HALVES)
+        xm_hbm = xm[0].rearrange("(g p j) d -> g p j d", j=PACK, g=HALVES)
+        w_hbm = wT.rearrange("(p j) t -> j p t", j=PACK)
+        nc.sync.dma_start(out=x_raw[0][:], in_=x_hbm[0])
+        for j in range(PACK):
+            nc.sync.dma_start(out=w_table[j][:], in_=w_hbm[j])
+        nc.sync.dma_start(out=y_raw[0][:], in_=y_hbm[0])
+        nc.sync.dma_start(out=x_raw[1][:], in_=x_hbm[1])
+        nc.sync.dma_start(out=y_raw[1][:], in_=y_hbm[1])
+        for g in range(HALVES):
+            nc.sync.dma_start(out=xm_raw[g][:], in_=xm_hbm[g])
+
+        ident = keep.tile([P, P], F32, name="ident")
+        make_identity(nc, ident[:])
+
+        warm = keep.tile([P, 1], F32, name="warm")
+        nc.scalar.activation(out=warm[:], in_=ident[:, 0:1], func=ACT.Sigmoid)
+
+        windows = [keep.tile([P, T], F32, name=f"window{c}") for c in range(D // P)]
+        for window in windows:
+            nc.gpsimd.memset(window[:], 0.0)
+
+        wt_free = []
+        for g in range(HALVES):
+            turned = bank("turn", 3)
+            for j in range(PACK):
+                nc.tensor.transpose(turned[:, j * P : (j + 1) * P], wt_rows[:, g, j : j + 1].to_broadcast([P, P]), ident[:])
+            wide = keep.tile([P, K_PASS], F32, name=f"wt_free{g}")
+            nc.scalar.copy(
+                out=wide[:].rearrange("q (u p e) -> q u p e", u=2, e=2),
+                in_=turned[:].rearrange("q (u e p) -> q u p e", u=2, e=2),
+            )
+            wt_free.append(wide)
+
+        x_mx = [mx_tiles(f"x{g}", K_PASS) for g in range(HALVES)]
+        x_grouped = [keep.tile([P, K_PASS, PACK], BF16, name=f"x_grouped{g}", align_bytes=64) for g in range(HALVES)]
+        whole = slice(0, K_PASS)
+
+        def flat(grouped):
+            return grouped[:].rearrange("p c j -> p (c j)")
+
+        interleave(nc.scalar.copy, x_grouped[0], x_raw[0])
+
+        per_slot = []
+        for name, table in (("ts", ts_table), ("kb", kb_table)):
+            picked = keep.tile([P, N], F32, name=name + "_picked")
+            nc.vector.tensor_copy(picked[:], table[:].indirect(offsets[:]))
+            turned = bank("turn", 3)
+            for t in range(BLOCKS):
+                nc.tensor.transpose(turned[:, t * P : (t + 1) * P], picked[:, t * P : (t + 1) * P], ident[:])
+            column = keep.tile([P, BLOCKS], F32, name=name + "_slot")
+            nc.scalar.copy(out=column[:], in_=turned[:, 0 : N : P])
+            per_slot.append(column)
+        ts_slot, kb_slot = per_slot
+
+        quantize(x_mx[0], whole, flat(x_grouped[0]), E4M3)
+
+        w_grouped = keep.tile([P, N, PACK], BF16, name="w_grouped", align_bytes=64)
+        w_mx = mx_tiles("w", N)
+        for j in range(PACK - 1):
+            nc.vector.tensor_copy(w_grouped[:, :, j], w_table[j][:].indirect(offsets[:]))
+        for half in range(2):
+            slots = slice(half * N // 2, (half + 1) * N // 2)
+            nc.vector.tensor_copy(
+                w_grouped[:, slots, PACK - 1],
+                w_table[PACK - 1][:].indirect(offsets[:, half * 16 : (half + 1) * 16]),
+            )
+        for half in range(2):
+            slots = slice(half * N // 2, (half + 1) * N // 2)
+            quantize(w_mx, slots, w_grouped[:, slots, :].rearrange("p c j -> p (c j)"), E4M3)
+
+        h_rows = [keep.tile([P, N, PACK], BF16, name=f"h_rows{g}", align_bytes=64) for g in range(HALVES)]
+        h_rows_mx = [mx_tiles(f"h_rows{g}", N) for g in range(HALVES)]
+        xm_mx = [mx_tiles(f"xm{g}", D) for g in range(HALVES)]
+        xm_grouped = [keep.tile([P, D, PACK], BF16, name=f"xm_grouped{g}", align_bytes=64) for g in range(HALVES)]
+        diffs = {}
+        turned_h = {}
+
+        def difference(g, t):
+            slots = slice(t * P, (t + 1) * P)
+            scores = bank("mm", 3)
+            matmul(scores[:], w_mx, slots, E4M3, x_mx[g], E4M3, True, True)
+            labels = bank("turn", 3)
+            for j in range(PACK):
+                nc.tensor.transpose(labels[:, j * P : (j + 1) * P], y_raw[g][:, j, slots], ident[:])
+            prob = ring.tile([P, K_PASS], F32, name="prob")
+            nc.scalar.activation(
+                out=prob[:].rearrange("m (u p e) -> m u p e", u=2, e=2),
+                in_=scores[:].rearrange("m (p u e) -> m u p e", u=2, e=2),
+                func=ACT.Sigmoid,
+                bias=kb_slot[:, t : t + 1],
+                scale=ts_slot[:, t : t + 1],
+            )
+            diff = ring.tile([P, K_PASS], F32, name="diff")
+            nc.vector.tensor_tensor(
+                out=diff[:].rearrange("m (u p e) -> m u p e", u=2, e=2),
+                in0=prob[:].rearrange("m (u p e) -> m u p e", u=2, e=2),
+                in1=labels[:].rearrange("m (u e p) -> m u p e", u=2, e=2),
+                op=ALU.subtract,
+            )
+            diffs[g, t] = diff
+
+        def weigh(g, t):
+            h_slots = ring.tile([P, K_PASS], BF16, name="h_slots")
+            nc.vector.scalar_tensor_tensor(
+                out=h_slots[:],
+                in0=diffs[g, t][:],
+                scalar=ts_slot[:, t : t + 1],
+                in1=wt_free[g][:],
+                op0=ALU.mult,
+                op1=ALU.mult,
+            )
+            if t % 2 == 0:
+                turned_h[g, t // 2] = bank("pairs", 2)
+            turned = turned_h[g, t // 2]
+            words = h_slots[:].bitcast(F32)
+            for u in range(2):
+                first = u * 2 * P + (t % 2) * P
+                nc.tensor.transpose(turned[:, first : first + P], words[:, u * P : (u + 1) * P], ident[:])
+            if t % 2 == 1:
+                pair = slice((t - 1) * P, (t + 1) * P)
+                grouped = h_rows[g][:, pair, :].rearrange("p i j -> p (i j)")
+                nc.scalar.copy(
+                    out=grouped.bitcast(F32).rearrange("p (i u) -> p i u", u=2),
+                    in_=turned[:].rearrange("p (u i) -> p i u", u=2),
+                )
+
+        def quantize_rows(g, half):
+            pair = slice(half * 2 * P, (half + 1) * 2 * P)
+            quantize(h_rows_mx[g], pair, h_rows[g][:, pair, :].rearrange("p i j -> p (i j)"), E5M2)
+
+        units = [(g, t) for g in range(HALVES) for t in range(BLOCKS)]
+        difference(*units[0])
+        for n, unit in enumerate(units):
+            if n == 1:
+                interleave(nc.scalar.copy, x_grouped[1], x_raw[1])
+            if n == 2:
+                quantize(x_mx[1], whole, flat(x_grouped[1]), E4M3)
+            if n + 1 < len(units):
+                difference(*units[n + 1])
+            weigh(*unit)
+            if n in (3, 5):
+                quantize_rows(*divmod((n - 3) // 2, 2))
+            if n == 4:
+                interleave(nc.scalar.copy, xm_grouped[0], xm_raw[0])
+            if n == 6:
+                interleave(nc.vector.tensor_copy, xm_grouped[1], xm_raw[1])
+                quantize(xm_mx[0], whole, flat(xm_grouped[0]), E4M3)
+        quantize_rows(1, 0)
+        quantize(xm_mx[1], whole, flat(xm_grouped[1]), E4M3)
+        quantize_rows(1, 1)
+
+        def table_gradient(c):
+            rows = slice(c * P, (c + 1) * P)
+            acc = bank("mm", 3)
+            for g in range(HALVES):
+                matmul(acc[:], xm_mx[g], rows, E4M3, h_rows_mx[g], E5M2, g == 0, g == HALVES - 1)
+            dense = ring.tile([P, N], F32, name="dense")
+            nc.scalar.copy(out=dense[:], in_=acc[:])
+            nc.vector.tensor_copy(windows[c][:].indirect(offsets[:]), dense[:])
+            nc.sync.dma_start(out=out_0[rows, :], in_=windows[c][:])
+
+        def turn_slots(grouped_words, u, order, dest):
+            turned = bank("turn", 3)
+            for t in range(PACK):
+                nc.tensor.transpose(turned[:, t * P : (t + 1) * P], grouped_words[:, 2 * t + u : 2 * N : 2 * PACK], ident[:])
+            nc.scalar.copy(
+                out=dest.rearrange(f"m ({order}) t -> m {order} t", e=2),
+                in_=turned[:].bitcast(BF16).rearrange(f"m (t p e) -> m {order} t", t=PACK, e=2),
+            )
+
+        w_slots = keep.tile([P, D, PACK], BF16, name="w_slots", align_bytes=64)
+        w_slots_mx = mx_tiles("w_slots", D)
+        h_cols = [keep.tile([P, K_PASS, PACK], BF16, name=f"h_cols{g}", align_bytes=64) for g in range(HALVES)]
+        h_cols_mx = [mx_tiles(f"h_cols{g}", K_PASS) for g in range(HALVES)]
+        out_1_hbm = out_1[0].rearrange("(g p u e) d -> g u p e d", g=HALVES, u=2, e=2)
+
+        def turn_w():
+            for u in range(2):
+                turn_slots(flat(w_grouped).bitcast(F32), u, "p e", w_slots[:, u * 2 * P : (u + 1) * 2 * P, :])
+
+        def turn_h(g, u):
+            turn_slots(flat(h_rows[g]).bitcast(F32), u, "e p", h_cols[g][:, u * 2 * P : (u + 1) * 2 * P, :])
+
+        def quantize_cols(g, u):
+            cols = slice(u * 2 * P, (u + 1) * 2 * P)
+            quantize(h_cols_mx[g], cols, h_cols[g][:, cols, :].rearrange("p c j -> p (c j)"), E5M2)
+
+        def row_gradient(g, u):
+            staged = ring.tile([P, 2, D], F32, name="staged")
+            for e in range(2):
+                first = (2 * u + e) * P
+                acc = bank("mm", 3)
+                matmul(acc[:], h_cols_mx[g], slice(first, first + P), E5M2, w_slots_mx, E4M3, True, True)
+                nc.scalar.copy(
+                    out=staged[:, e, :].rearrange("r (p u e) -> r p u e", u=2, e=2),
+                    in_=acc[:].rearrange("r (u p e) -> r p u e", u=2, e=2),
+                )
+            nc.sync.dma_start(out=out_1_hbm[g, u], in_=staged[:])
+
+        table_gradient(0)
+        turn_w()
+        turn_h(0, 0)
+        table_gradient(1)
+        quantize(w_slots_mx, whole, flat(w_slots), E4M3)
+        quantize_cols(0, 0)
+        turn_h(0, 1)
+        row_gradient(0, 0)
+        turn_h(1, 0)
+        table_gradient(2)
+        quantize_cols(0, 1)
+        quantize_cols(1, 0)
+        turn_h(1, 1)
+        row_gradient(0, 1)
+        row_gradient(1, 0)
+        quantize_cols(1, 1)
+        table_gradient(3)
+        row_gradient(1, 1)

@@ -30,8 +30,7 @@ def tile_attend_gnce_wx_ts_kb_kernel(tc, xT, wT, y, wt, ts, kb, xm, offs, out_0,
         ring = ctx.enter_context(tc.tile_pool(name="ring", bufs=3))
         psum = ctx.enter_context(tc.psum_pool(name="psum", bufs=1))
 
-        def bank(tag, bufs):
-            return psum.tile([P, K_PASS], F32, name=tag, tag=tag, bufs=bufs)
+        banks = [psum.tile([P, K_PASS], F32, name=f"bank{b}") for b in range(8)]
 
         def mx_tiles(name, width):
             codes = keep.tile([P, width], U32, name=name + "_codes", align_bytes=64)
@@ -52,10 +51,10 @@ def tile_attend_gnce_wx_ts_kb_kernel(tc, xT, wT, y, wt, ts, kb, xm, offs, out_0,
                 stop=stop,
             )
 
-        def interleave(copy, grouped, raw):
+        def interleave(copy, grouped, raw, cols):
             copy(
-                out=grouped[:].rearrange("p (c i) j -> p c j i", i=4),
-                in_=raw[:].rearrange("p j (c i) -> p c j i", i=4),
+                out=grouped[:, cols, :].rearrange("p (c i) j -> p c j i", i=4),
+                in_=raw[:, :, cols].rearrange("p j (c i) -> p c j i", i=4),
             )
 
         offsets = keep.tile([P, N // 16], U16, name="offsets")
@@ -63,26 +62,34 @@ def tile_attend_gnce_wx_ts_kb_kernel(tc, xT, wT, y, wt, ts, kb, xm, offs, out_0,
 
         ts_table = keep.tile([P, T], F32, name="ts_table")
         kb_table = keep.tile([P, T], F32, name="kb_table")
-        nc.vector.memset(ts_table[:], 0.0)
-        nc.vector.memset(kb_table[:], 0.0)
+        for table in (ts_table, kb_table):
+            nc.vector.memset(table[:], 0.0)
         wt_rows = keep.tile([P, HALVES, PACK], F32, name="wt_rows")
         nc.scalar.dma_start(out=wt_rows[:], in_=wt[0].rearrange("(g p j) o -> p g (j o)", g=HALVES, j=PACK))
-        nc.scalar.dma_start(out=ts_table[0:1, :], in_=ts[0:1, :])
-        nc.scalar.dma_start(out=kb_table[0:1, :], in_=kb[0:1, :])
 
         x_raw = [keep.tile([P, PACK, K_PASS], F32, name=f"x_raw{g}") for g in range(HALVES)]
-        y_raw = [keep.tile([P, PACK, N], F32, name=f"y_raw{g}") for g in range(HALVES)]
+        y_raw = [keep.tile([P, PACK, N], F32, name=f"y_raw{g}", tag=f"y_raw{g}") for g in range(HALVES)]
         xm_raw = [keep.tile([P, PACK, D], F32, name=f"xm_raw{g}") for g in range(HALVES)]
-        w_table = [keep.tile([P, T], F32, name=f"w_table{j}") for j in range(PACK)]
+        w_table = [keep.tile([P, T], F32, name=f"w_table{j}", tag=f"w_table{j}") for j in range(PACK)]
         x_hbm = xT[0].rearrange("(p j) (g r) -> g p j r", j=PACK, g=HALVES)
         y_hbm = y[0].rearrange("(g p j) i -> g p j i", j=PACK, g=HALVES)
         xm_hbm = xm[0].rearrange("(g p j) d -> g p j d", j=PACK, g=HALVES)
         w_hbm = wT.rearrange("(p j) t -> j p t", j=PACK)
-        nc.sync.dma_start(out=x_raw[0][:], in_=x_hbm[0])
-        for j in range(PACK):
-            nc.sync.dma_start(out=w_table[j][:], in_=w_hbm[j])
-        nc.sync.dma_start(out=y_raw[0][:], in_=y_hbm[0])
-        nc.sync.dma_start(out=x_raw[1][:], in_=x_hbm[1])
+        loads = [
+            (x_raw[0][:], x_hbm[0]),
+            (ts_table[0:1, :], ts[0:1, :]),
+            (x_raw[1][:], x_hbm[1]),
+            (kb_table[0:1, :], kb[0:1, :]),
+            (w_table[0][:], w_hbm[0]),
+            (w_table[1][:], w_hbm[1]),
+            (w_table[2][:], w_hbm[2]),
+            (w_table[3][:], w_hbm[3]),
+        ]
+        for dest, source in loads:
+            nc.sync.dma_start(out=dest, in_=source)
+        for half in range(2):
+            cols = slice(half * N // 2, (half + 1) * N // 2)
+            nc.sync.dma_start(out=y_raw[0][:, :, cols], in_=y_hbm[0][:, :, cols])
         nc.sync.dma_start(out=y_raw[1][:], in_=y_hbm[1])
         for g in range(HALVES):
             nc.sync.dma_start(out=xm_raw[g][:], in_=xm_hbm[g])
@@ -93,13 +100,19 @@ def tile_attend_gnce_wx_ts_kb_kernel(tc, xT, wT, y, wt, ts, kb, xm, offs, out_0,
         warm = keep.tile([P, 1], F32, name="warm")
         nc.scalar.activation(out=warm[:], in_=ident[:, 0:1], func=ACT.Sigmoid)
 
-        windows = [keep.tile([P, T], F32, name=f"window{c}") for c in range(D // P)]
+        windows = [keep.tile([P, T], F32, name=f"window{c}") for c in range(3)]
         for window in windows:
-            nc.gpsimd.memset(window[:], 0.0)
+            nc.vector.memset(window[:], 0.0)
+
+        def late_window(tag):
+            window = keep.tile([P, T], F32, name=f"window{len(windows)}", tag=tag)
+            for first in range(0, T, K_PASS):
+                nc.gpsimd.memset(window[:, first : first + K_PASS], 0.0)
+            windows.append(window)
 
         wt_free = []
         for g in range(HALVES):
-            turned = bank("turn", 3)
+            turned = banks[3 + g]
             for j in range(PACK):
                 nc.tensor.transpose(turned[:, j * P : (j + 1) * P], wt_rows[:, g, j : j + 1].to_broadcast([P, P]), ident[:])
             wide = keep.tile([P, K_PASS], F32, name=f"wt_free{g}")
@@ -116,13 +129,12 @@ def tile_attend_gnce_wx_ts_kb_kernel(tc, xT, wT, y, wt, ts, kb, xm, offs, out_0,
         def flat(grouped):
             return grouped[:].rearrange("p c j -> p (c j)")
 
-        interleave(nc.scalar.copy, x_grouped[0], x_raw[0])
+        interleave(nc.scalar.copy, x_grouped[0], x_raw[0], whole)
 
         per_slot = []
-        for name, table in (("ts", ts_table), ("kb", kb_table)):
+        for name, table, turned in (("ts", ts_table, banks[5]), ("kb", kb_table, banks[3])):
             picked = keep.tile([P, N], F32, name=name + "_picked")
             nc.vector.tensor_copy(picked[:], table[:].indirect(offsets[:]))
-            turned = bank("turn", 3)
             for t in range(BLOCKS):
                 nc.tensor.transpose(turned[:, t * P : (t + 1) * P], picked[:, t * P : (t + 1) * P], ident[:])
             column = keep.tile([P, BLOCKS], F32, name=name + "_slot")
@@ -142,8 +154,6 @@ def tile_attend_gnce_wx_ts_kb_kernel(tc, xT, wT, y, wt, ts, kb, xm, offs, out_0,
                 w_grouped[:, slots, PACK - 1],
                 w_table[PACK - 1][:].indirect(offsets[:, half * 16 : (half + 1) * 16]),
             )
-        for half in range(2):
-            slots = slice(half * N // 2, (half + 1) * N // 2)
             quantize(w_mx, slots, w_grouped[:, slots, :].rearrange("p c j -> p (c j)"), E4M3)
 
         h_rows = [keep.tile([P, N, PACK], BF16, name=f"h_rows{g}", align_bytes=64) for g in range(HALVES)]
@@ -151,16 +161,14 @@ def tile_attend_gnce_wx_ts_kb_kernel(tc, xT, wT, y, wt, ts, kb, xm, offs, out_0,
         xm_mx = [mx_tiles(f"xm{g}", D) for g in range(HALVES)]
         xm_grouped = [keep.tile([P, D, PACK], BF16, name=f"xm_grouped{g}", align_bytes=64) for g in range(HALVES)]
         diffs = {}
-        turned_h = {}
 
-        def difference(g, t):
+        probs = {}
+
+        def score(g, t):
             slots = slice(t * P, (t + 1) * P)
-            scores = bank("mm", 3)
+            scores = banks[(BLOCKS * g + t) % 3]
             matmul(scores[:], w_mx, slots, E4M3, x_mx[g], E4M3, True, True)
-            labels = bank("turn", 3)
-            for j in range(PACK):
-                nc.tensor.transpose(labels[:, j * P : (j + 1) * P], y_raw[g][:, j, slots], ident[:])
-            prob = ring.tile([P, K_PASS], F32, name="prob")
+            prob = ring.tile([P, K_PASS], F32, name="prob", bufs=4)
             nc.scalar.activation(
                 out=prob[:].rearrange("m (u p e) -> m u p e", u=2, e=2),
                 in_=scores[:].rearrange("m (p u e) -> m u p e", u=2, e=2),
@@ -168,29 +176,39 @@ def tile_attend_gnce_wx_ts_kb_kernel(tc, xT, wT, y, wt, ts, kb, xm, offs, out_0,
                 bias=kb_slot[:, t : t + 1],
                 scale=ts_slot[:, t : t + 1],
             )
+            probs[g, t] = prob
+
+        def turn_labels(g, t):
+            labels = banks[3 + (BLOCKS * g + t) % 3]
+            for j in range(PACK):
+                nc.tensor.transpose(labels[:, j * P : (j + 1) * P], y_raw[g][:, j, t * P : (t + 1) * P], ident[:])
+
+        def difference(g, t):
+            labels = banks[3 + (BLOCKS * g + t) % 3]
             diff = ring.tile([P, K_PASS], F32, name="diff")
             nc.vector.tensor_tensor(
                 out=diff[:].rearrange("m (u p e) -> m u p e", u=2, e=2),
-                in0=prob[:].rearrange("m (u p e) -> m u p e", u=2, e=2),
+                in0=probs[g, t][:].rearrange("m (u p e) -> m u p e", u=2, e=2),
                 in1=labels[:].rearrange("m (u e p) -> m u p e", u=2, e=2),
                 op=ALU.subtract,
             )
             diffs[g, t] = diff
 
         def weigh(g, t):
-            h_slots = ring.tile([P, K_PASS], BF16, name="h_slots")
+            if (g, t) == units[-1]:
+                h_slots = flat(h_cols[0])[:, 5 * K_PASS // 4 : 9 * K_PASS // 4]
+            else:
+                h_slots = ring.tile([P, K_PASS], BF16, name="h_slots")[:]
             nc.vector.scalar_tensor_tensor(
-                out=h_slots[:],
+                out=h_slots,
                 in0=diffs[g, t][:],
                 scalar=ts_slot[:, t : t + 1],
                 in1=wt_free[g][:],
                 op0=ALU.mult,
                 op1=ALU.mult,
             )
-            if t % 2 == 0:
-                turned_h[g, t // 2] = bank("pairs", 2)
-            turned = turned_h[g, t // 2]
-            words = h_slots[:].bitcast(F32)
+            turned = banks[6 + t // 2]
+            words = h_slots.bitcast(F32)
             for u in range(2):
                 first = u * 2 * P + (t % 2) * P
                 nc.tensor.transpose(turned[:, first : first + P], words[:, u * P : (u + 1) * P], ident[:])
@@ -206,39 +224,21 @@ def tile_attend_gnce_wx_ts_kb_kernel(tc, xT, wT, y, wt, ts, kb, xm, offs, out_0,
             pair = slice(half * 2 * P, (half + 1) * 2 * P)
             quantize(h_rows_mx[g], pair, h_rows[g][:, pair, :].rearrange("p i j -> p (i j)"), E5M2)
 
-        units = [(g, t) for g in range(HALVES) for t in range(BLOCKS)]
-        difference(*units[0])
-        for n, unit in enumerate(units):
-            if n == 1:
-                interleave(nc.scalar.copy, x_grouped[1], x_raw[1])
-            if n == 2:
-                quantize(x_mx[1], whole, flat(x_grouped[1]), E4M3)
-            if n + 1 < len(units):
-                difference(*units[n + 1])
-            weigh(*unit)
-            if n in (3, 5):
-                quantize_rows(*divmod((n - 3) // 2, 2))
-            if n == 4:
-                interleave(nc.scalar.copy, xm_grouped[0], xm_raw[0])
-            if n == 6:
-                interleave(nc.vector.tensor_copy, xm_grouped[1], xm_raw[1])
-                quantize(xm_mx[0], whole, flat(xm_grouped[0]), E4M3)
-        quantize_rows(1, 0)
-        quantize(xm_mx[1], whole, flat(xm_grouped[1]), E4M3)
-        quantize_rows(1, 1)
+        products = {}
 
-        def table_gradient(c):
+        def table_product(c, acc):
             rows = slice(c * P, (c + 1) * P)
-            acc = bank("mm", 3)
             for g in range(HALVES):
                 matmul(acc[:], xm_mx[g], rows, E4M3, h_rows_mx[g], E5M2, g == 0, g == HALVES - 1)
-            dense = ring.tile([P, N], F32, name="dense")
+            dense = ring.tile([P, N], F32, name="dense", bufs=4)
             nc.scalar.copy(out=dense[:], in_=acc[:])
-            nc.vector.tensor_copy(windows[c][:].indirect(offsets[:]), dense[:])
-            nc.sync.dma_start(out=out_0[rows, :], in_=windows[c][:])
+            products[c] = dense
 
-        def turn_slots(grouped_words, u, order, dest):
-            turned = bank("turn", 3)
+        def place(c):
+            nc.vector.tensor_copy(windows[c][:].indirect(offsets[:]), products[c][:])
+            nc.sync.dma_start(out=out_0[c * P : (c + 1) * P, :], in_=windows[c][:])
+
+        def turn_slots(turned, grouped_words, u, order, dest):
             for t in range(PACK):
                 nc.tensor.transpose(turned[:, t * P : (t + 1) * P], grouped_words[:, 2 * t + u : 2 * N : 2 * PACK], ident[:])
             nc.scalar.copy(
@@ -252,44 +252,83 @@ def tile_attend_gnce_wx_ts_kb_kernel(tc, xT, wT, y, wt, ts, kb, xm, offs, out_0,
         h_cols_mx = [mx_tiles(f"h_cols{g}", K_PASS) for g in range(HALVES)]
         out_1_hbm = out_1[0].rearrange("(g p u e) d -> g u p e d", g=HALVES, u=2, e=2)
 
-        def turn_w():
-            for u in range(2):
-                turn_slots(flat(w_grouped).bitcast(F32), u, "p e", w_slots[:, u * 2 * P : (u + 1) * 2 * P, :])
+        def turn_w(turned, u):
+            turn_slots(turned, flat(w_grouped).bitcast(F32), u, "p e", w_slots[:, u * 2 * P : (u + 1) * 2 * P, :])
 
-        def turn_h(g, u):
-            turn_slots(flat(h_rows[g]).bitcast(F32), u, "e p", h_cols[g][:, u * 2 * P : (u + 1) * 2 * P, :])
+        def turn_h(turned, g, u):
+            turn_slots(turned, flat(h_rows[g]).bitcast(F32), u, "e p", h_cols[g][:, u * 2 * P : (u + 1) * 2 * P, :])
 
         def quantize_cols(g, u):
             cols = slice(u * 2 * P, (u + 1) * 2 * P)
             quantize(h_cols_mx[g], cols, h_cols[g][:, cols, :].rearrange("p c j -> p (c j)"), E5M2)
 
-        def row_gradient(g, u):
-            staged = ring.tile([P, 2, D], F32, name="staged")
+        def row_gradient(g, u, accs):
+            staged = ring.tile([P, 2, D], F32, name="staged", bufs=4)
             for e in range(2):
                 first = (2 * u + e) * P
-                acc = bank("mm", 3)
+                acc = accs[e]
                 matmul(acc[:], h_cols_mx[g], slice(first, first + P), E5M2, w_slots_mx, E4M3, True, True)
                 nc.scalar.copy(
                     out=staged[:, e, :].rearrange("r (p u e) -> r p u e", u=2, e=2),
                     in_=acc[:].rearrange("r (u p e) -> r p u e", u=2, e=2),
                 )
-            nc.sync.dma_start(out=out_1_hbm[g, u], in_=staged[:])
+            nc.scalar.dma_start(out=out_1_hbm[g, u], in_=staged[:])
 
-        table_gradient(0)
-        turn_w()
-        turn_h(0, 0)
-        table_gradient(1)
+        units = [(g, t) for g in range(HALVES) for t in range(BLOCKS)]
+        halves = [slice(0, K_PASS // 2), slice(K_PASS // 2, K_PASS)]
+        pieces = [slice(first, first + 256) for first in range(0, D, 256)]
+        for cols in halves:
+            interleave(nc.scalar.copy, x_grouped[1], x_raw[1], cols)
+        quantize(x_mx[1], whole, flat(x_grouped[1]), E4M3)
+        turn_w(banks[6], 0)
+        late_window("w_table3")
+        for unit in units[:3]:
+            score(*unit)
+        turn_labels(*units[0])
+        difference(*units[0])
+        turn_labels(*units[1])
+        for n, unit in enumerate(units):
+            if n + 3 < len(units):
+                score(*units[n + 3])
+            if n + 2 < len(units):
+                turn_labels(*units[n + 2])
+            if n + 1 < len(units):
+                difference(*units[n + 1])
+            if n == -1:
+                turn_w(banks[7], 1)
+            weigh(*unit)
+            if n == 3:
+                turn_w(banks[7], 1)
+            if n in (3, 5):
+                quantize_rows(*divmod((n - 3) // 2, 2))
+        quantize_rows(1, 1)
+        quantize_rows(1, 0)
+        for g in range(HALVES):
+            for n, cols in enumerate(pieces):
+                on_vector = g * len(pieces) + n >= 3
+                interleave(nc.vector.tensor_copy if on_vector else nc.scalar.copy, xm_grouped[g], xm_raw[g], cols)
+        for g in range(HALVES):
+            for cols in halves:
+                quantize(xm_mx[g], cols, xm_grouped[g][:, cols, :].rearrange("p c j -> p (c j)"), E4M3)
+
+        table_product(0, banks[0])
+        place(0)
+        turn_h(banks[2], 0, 0)
+        turn_h(banks[3], 0, 1)
         quantize(w_slots_mx, whole, flat(w_slots), E4M3)
         quantize_cols(0, 0)
-        turn_h(0, 1)
-        row_gradient(0, 0)
-        turn_h(1, 0)
-        table_gradient(2)
         quantize_cols(0, 1)
+        table_product(1, banks[1])
+        place(1)
+        row_gradient(0, 0, banks[2:4])
+        row_gradient(0, 1, banks[4:6])
+        turn_h(banks[2], 1, 0)
+        turn_h(banks[3], 1, 1)
         quantize_cols(1, 0)
-        turn_h(1, 1)
-        row_gradient(0, 1)
-        row_gradient(1, 0)
         quantize_cols(1, 1)
-        table_gradient(3)
-        row_gradient(1, 1)
+        table_product(2, banks[2])
+        place(2)
+        row_gradient(1, 0, banks[0:2])
+        table_product(3, banks[3])
+        place(3)
+        row_gradient(1, 1, banks[4:6])

@@ -32,8 +32,8 @@ def tile_attend_gnce_wx_ts_kb_kernel(tc, xT, wT, y, wt, ts, kb, xm, offs, out_0,
 
         banks = [psum.tile([P, K_PASS], F32, name=f"bank{b}") for b in range(8)]
 
-        def mx_tiles(name, width):
-            codes = keep.tile([P, width], U32, name=name + "_codes", align_bytes=64)
+        def mx_tiles(name, width, tag=""):
+            codes = keep.tile([P, width], U32, name=name + "_codes", tag=tag, align_bytes=64)
             scales = keep.tile([P, width], U8, name=name + "_scales", align_bytes=64)
             return codes, scales
 
@@ -67,32 +67,31 @@ def tile_attend_gnce_wx_ts_kb_kernel(tc, xT, wT, y, wt, ts, kb, xm, offs, out_0,
         wt_rows = keep.tile([P, HALVES, PACK], F32, name="wt_rows")
         nc.scalar.dma_start(out=wt_rows[:], in_=wt[0].rearrange("(g p j) o -> p g (j o)", g=HALVES, j=PACK))
 
-        x_raw = [keep.tile([P, PACK, K_PASS], F32, name=f"x_raw{g}") for g in range(HALVES)]
+        x_raw = [keep.tile([P, PACK, K_PASS], F32, name=f"x_raw{g}", tag=f"x_raw{g}") for g in range(HALVES)]
         y_raw = [keep.tile([P, PACK, N], F32, name=f"y_raw{g}", tag=f"y_raw{g}") for g in range(HALVES)]
-        xm_raw = [keep.tile([P, PACK, D], F32, name=f"xm_raw{g}") for g in range(HALVES)]
+        xm_raw = [keep.tile([P, PACK, D], F32, name=f"xm_raw{g}", tag=f"xm_raw{g}") for g in range(HALVES)]
         w_table = [keep.tile([P, T], F32, name=f"w_table{j}", tag=f"w_table{j}") for j in range(PACK)]
         x_hbm = xT[0].rearrange("(p j) (g r) -> g p j r", j=PACK, g=HALVES)
         y_hbm = y[0].rearrange("(g p j) i -> g p j i", j=PACK, g=HALVES)
         xm_hbm = xm[0].rearrange("(g p j) d -> g p j d", j=PACK, g=HALVES)
         w_hbm = wT.rearrange("(p j) t -> j p t", j=PACK)
         loads = [
-            (x_raw[0][:], x_hbm[0]),
-            (ts_table[0:1, :], ts[0:1, :]),
-            (x_raw[1][:], x_hbm[1]),
-            (kb_table[0:1, :], kb[0:1, :]),
             (w_table[0][:], w_hbm[0]),
+            (ts_table[0:1, :], ts[0:1, :]),
             (w_table[1][:], w_hbm[1]),
+            (kb_table[0:1, :], kb[0:1, :]),
             (w_table[2][:], w_hbm[2]),
             (w_table[3][:], w_hbm[3]),
+            (x_raw[0][:], x_hbm[0]),
+            (y_raw[0][:, :, : N // 2], y_hbm[0][:, :, : N // 2]),
+            (x_raw[1][:], x_hbm[1]),
+            (y_raw[0][:, :, N // 2 :], y_hbm[0][:, :, N // 2 :]),
+            (y_raw[1][:], y_hbm[1]),
+            (xm_raw[0][:], xm_hbm[0]),
+            (xm_raw[1][:], xm_hbm[1]),
         ]
         for dest, source in loads:
             nc.sync.dma_start(out=dest, in_=source)
-        for half in range(2):
-            cols = slice(half * N // 2, (half + 1) * N // 2)
-            nc.sync.dma_start(out=y_raw[0][:, :, cols], in_=y_hbm[0][:, :, cols])
-        nc.sync.dma_start(out=y_raw[1][:], in_=y_hbm[1])
-        for g in range(HALVES):
-            nc.sync.dma_start(out=xm_raw[g][:], in_=xm_hbm[g])
 
         ident = keep.tile([P, P], F32, name="ident")
         make_identity(nc, ident[:])
@@ -100,14 +99,15 @@ def tile_attend_gnce_wx_ts_kb_kernel(tc, xT, wT, y, wt, ts, kb, xm, offs, out_0,
         warm = keep.tile([P, 1], F32, name="warm")
         nc.scalar.activation(out=warm[:], in_=ident[:, 0:1], func=ACT.Sigmoid)
 
-        windows = [keep.tile([P, T], F32, name=f"window{c}") for c in range(3)]
+        windows = [keep.tile([P, T], F32, name=f"window{c}") for c in range(1)]
         for window in windows:
             nc.vector.memset(window[:], 0.0)
 
-        def late_window(tag):
-            window = keep.tile([P, T], F32, name=f"window{len(windows)}", tag=tag)
-            for first in range(0, T, K_PASS):
-                nc.gpsimd.memset(window[:, first : first + K_PASS], 0.0)
+        def late_window(engine, tag, align=None):
+            window = keep.tile([P, T], F32, name=f"window{len(windows)}", tag=tag, align_bytes=align)
+            piece = T if engine is nc.vector else K_PASS
+            for first in range(0, T, piece):
+                engine.memset(window[:, first : first + piece], 0.0)
             windows.append(window)
 
         wt_free = []
@@ -123,13 +123,12 @@ def tile_attend_gnce_wx_ts_kb_kernel(tc, xT, wT, y, wt, ts, kb, xm, offs, out_0,
             wt_free.append(wide)
 
         x_mx = [mx_tiles(f"x{g}", K_PASS) for g in range(HALVES)]
-        x_grouped = [keep.tile([P, K_PASS, PACK], BF16, name=f"x_grouped{g}", align_bytes=64) for g in range(HALVES)]
+        x_grouped = [keep.tile([P, K_PASS, PACK], BF16, name=f"x_grouped{g}", tag=f"x_grouped{g}", align_bytes=64) for g in range(HALVES)]
         whole = slice(0, K_PASS)
 
         def flat(grouped):
             return grouped[:].rearrange("p c j -> p (c j)")
 
-        interleave(nc.scalar.copy, x_grouped[0], x_raw[0], whole)
 
         per_slot = []
         for name, table, turned in (("ts", ts_table, banks[5]), ("kb", kb_table, banks[3])):
@@ -142,7 +141,6 @@ def tile_attend_gnce_wx_ts_kb_kernel(tc, xT, wT, y, wt, ts, kb, xm, offs, out_0,
             per_slot.append(column)
         ts_slot, kb_slot = per_slot
 
-        quantize(x_mx[0], whole, flat(x_grouped[0]), E4M3)
 
         w_grouped = keep.tile([P, N, PACK], BF16, name="w_grouped", align_bytes=64)
         w_mx = mx_tiles("w", N)
@@ -155,6 +153,9 @@ def tile_attend_gnce_wx_ts_kb_kernel(tc, xT, wT, y, wt, ts, kb, xm, offs, out_0,
                 w_table[PACK - 1][:].indirect(offsets[:, half * 16 : (half + 1) * 16]),
             )
             quantize(w_mx, slots, w_grouped[:, slots, :].rearrange("p c j -> p (c j)"), E4M3)
+
+        interleave(nc.vector.tensor_copy, x_grouped[0], x_raw[0], whole)
+        quantize(x_mx[0], whole, flat(x_grouped[0]), E4M3)
 
         h_rows = [keep.tile([P, N, PACK], BF16, name=f"h_rows{g}", align_bytes=64) for g in range(HALVES)]
         h_rows_mx = [mx_tiles(f"h_rows{g}", N) for g in range(HALVES)]
@@ -213,11 +214,10 @@ def tile_attend_gnce_wx_ts_kb_kernel(tc, xT, wT, y, wt, ts, kb, xm, offs, out_0,
                 first = u * 2 * P + (t % 2) * P
                 nc.tensor.transpose(turned[:, first : first + P], words[:, u * P : (u + 1) * P], ident[:])
             if t % 2 == 1:
-                pair = slice((t - 1) * P, (t + 1) * P)
-                grouped = h_rows[g][:, pair, :].rearrange("p i j -> p (i j)")
+                placed = flat(h_rows[g]).bitcast(F32).rearrange("p (q m u) -> p q m u", q=PACK, u=2)
                 nc.scalar.copy(
-                    out=grouped.bitcast(F32).rearrange("p (i u) -> p i u", u=2),
-                    in_=turned[:].rearrange("p (u i) -> p i u", u=2),
+                    out=placed[:, :, (t - 1) * P // PACK : (t + 1) * P // PACK, :],
+                    in_=turned[:].rearrange("p (u m q) -> p q m u", u=2, q=PACK),
                 )
 
         def quantize_rows(g, half):
@@ -231,32 +231,37 @@ def tile_attend_gnce_wx_ts_kb_kernel(tc, xT, wT, y, wt, ts, kb, xm, offs, out_0,
             for g in range(HALVES):
                 matmul(acc[:], xm_mx[g], rows, E4M3, h_rows_mx[g], E5M2, g == 0, g == HALVES - 1)
             dense = ring.tile([P, N], F32, name="dense", bufs=4)
-            nc.scalar.copy(out=dense[:], in_=acc[:])
+            nc.scalar.copy(
+                out=dense[:].rearrange("d (m q) -> d m q", q=PACK),
+                in_=acc[:].rearrange("d (q m) -> d m q", q=PACK),
+            )
             products[c] = dense
 
         def place(c):
             nc.vector.tensor_copy(windows[c][:].indirect(offsets[:]), products[c][:])
             nc.sync.dma_start(out=out_0[c * P : (c + 1) * P, :], in_=windows[c][:])
 
-        def turn_slots(turned, grouped_words, u, order, dest):
+        def turn_slots(turned, words_of, order, dest):
             for t in range(PACK):
-                nc.tensor.transpose(turned[:, t * P : (t + 1) * P], grouped_words[:, 2 * t + u : 2 * N : 2 * PACK], ident[:])
+                nc.tensor.transpose(turned[:, t * P : (t + 1) * P], words_of(t), ident[:])
             nc.scalar.copy(
                 out=dest.rearrange(f"m ({order}) t -> m {order} t", e=2),
                 in_=turned[:].bitcast(BF16).rearrange(f"m (t p e) -> m {order} t", t=PACK, e=2),
             )
 
-        w_slots = keep.tile([P, D, PACK], BF16, name="w_slots", align_bytes=64)
-        w_slots_mx = mx_tiles("w_slots", D)
+        w_slots = keep.tile([P, D, PACK], BF16, name="w_slots", tag="w_slots", align_bytes=64)
+        w_slots_mx = mx_tiles("w_slots", D, "x_grouped0")
         h_cols = [keep.tile([P, K_PASS, PACK], BF16, name=f"h_cols{g}", align_bytes=64) for g in range(HALVES)]
         h_cols_mx = [mx_tiles(f"h_cols{g}", K_PASS) for g in range(HALVES)]
         out_1_hbm = out_1[0].rearrange("(g p u e) d -> g u p e d", g=HALVES, u=2, e=2)
 
         def turn_w(turned, u):
-            turn_slots(turned, flat(w_grouped).bitcast(F32), u, "p e", w_slots[:, u * 2 * P : (u + 1) * 2 * P, :])
+            words = flat(w_grouped).bitcast(F32)
+            turn_slots(turned, lambda t: words[:, 2 * t + u : 2 * N : 2 * PACK], "p e", w_slots[:, u * 2 * P : (u + 1) * 2 * P, :])
 
         def turn_h(turned, g, u):
-            turn_slots(turned, flat(h_rows[g]).bitcast(F32), u, "e p", h_cols[g][:, u * 2 * P : (u + 1) * 2 * P, :])
+            words = flat(h_rows[g]).bitcast(F32)
+            turn_slots(turned, lambda t: words[:, 2 * t * P + u : 2 * (t + 1) * P : 2], "e p", h_cols[g][:, u * 2 * P : (u + 1) * 2 * P, :])
 
         def quantize_cols(g, u):
             cols = slice(u * 2 * P, (u + 1) * 2 * P)
@@ -277,17 +282,21 @@ def tile_attend_gnce_wx_ts_kb_kernel(tc, xT, wT, y, wt, ts, kb, xm, offs, out_0,
         units = [(g, t) for g in range(HALVES) for t in range(BLOCKS)]
         halves = [slice(0, K_PASS // 2), slice(K_PASS // 2, K_PASS)]
         pieces = [slice(first, first + 256) for first in range(0, D, 256)]
-        for cols in halves:
-            interleave(nc.scalar.copy, x_grouped[1], x_raw[1], cols)
-        quantize(x_mx[1], whole, flat(x_grouped[1]), E4M3)
         turn_w(banks[6], 0)
-        late_window("w_table3")
+        turn_w(banks[7], 1)
+        late_window(nc.vector, "x_raw0")
+        quantize(w_slots_mx, whole, flat(w_slots), E4M3)
+        late_window(nc.gpsimd, "w_slots", 64)
         for unit in units[:3]:
             score(*unit)
         turn_labels(*units[0])
         difference(*units[0])
         turn_labels(*units[1])
         for n, unit in enumerate(units):
+            if n == 0:
+                interleave(nc.scalar.copy, x_grouped[1], x_raw[1], halves[0])
+                interleave(nc.vector.tensor_copy, x_grouped[1], x_raw[1], halves[1])
+                quantize(x_mx[1], whole, flat(x_grouped[1]), E4M3)
             if n + 3 < len(units):
                 score(*units[n + 3])
             if n + 2 < len(units):
@@ -297,12 +306,12 @@ def tile_attend_gnce_wx_ts_kb_kernel(tc, xT, wT, y, wt, ts, kb, xm, offs, out_0,
             if n == -1:
                 turn_w(banks[7], 1)
             weigh(*unit)
-            if n == 3:
+            if n == -1:
                 turn_w(banks[7], 1)
-            if n in (3, 5):
-                quantize_rows(*divmod((n - 3) // 2, 2))
-        quantize_rows(1, 1)
-        quantize_rows(1, 0)
+            if n == 4:
+                quantize(h_rows_mx[0], whole, flat(h_rows[0]), E5M2)
+        late_window(nc.gpsimd, "y_raw0")
+        quantize(h_rows_mx[1], whole, flat(h_rows[1]), E5M2)
         for g in range(HALVES):
             for n, cols in enumerate(pieces):
                 on_vector = g * len(pieces) + n >= 3
@@ -315,7 +324,6 @@ def tile_attend_gnce_wx_ts_kb_kernel(tc, xT, wT, y, wt, ts, kb, xm, offs, out_0,
         place(0)
         turn_h(banks[2], 0, 0)
         turn_h(banks[3], 0, 1)
-        quantize(w_slots_mx, whole, flat(w_slots), E4M3)
         quantize_cols(0, 0)
         quantize_cols(0, 1)
         table_product(1, banks[1])

@@ -21,6 +21,13 @@ PACK = 4
 K_PASS = P * PACK
 HALVES = R // K_PASS
 BLOCKS = N // P
+LIST_ROWS = 16
+SCORE_BANKS = 3
+LABEL_BANKS = 3
+PAIR_BANK = SCORE_BANKS + LABEL_BANKS
+X_ON_SCALAR = 192
+XM_PIECES_ON_SCALAR = 3
+EARLY_WINDOWS = 2
 
 
 def tile_attend_gnce_wx_ts_kb_kernel(tc, xT, wT, y, wt, ts, kb, xm, offs, out_0, out_1):
@@ -31,14 +38,23 @@ def tile_attend_gnce_wx_ts_kb_kernel(tc, xT, wT, y, wt, ts, kb, xm, offs, out_0,
         psum = ctx.enter_context(tc.psum_pool(name="psum", bufs=1))
 
         banks = [psum.tile([P, K_PASS], F32, name=f"bank{b}") for b in range(8)]
+        whole = slice(0, K_PASS)
+        column_halves = [slice(0, K_PASS // 2), slice(K_PASS // 2, K_PASS)]
 
-        def mx_tiles(name, width, tag=""):
-            codes = keep.tile([P, width], U32, name=name + "_codes", tag=tag, align_bytes=64)
-            scales = keep.tile([P, width], U8, name=name + "_scales", align_bytes=64)
+        def mx_tiles(name, tag=""):
+            codes = keep.tile([P, K_PASS], U32, name=name + "_codes", tag=tag, align_bytes=64)
+            scales = keep.tile([P, K_PASS], U8, name=name + "_scales", align_bytes=64)
             return codes, scales
 
-        def quantize(mx, cols, grouped, fmt):
-            nc.vector.quantize_mx(out=mx[0][:, cols].bitcast(fmt), scales=mx[1][:, cols], in_=grouped)
+        def grouped_tile(name):
+            return keep.tile([P, K_PASS, PACK], BF16, name=name, tag=name, align_bytes=64)
+
+        def flat(grouped):
+            return grouped.rearrange("p c j -> p (c j)")
+
+        def quantize(mx, grouped, cols, fmt):
+            codes, scales = mx
+            nc.vector.quantize_mx(out=codes[:, cols].bitcast(fmt), scales=scales[:, cols], in_=flat(grouped[:, cols, :]))
 
         def matmul(out, lhs, lhs_cols, lhs_fmt, rhs, rhs_fmt, start, stop):
             nc.tensor.matmul_mx(
@@ -51,13 +67,13 @@ def tile_attend_gnce_wx_ts_kb_kernel(tc, xT, wT, y, wt, ts, kb, xm, offs, out_0,
                 stop=stop,
             )
 
-        def interleave(copy, grouped, raw, cols):
+        def group(copy, grouped, raw, cols):
             copy(
                 out=grouped[:, cols, :].rearrange("p (c i) j -> p c j i", i=4),
                 in_=raw[:, :, cols].rearrange("p j (c i) -> p c j i", i=4),
             )
 
-        offsets = keep.tile([P, N // 16], U16, name="offsets")
+        offsets = keep.tile([P, N // LIST_ROWS], U16, name="offsets")
         nc.sync.dma_start(offsets[:], offs)
 
         ts_table = keep.tile([P, T], F32, name="ts_table")
@@ -69,8 +85,8 @@ def tile_attend_gnce_wx_ts_kb_kernel(tc, xT, wT, y, wt, ts, kb, xm, offs, out_0,
 
         x_raw = [keep.tile([P, PACK, K_PASS], F32, name=f"x_raw{g}", tag=f"x_raw{g}") for g in range(HALVES)]
         y_raw = [keep.tile([P, PACK, N], F32, name=f"y_raw{g}", tag=f"y_raw{g}") for g in range(HALVES)]
-        xm_raw = [keep.tile([P, PACK, D], F32, name=f"xm_raw{g}", tag=f"xm_raw{g}") for g in range(HALVES)]
-        w_table = [keep.tile([P, T], F32, name=f"w_table{j}", tag=f"w_table{j}") for j in range(PACK)]
+        xm_raw = [keep.tile([P, PACK, D], F32, name=f"xm_raw{g}") for g in range(HALVES)]
+        w_table = [keep.tile([P, T], F32, name=f"w_table{j}") for j in range(PACK)]
         x_hbm = xT[0].rearrange("(p j) (g r) -> g p j r", j=PACK, g=HALVES)
         y_hbm = y[0].rearrange("(g p j) i -> g p j i", j=PACK, g=HALVES)
         xm_hbm = xm[0].rearrange("(g p j) d -> g p j d", j=PACK, g=HALVES)
@@ -83,9 +99,9 @@ def tile_attend_gnce_wx_ts_kb_kernel(tc, xT, wT, y, wt, ts, kb, xm, offs, out_0,
             (w_table[2][:], w_hbm[2]),
             (w_table[3][:], w_hbm[3]),
             (x_raw[0][:], x_hbm[0]),
-            (y_raw[0][:, :, : N // 2], y_hbm[0][:, :, : N // 2]),
+            (y_raw[0][:, :, column_halves[0]], y_hbm[0][:, :, column_halves[0]]),
             (x_raw[1][:], x_hbm[1]),
-            (y_raw[0][:, :, N // 2 :], y_hbm[0][:, :, N // 2 :]),
+            (y_raw[0][:, :, column_halves[1]], y_hbm[0][:, :, column_halves[1]]),
             (y_raw[1][:], y_hbm[1]),
             (xm_raw[0][:], xm_hbm[0]),
             (xm_raw[1][:], xm_hbm[1]),
@@ -96,39 +112,28 @@ def tile_attend_gnce_wx_ts_kb_kernel(tc, xT, wT, y, wt, ts, kb, xm, offs, out_0,
         ident = keep.tile([P, P], F32, name="ident")
         make_identity(nc, ident[:])
 
-        warm = keep.tile([P, 1], F32, name="warm")
-        nc.scalar.activation(out=warm[:], in_=ident[:, 0:1], func=ACT.Sigmoid)
-
-        windows = [keep.tile([P, T], F32, name=f"window{c}") for c in range(1)]
+        windows = [keep.tile([P, T], F32, name=f"window{c}") for c in range(EARLY_WINDOWS)]
         for window in windows:
             nc.vector.memset(window[:], 0.0)
 
-        def late_window(engine, tag, align=None):
-            window = keep.tile([P, T], F32, name=f"window{len(windows)}", tag=tag, align_bytes=align)
-            piece = T if engine is nc.vector else K_PASS
+        def late_window(engine, piece, tag):
+            window = keep.tile([P, T], F32, name=f"window{len(windows)}", tag=tag)
             for first in range(0, T, piece):
                 engine.memset(window[:, first : first + piece], 0.0)
             windows.append(window)
 
         wt_free = []
         for g in range(HALVES):
-            turned = banks[3 + g]
+            turned = banks[SCORE_BANKS + g]
             for j in range(PACK):
-                nc.tensor.transpose(turned[:, j * P : (j + 1) * P], wt_rows[:, g, j : j + 1].to_broadcast([P, P]), ident[:])
+                repeated = wt_rows[:, g, j : j + 1].to_broadcast([P, P])
+                nc.tensor.transpose(turned[:, j * P : (j + 1) * P], repeated, ident[:])
             wide = keep.tile([P, K_PASS], F32, name=f"wt_free{g}")
             nc.scalar.copy(
                 out=wide[:].rearrange("q (u p e) -> q u p e", u=2, e=2),
                 in_=turned[:].rearrange("q (u e p) -> q u p e", u=2, e=2),
             )
             wt_free.append(wide)
-
-        x_mx = [mx_tiles(f"x{g}", K_PASS) for g in range(HALVES)]
-        x_grouped = [keep.tile([P, K_PASS, PACK], BF16, name=f"x_grouped{g}", tag=f"x_grouped{g}", align_bytes=64) for g in range(HALVES)]
-        whole = slice(0, K_PASS)
-
-        def flat(grouped):
-            return grouped[:].rearrange("p c j -> p (c j)")
-
 
         per_slot = []
         for name, table, turned in (("ts", ts_table, banks[5]), ("kb", kb_table, banks[3])):
@@ -137,206 +142,184 @@ def tile_attend_gnce_wx_ts_kb_kernel(tc, xT, wT, y, wt, ts, kb, xm, offs, out_0,
             for t in range(BLOCKS):
                 nc.tensor.transpose(turned[:, t * P : (t + 1) * P], picked[:, t * P : (t + 1) * P], ident[:])
             column = keep.tile([P, BLOCKS], F32, name=name + "_slot")
-            nc.scalar.copy(out=column[:], in_=turned[:, 0 : N : P])
+            nc.scalar.copy(out=column[:], in_=turned[:, 0:N:P])
             per_slot.append(column)
         ts_slot, kb_slot = per_slot
 
-
-        w_grouped = keep.tile([P, N, PACK], BF16, name="w_grouped", align_bytes=64)
-        w_mx = mx_tiles("w", N)
+        w_picked = keep.tile([P, PACK, N], F32, name="w_picked")
+        w_grouped = grouped_tile("w_grouped")
+        w_mx = mx_tiles("w")
         for j in range(PACK - 1):
-            nc.vector.tensor_copy(w_grouped[:, :, j], w_table[j][:].indirect(offsets[:]))
-        for half in range(2):
-            slots = slice(half * N // 2, (half + 1) * N // 2)
-            nc.vector.tensor_copy(
-                w_grouped[:, slots, PACK - 1],
-                w_table[PACK - 1][:].indirect(offsets[:, half * 16 : (half + 1) * 16]),
-            )
-            quantize(w_mx, slots, w_grouped[:, slots, :].rearrange("p c j -> p (c j)"), E4M3)
+            nc.vector.tensor_copy(w_picked[:, j, :], w_table[j][:].indirect(offsets[:]))
+        for slots in column_halves:
+            listed = offsets[:, slots.start // LIST_ROWS : slots.stop // LIST_ROWS]
+            nc.vector.tensor_copy(w_picked[:, PACK - 1, slots], w_table[PACK - 1][:].indirect(listed))
+        for slots in column_halves:
+            group(nc.vector.tensor_copy, w_grouped, w_picked, slots)
+        for slots in column_halves:
+            quantize(w_mx, w_grouped, slots, E4M3)
 
-        interleave(nc.vector.tensor_copy, x_grouped[0], x_raw[0], whole)
-        quantize(x_mx[0], whole, flat(x_grouped[0]), E4M3)
+        x_grouped = [grouped_tile(f"x_grouped{g}") for g in range(HALVES)]
+        x_mx = [mx_tiles(f"x{g}") for g in range(HALVES)]
 
-        h_rows = [keep.tile([P, N, PACK], BF16, name=f"h_rows{g}", align_bytes=64) for g in range(HALVES)]
-        h_rows_mx = [mx_tiles(f"h_rows{g}", N) for g in range(HALVES)]
-        xm_mx = [mx_tiles(f"xm{g}", D) for g in range(HALVES)]
-        xm_grouped = [keep.tile([P, D, PACK], BF16, name=f"xm_grouped{g}", align_bytes=64) for g in range(HALVES)]
+        def prepare_x(g):
+            group(nc.scalar.copy, x_grouped[g], x_raw[g], slice(0, X_ON_SCALAR))
+            group(nc.vector.tensor_copy, x_grouped[g], x_raw[g], slice(X_ON_SCALAR, K_PASS))
+            quantize(x_mx[g], x_grouped[g], whole, E4M3)
+
+        prepare_x(0)
+
+        w_slots = grouped_tile("w_slots")
+        w_slots_mx = mx_tiles("w_slots", tag="x_grouped0")
+        for j in range(PACK):
+            turned = banks[PAIR_BANK + j % 2]
+            for q in range(PACK):
+                nc.tensor.transpose(turned[:, q * P : (q + 1) * P], w_picked[:, j, q:N:PACK], ident[:])
+            nc.scalar.copy(out=w_slots[:, j * P : (j + 1) * P, :], in_=turned[:].rearrange("m (q p) -> m p q", q=PACK))
+        quantize(w_slots_mx, w_slots, whole, E4M3)
+        late_window(nc.vector, T, "x_raw0")
+
+        h_rows = [grouped_tile(f"h_rows{g}") for g in range(HALVES)]
+        h_rows_mx = [mx_tiles(f"h_rows{g}") for g in range(HALVES)]
+        h_cols = [grouped_tile(f"h_cols{g}") for g in range(HALVES)]
+        h_cols_mx = [mx_tiles(f"h_cols{g}") for g in range(HALVES)]
+        units = [(g, t) for g in range(HALVES) for t in range(BLOCKS)]
+        probs = {}
         diffs = {}
 
-        probs = {}
-
-        def score(g, t):
-            slots = slice(t * P, (t + 1) * P)
-            scores = banks[(BLOCKS * g + t) % 3]
-            matmul(scores[:], w_mx, slots, E4M3, x_mx[g], E4M3, True, True)
-            prob = ring.tile([P, K_PASS], F32, name="prob", bufs=4)
+        def score(n):
+            g, t = units[n]
+            scores = banks[n % SCORE_BANKS]
+            matmul(scores[:], w_mx, slice(t * P, (t + 1) * P), E4M3, x_mx[g], E4M3, True, True)
+            probs[n] = ring.tile([P, K_PASS], F32, name="prob", bufs=SCORE_BANKS + 1)
             nc.scalar.activation(
-                out=prob[:].rearrange("m (u p e) -> m u p e", u=2, e=2),
+                out=probs[n][:].rearrange("m (u p e) -> m u p e", u=2, e=2),
                 in_=scores[:].rearrange("m (p u e) -> m u p e", u=2, e=2),
                 func=ACT.Sigmoid,
                 bias=kb_slot[:, t : t + 1],
                 scale=ts_slot[:, t : t + 1],
             )
-            probs[g, t] = prob
 
-        def turn_labels(g, t):
-            labels = banks[3 + (BLOCKS * g + t) % 3]
+        def label_bank(n):
+            return banks[SCORE_BANKS + n % LABEL_BANKS]
+
+        def turn_labels(n):
+            g, t = units[n]
             for j in range(PACK):
-                nc.tensor.transpose(labels[:, j * P : (j + 1) * P], y_raw[g][:, j, t * P : (t + 1) * P], ident[:])
+                nc.tensor.transpose(label_bank(n)[:, j * P : (j + 1) * P], y_raw[g][:, j, t * P : (t + 1) * P], ident[:])
 
-        def difference(g, t):
-            labels = banks[3 + (BLOCKS * g + t) % 3]
-            diff = ring.tile([P, K_PASS], F32, name="diff")
+        def difference(n):
+            diffs[n] = ring.tile([P, K_PASS], F32, name="diff")
             nc.vector.tensor_tensor(
-                out=diff[:].rearrange("m (u p e) -> m u p e", u=2, e=2),
-                in0=probs[g, t][:].rearrange("m (u p e) -> m u p e", u=2, e=2),
-                in1=labels[:].rearrange("m (u e p) -> m u p e", u=2, e=2),
+                out=diffs[n][:].rearrange("m (u p e) -> m u p e", u=2, e=2),
+                in0=probs[n][:].rearrange("m (u p e) -> m u p e", u=2, e=2),
+                in1=label_bank(n)[:].rearrange("m (u e p) -> m u p e", u=2, e=2),
                 op=ALU.subtract,
             )
-            diffs[g, t] = diff
 
-        def weigh(g, t):
-            if (g, t) == units[-1]:
-                h_slots = flat(h_cols[0])[:, 5 * K_PASS // 4 : 9 * K_PASS // 4]
+        def weigh(n):
+            g, t = units[n]
+            if n == len(units) - 1:
+                first = 2 * K_PASS - 3 * K_PASS // 4
+                h_unit = flat(h_cols[0][:])[:, first : first + K_PASS]
             else:
-                h_slots = ring.tile([P, K_PASS], BF16, name="h_slots")[:]
+                h_unit = ring.tile([P, K_PASS], BF16, name="h_unit")[:]
             nc.vector.scalar_tensor_tensor(
-                out=h_slots,
-                in0=diffs[g, t][:],
+                out=h_unit,
+                in0=diffs[n][:],
                 scalar=ts_slot[:, t : t + 1],
                 in1=wt_free[g][:],
                 op0=ALU.mult,
                 op1=ALU.mult,
             )
-            turned = banks[6 + t // 2]
-            words = h_slots.bitcast(F32)
+            turned = banks[PAIR_BANK + t // 2]
+            pairs = h_unit.bitcast(F32)
             for u in range(2):
-                first = u * 2 * P + (t % 2) * P
-                nc.tensor.transpose(turned[:, first : first + P], words[:, u * P : (u + 1) * P], ident[:])
+                place = u * 2 * P + (t % 2) * P
+                nc.tensor.transpose(turned[:, place : place + P], pairs[:, u * P : (u + 1) * P], ident[:])
             if t % 2 == 1:
-                placed = flat(h_rows[g]).bitcast(F32).rearrange("p (q m u) -> p q m u", q=PACK, u=2)
+                by_q = flat(h_rows[g][:]).bitcast(F32).rearrange("p (q m u) -> p q m u", q=PACK, u=2)
                 nc.scalar.copy(
-                    out=placed[:, :, (t - 1) * P // PACK : (t + 1) * P // PACK, :],
+                    out=by_q[:, :, (t - 1) * P // PACK : (t + 1) * P // PACK, :],
                     in_=turned[:].rearrange("p (u m q) -> p q m u", u=2, q=PACK),
                 )
 
-        def quantize_rows(g, half):
-            pair = slice(half * 2 * P, (half + 1) * 2 * P)
-            quantize(h_rows_mx[g], pair, h_rows[g][:, pair, :].rearrange("p i j -> p (i j)"), E5M2)
+        for n in range(SCORE_BANKS):
+            score(n)
+        turn_labels(0)
+        difference(0)
+        turn_labels(1)
+        for n in range(len(units)):
+            if n == 0:
+                prepare_x(1)
+            if n + SCORE_BANKS < len(units):
+                score(n + SCORE_BANKS)
+            if n + 2 < len(units):
+                turn_labels(n + 2)
+            if n + 1 < len(units):
+                difference(n + 1)
+            weigh(n)
+            if n == BLOCKS:
+                quantize(h_rows_mx[0], h_rows[0], whole, E5M2)
+        late_window(nc.gpsimd, K_PASS, "y_raw0")
+        quantize(h_rows_mx[1], h_rows[1], whole, E5M2)
 
-        products = {}
+        xm_grouped = [grouped_tile(f"xm_grouped{g}") for g in range(HALVES)]
+        xm_mx = [mx_tiles(f"xm{g}") for g in range(HALVES)]
+        xm_pieces = [(g, cols) for g in range(HALVES) for cols in column_halves]
+        for n, (g, cols) in enumerate(xm_pieces):
+            copy = nc.scalar.copy if n < XM_PIECES_ON_SCALAR else nc.vector.tensor_copy
+            group(copy, xm_grouped[g], xm_raw[g], cols)
+        for g, cols in xm_pieces:
+            quantize(xm_mx[g], xm_grouped[g], cols, E4M3)
 
-        def table_product(c, acc):
-            rows = slice(c * P, (c + 1) * P)
+        out_1_hbm = out_1[0].rearrange("(g p u e) d -> g u p e d", g=HALVES, u=2, e=2)
+
+        def table_gradient(c, acc):
+            features = slice(c * P, (c + 1) * P)
             for g in range(HALVES):
-                matmul(acc[:], xm_mx[g], rows, E4M3, h_rows_mx[g], E5M2, g == 0, g == HALVES - 1)
-            dense = ring.tile([P, N], F32, name="dense", bufs=4)
+                matmul(acc[:], xm_mx[g], features, E4M3, h_rows_mx[g], E5M2, g == 0, g == HALVES - 1)
+            dense = ring.tile([P, N], F32, name="dense", bufs=BLOCKS)
             nc.scalar.copy(
                 out=dense[:].rearrange("d (m q) -> d m q", q=PACK),
                 in_=acc[:].rearrange("d (q m) -> d m q", q=PACK),
             )
-            products[c] = dense
+            nc.vector.tensor_copy(windows[c][:].indirect(offsets[:]), dense[:])
+            nc.sync.dma_start(out=out_0[features, :], in_=windows[c][:])
 
-        def place(c):
-            nc.vector.tensor_copy(windows[c][:].indirect(offsets[:]), products[c][:])
-            nc.sync.dma_start(out=out_0[c * P : (c + 1) * P, :], in_=windows[c][:])
-
-        def turn_slots(turned, words_of, order, dest):
-            for t in range(PACK):
-                nc.tensor.transpose(turned[:, t * P : (t + 1) * P], words_of(t), ident[:])
+        def turn_h(g, u, turned):
+            pairs = flat(h_rows[g][:]).bitcast(F32)
+            for q in range(PACK):
+                nc.tensor.transpose(turned[:, q * P : (q + 1) * P], pairs[:, 2 * q * P + u : 2 * (q + 1) * P : 2], ident[:])
             nc.scalar.copy(
-                out=dest.rearrange(f"m ({order}) t -> m {order} t", e=2),
-                in_=turned[:].bitcast(BF16).rearrange(f"m (t p e) -> m {order} t", t=PACK, e=2),
+                out=h_cols[g][:, column_halves[u], :].rearrange("m (e p) q -> m e p q", e=2),
+                in_=turned[:].bitcast(BF16).rearrange("m (q p e) -> m e p q", q=PACK, e=2),
             )
 
-        w_slots = keep.tile([P, D, PACK], BF16, name="w_slots", tag="w_slots", align_bytes=64)
-        w_slots_mx = mx_tiles("w_slots", D, "x_grouped0")
-        h_cols = [keep.tile([P, K_PASS, PACK], BF16, name=f"h_cols{g}", align_bytes=64) for g in range(HALVES)]
-        h_cols_mx = [mx_tiles(f"h_cols{g}", K_PASS) for g in range(HALVES)]
-        out_1_hbm = out_1[0].rearrange("(g p u e) d -> g u p e d", g=HALVES, u=2, e=2)
-
-        def turn_w(turned, u):
-            words = flat(w_grouped).bitcast(F32)
-            turn_slots(turned, lambda t: words[:, 2 * t + u : 2 * N : 2 * PACK], "p e", w_slots[:, u * 2 * P : (u + 1) * 2 * P, :])
-
-        def turn_h(turned, g, u):
-            words = flat(h_rows[g]).bitcast(F32)
-            turn_slots(turned, lambda t: words[:, 2 * t * P + u : 2 * (t + 1) * P : 2], "e p", h_cols[g][:, u * 2 * P : (u + 1) * 2 * P, :])
-
-        def quantize_cols(g, u):
-            cols = slice(u * 2 * P, (u + 1) * 2 * P)
-            quantize(h_cols_mx[g], cols, h_cols[g][:, cols, :].rearrange("p c j -> p (c j)"), E5M2)
-
         def row_gradient(g, u, accs):
-            staged = ring.tile([P, 2, D], F32, name="staged", bufs=4)
+            staged = ring.tile([P, 2, D], F32, name="staged", bufs=2 * HALVES)
             for e in range(2):
                 first = (2 * u + e) * P
-                acc = accs[e]
-                matmul(acc[:], h_cols_mx[g], slice(first, first + P), E5M2, w_slots_mx, E4M3, True, True)
+                matmul(accs[e][:], h_cols_mx[g], slice(first, first + P), E5M2, w_slots_mx, E4M3, True, True)
                 nc.scalar.copy(
-                    out=staged[:, e, :].rearrange("r (p u e) -> r p u e", u=2, e=2),
-                    in_=acc[:].rearrange("r (u p e) -> r p u e", u=2, e=2),
+                    out=staged[:, e, :].rearrange("r (p j) -> r p j", j=PACK),
+                    in_=accs[e][:].rearrange("r (j p) -> r p j", j=PACK),
                 )
             nc.scalar.dma_start(out=out_1_hbm[g, u], in_=staged[:])
 
-        units = [(g, t) for g in range(HALVES) for t in range(BLOCKS)]
-        halves = [slice(0, K_PASS // 2), slice(K_PASS // 2, K_PASS)]
-        pieces = [slice(first, first + 256) for first in range(0, D, 256)]
-        turn_w(banks[6], 0)
-        turn_w(banks[7], 1)
-        late_window(nc.vector, "x_raw0")
-        quantize(w_slots_mx, whole, flat(w_slots), E4M3)
-        late_window(nc.gpsimd, "w_slots", 64)
-        for unit in units[:3]:
-            score(*unit)
-        turn_labels(*units[0])
-        difference(*units[0])
-        turn_labels(*units[1])
-        for n, unit in enumerate(units):
-            if n == 0:
-                interleave(nc.scalar.copy, x_grouped[1], x_raw[1], halves[0])
-                interleave(nc.vector.tensor_copy, x_grouped[1], x_raw[1], halves[1])
-                quantize(x_mx[1], whole, flat(x_grouped[1]), E4M3)
-            if n + 3 < len(units):
-                score(*units[n + 3])
-            if n + 2 < len(units):
-                turn_labels(*units[n + 2])
-            if n + 1 < len(units):
-                difference(*units[n + 1])
-            if n == -1:
-                turn_w(banks[7], 1)
-            weigh(*unit)
-            if n == -1:
-                turn_w(banks[7], 1)
-            if n == 4:
-                quantize(h_rows_mx[0], whole, flat(h_rows[0]), E5M2)
-        late_window(nc.gpsimd, "y_raw0")
-        quantize(h_rows_mx[1], whole, flat(h_rows[1]), E5M2)
-        for g in range(HALVES):
-            for n, cols in enumerate(pieces):
-                on_vector = g * len(pieces) + n >= 3
-                interleave(nc.vector.tensor_copy if on_vector else nc.scalar.copy, xm_grouped[g], xm_raw[g], cols)
-        for g in range(HALVES):
-            for cols in halves:
-                quantize(xm_mx[g], cols, xm_grouped[g][:, cols, :].rearrange("p c j -> p (c j)"), E4M3)
-
-        table_product(0, banks[0])
-        place(0)
-        turn_h(banks[2], 0, 0)
-        turn_h(banks[3], 0, 1)
-        quantize_cols(0, 0)
-        quantize_cols(0, 1)
-        table_product(1, banks[1])
-        place(1)
+        table_gradient(0, banks[0])
+        for u in range(2):
+            turn_h(0, u, banks[2 + u])
+        for cols in column_halves:
+            quantize(h_cols_mx[0], h_cols[0], cols, E5M2)
+        table_gradient(1, banks[1])
         row_gradient(0, 0, banks[2:4])
         row_gradient(0, 1, banks[4:6])
-        turn_h(banks[2], 1, 0)
-        turn_h(banks[3], 1, 1)
-        quantize_cols(1, 0)
-        quantize_cols(1, 1)
-        table_product(2, banks[2])
-        place(2)
+        for u in range(2):
+            turn_h(1, u, banks[2 + u])
+        for cols in column_halves:
+            quantize(h_cols_mx[1], h_cols[1], cols, E5M2)
+        table_gradient(2, banks[2])
         row_gradient(1, 0, banks[0:2])
-        table_product(3, banks[3])
-        place(3)
+        table_gradient(3, banks[3])
         row_gradient(1, 1, banks[4:6])

@@ -22,12 +22,10 @@ K_PASS = P * PACK
 HALVES = R // K_PASS
 BLOCKS = N // P
 LIST_ROWS = 16
-SCORE_BANKS = 3
-LABEL_BANKS = 3
-PAIR_BANK = SCORE_BANKS + LABEL_BANKS
-X_ON_SCALAR = 192
-XM_PIECES_ON_SCALAR = 3
-EARLY_WINDOWS = 2
+SCORE_BANK = 0
+TURN_BANK = 4
+WINDOWS = 3
+RUN = 8
 
 
 def tile_attend_gnce_wx_ts_kb_kernel(tc, xT, wT, y, wt, ts, kb, xm, offs, out_0, out_1):
@@ -39,22 +37,23 @@ def tile_attend_gnce_wx_ts_kb_kernel(tc, xT, wT, y, wt, ts, kb, xm, offs, out_0,
 
         banks = [psum.tile([P, K_PASS], F32, name=f"bank{b}") for b in range(8)]
         whole = slice(0, K_PASS)
-        column_halves = [slice(0, K_PASS // 2), slice(K_PASS // 2, K_PASS)]
+        HALF = K_PASS // 2
+        column_halves = [slice(0, HALF), slice(HALF, K_PASS)]
 
-        def mx_tiles(name, tag=""):
-            codes = keep.tile([P, K_PASS], U32, name=name + "_codes", tag=tag, align_bytes=64)
+        def mx_tiles(name):
+            codes = keep.tile([P, K_PASS], U32, name=name + "_codes", align_bytes=64)
             scales = keep.tile([P, K_PASS], U8, name=name + "_scales", align_bytes=64)
             return codes, scales
 
-        def grouped_tile(name):
-            return keep.tile([P, K_PASS, PACK], BF16, name=name, tag=name, align_bytes=64)
+        def grouped_tile(name, columns=K_PASS):
+            return keep.tile([P, columns, PACK], BF16, name=name, tag=name, align_bytes=64)
 
         def flat(grouped):
             return grouped.rearrange("p c j -> p (c j)")
 
-        def quantize(mx, grouped, cols, fmt):
+        def quantize(mx, cols, grouped, fmt):
             codes, scales = mx
-            nc.vector.quantize_mx(out=codes[:, cols].bitcast(fmt), scales=scales[:, cols], in_=flat(grouped[:, cols, :]))
+            nc.vector.quantize_mx(out=codes[:, cols].bitcast(fmt), scales=scales[:, cols], in_=flat(grouped))
 
         def matmul(out, lhs, lhs_cols, lhs_fmt, rhs, rhs_fmt, start, stop):
             nc.tensor.matmul_mx(
@@ -67,15 +66,14 @@ def tile_attend_gnce_wx_ts_kb_kernel(tc, xT, wT, y, wt, ts, kb, xm, offs, out_0,
                 stop=stop,
             )
 
-        def group(copy, grouped, raw, cols):
+        def group(copy, grouped, raw):
             copy(
-                out=grouped[:, cols, :].rearrange("p (c i) j -> p c j i", i=4),
-                in_=raw[:, :, cols].rearrange("p j (c i) -> p c j i", i=4),
+                out=grouped.rearrange("p (c i) j -> p c j i", i=4),
+                in_=raw.rearrange("p j (c i) -> p c j i", i=4),
             )
 
         offsets = keep.tile([P, N // LIST_ROWS], U16, name="offsets")
         nc.sync.dma_start(offsets[:], offs)
-
         ts_table = keep.tile([P, T], F32, name="ts_table")
         kb_table = keep.tile([P, T], F32, name="kb_table")
         for table in (ts_table, kb_table):
@@ -83,195 +81,168 @@ def tile_attend_gnce_wx_ts_kb_kernel(tc, xT, wT, y, wt, ts, kb, xm, offs, out_0,
         wt_rows = keep.tile([P, HALVES, PACK], F32, name="wt_rows")
         nc.scalar.dma_start(out=wt_rows[:], in_=wt[0].rearrange("(g p j) o -> p g (j o)", g=HALVES, j=PACK))
 
-        x_raw = [keep.tile([P, PACK, K_PASS], F32, name=f"x_raw{g}", tag=f"x_raw{g}") for g in range(HALVES)]
-        y_raw = [keep.tile([P, PACK, N], F32, name=f"y_raw{g}", tag=f"y_raw{g}") for g in range(HALVES)]
-        xm_raw = [keep.tile([P, PACK, D], F32, name=f"xm_raw{g}") for g in range(HALVES)]
-        w_table = [keep.tile([P, T], F32, name=f"w_table{j}") for j in range(PACK)]
+        x0_raw = [keep.tile([P, PACK, HALF], F32, name=f"x0_raw{a}", tag=f"x0_raw{a}") for a in range(2)]
+        x1_raw = keep.tile([P, PACK, K_PASS], F32, name="x1_raw")
+        y_raw = [keep.tile([P, PACK, N], F32, name=f"y_raw{g}") for g in range(HALVES)]
+        xm_raw = [[keep.tile([P, PACK, HALF], F32, name=f"xm_raw{a}{g}") for g in range(HALVES)] for a in range(2)]
+        w_table = [keep.tile([P, T], F32, name=f"w_table{j}", tag=f"w_table{j}") for j in range(PACK)]
         x_hbm = xT[0].rearrange("(p j) (g r) -> g p j r", j=PACK, g=HALVES)
         y_hbm = y[0].rearrange("(g p j) i -> g p j i", j=PACK, g=HALVES)
         xm_hbm = xm[0].rearrange("(g p j) d -> g p j d", j=PACK, g=HALVES)
         w_hbm = wT.rearrange("(p j) t -> j p t", j=PACK)
-        loads = [
-            (w_table[0][:], w_hbm[0]),
-            (ts_table[0:1, :], ts[0:1, :]),
-            (w_table[1][:], w_hbm[1]),
-            (kb_table[0:1, :], kb[0:1, :]),
-            (w_table[2][:], w_hbm[2]),
-            (w_table[3][:], w_hbm[3]),
-            (x_raw[0][:], x_hbm[0]),
-            (y_raw[0][:, :, column_halves[0]], y_hbm[0][:, :, column_halves[0]]),
-            (x_raw[1][:], x_hbm[1]),
-            (y_raw[0][:, :, column_halves[1]], y_hbm[0][:, :, column_halves[1]]),
-            (y_raw[1][:], y_hbm[1]),
-            (xm_raw[0][:], xm_hbm[0]),
-            (xm_raw[1][:], xm_hbm[1]),
-        ]
+        loads = [(w_table[j][:], w_hbm[j]) for j in range(PACK)]
+        loads.insert(1, (ts_table[0:1, :], ts[0:1, :]))
+        loads.insert(3, (kb_table[0:1, :], kb[0:1, :]))
+        loads.extend((x0_raw[a][:], x_hbm[0][:, :, column_halves[a]]) for a in range(2))
+        loads.append((x1_raw[:], x_hbm[1]))
+        loads.extend((y_raw[g][:], y_hbm[g]) for g in range(HALVES))
+        loads.extend((xm_raw[a][g][:], xm_hbm[g][:, :, column_halves[a]]) for a in range(2) for g in range(HALVES))
         for dest, source in loads:
             nc.sync.dma_start(out=dest, in_=source)
 
         ident = keep.tile([P, P], F32, name="ident")
         make_identity(nc, ident[:])
 
-        windows = [keep.tile([P, T], F32, name=f"window{c}") for c in range(EARLY_WINDOWS)]
+        warm = keep.tile([P, HALVES * PACK], F32, name="warm")
+        nc.scalar.activation(out=warm[:], in_=wt_rows[:].rearrange("p g j -> p (g j)"), func=ACT.Sigmoid)
+
+        windows = [keep.tile([P, T], F32, name=f"window{c}") for c in range(WINDOWS - 1)]
         for window in windows:
             nc.vector.memset(window[:], 0.0)
 
-        def late_window(engine, piece, tag):
-            window = keep.tile([P, T], F32, name=f"window{len(windows)}", tag=tag)
-            for first in range(0, T, piece):
-                engine.memset(window[:, first : first + piece], 0.0)
-            windows.append(window)
-
-        wt_free = []
-        for g in range(HALVES):
-            turned = banks[SCORE_BANKS + g]
-            for j in range(PACK):
-                repeated = wt_rows[:, g, j : j + 1].to_broadcast([P, P])
-                nc.tensor.transpose(turned[:, j * P : (j + 1) * P], repeated, ident[:])
-            wide = keep.tile([P, K_PASS], F32, name=f"wt_free{g}")
-            nc.scalar.copy(
-                out=wide[:].rearrange("q (u p e) -> q u p e", u=2, e=2),
-                in_=turned[:].rearrange("q (u e p) -> q u p e", u=2, e=2),
-            )
-            wt_free.append(wide)
-
         per_slot = []
-        for name, table, turned in (("ts", ts_table, banks[5]), ("kb", kb_table, banks[3])):
+        for n, (name, table) in enumerate((("ts", ts_table), ("kb", kb_table))):
             picked = keep.tile([P, N], F32, name=name + "_picked")
             nc.vector.tensor_copy(picked[:], table[:].indirect(offsets[:]))
+            dealt = keep.tile([P, N], F32, name=name + "_dealt")
+            nc.scalar.copy(
+                out=dealt[:].rearrange("p (q b m) -> p b q m", q=PACK, m=RUN),
+                in_=picked[:].rearrange("p (b q m) -> p b q m", q=PACK, m=RUN),
+            )
+            turned = banks[SCORE_BANK + n]
             for t in range(BLOCKS):
-                nc.tensor.transpose(turned[:, t * P : (t + 1) * P], picked[:, t * P : (t + 1) * P], ident[:])
+                nc.tensor.transpose(turned[:, t * P : (t + 1) * P], dealt[:, t * P : (t + 1) * P], ident[:])
             column = keep.tile([P, BLOCKS], F32, name=name + "_slot")
             nc.scalar.copy(out=column[:], in_=turned[:, 0:N:P])
             per_slot.append(column)
         ts_slot, kb_slot = per_slot
 
+        ts_free = banks[TURN_BANK + 3]
+        for t in range(BLOCKS):
+            nc.tensor.transpose(ts_free[:, t * P : (t + 1) * P], ts_slot[:, t : t + 1].to_broadcast([P, P]), ident[:])
+        factor = {}
+
+        def make_factor(g, tag):
+            factor[g] = keep.tile([P, PACK, N], F32, name=f"factor{g}", tag=tag)
+            for j in range(PACK):
+                nc.scalar.activation(out=factor[g][:, j, :], in_=ts_free[:], func=ACT.Copy, scale=wt_rows[:, g, j : j + 1])
+
+        make_factor(0, "factor0")
+
         w_picked = keep.tile([P, PACK, N], F32, name="w_picked")
         w_grouped = grouped_tile("w_grouped")
         w_mx = mx_tiles("w")
-        for j in range(PACK - 1):
+        for j in range(PACK):
             nc.vector.tensor_copy(w_picked[:, j, :], w_table[j][:].indirect(offsets[:]))
+        for q in range(PACK):
+            nc.vector.tensor_copy(
+                out=w_grouped[:, q * P : (q + 1) * P, :].rearrange("p (b c i) j -> p b c j i", c=2, i=4),
+                in_=w_picked[:].rearrange("p j (b q c i) -> p q b c j i", q=PACK, c=2, i=4)[:, q],
+            )
         for slots in column_halves:
-            listed = offsets[:, slots.start // LIST_ROWS : slots.stop // LIST_ROWS]
-            nc.vector.tensor_copy(w_picked[:, PACK - 1, slots], w_table[PACK - 1][:].indirect(listed))
-        for slots in column_halves:
-            group(nc.vector.tensor_copy, w_grouped, w_picked, slots)
-        for slots in column_halves:
-            quantize(w_mx, w_grouped, slots, E4M3)
+            quantize(w_mx, slots, w_grouped[:, slots, :], E4M3)
 
         x_grouped = [grouped_tile(f"x_grouped{g}") for g in range(HALVES)]
         x_mx = [mx_tiles(f"x{g}") for g in range(HALVES)]
+        group(nc.scalar.copy, x_grouped[0][:, 0:HALF, :], x0_raw[0][:])
+        quantize(x_mx[0], column_halves[0], x_grouped[0][:, 0:HALF, :], E4M3)
+        group(nc.scalar.copy, x_grouped[0][:, HALF : HALF + P, :], x0_raw[1][:, :, 0:P])
+        group(nc.vector.tensor_copy, x_grouped[0][:, HALF + P :, :], x0_raw[1][:, :, P:])
+        quantize(x_mx[0], column_halves[1], x_grouped[0][:, HALF:, :], E4M3)
 
-        def prepare_x(g):
-            group(nc.scalar.copy, x_grouped[g], x_raw[g], slice(0, X_ON_SCALAR))
-            group(nc.vector.tensor_copy, x_grouped[g], x_raw[g], slice(X_ON_SCALAR, K_PASS))
-            quantize(x_mx[g], x_grouped[g], whole, E4M3)
-
-        prepare_x(0)
+        group(nc.vector.tensor_copy, x_grouped[1][:], x1_raw[:])
+        quantize(x_mx[1], whole, x_grouped[1][:], E4M3)
+        windows.append(keep.tile([P, T], F32, name="window2", tag="x_grouped0", align_bytes=64))
+        nc.vector.memset(windows[-1][:], 0.0)
 
         w_slots = grouped_tile("w_slots")
-        w_slots_mx = mx_tiles("w_slots", tag="x_grouped0")
-        for j in range(PACK):
-            turned = banks[PAIR_BANK + j % 2]
+        w_slots_mx = mx_tiles("w_slots")
+
+        def turn(source, dest, mx, u, step, turned, fmt):
+            pairs = flat(source[:]).bitcast(F32)
             for q in range(PACK):
-                nc.tensor.transpose(turned[:, q * P : (q + 1) * P], w_picked[:, j, q:N:PACK], ident[:])
-            nc.scalar.copy(out=w_slots[:, j * P : (j + 1) * P, :], in_=turned[:].rearrange("m (q p) -> m p q", q=PACK))
-        quantize(w_slots_mx, w_slots, whole, E4M3)
-        late_window(nc.vector, T, "x_raw0")
+                nc.tensor.transpose(turned[:, q * P : (q + 1) * P], pairs[:, 2 * q * P + u : 2 * (q + 1) * P : 2], ident[:])
+            nc.scalar.copy(
+                out=dest[:, column_halves[u], :].rearrange("m (e p) q -> m e p q", e=2),
+                in_=turned[:].bitcast(BF16).rearrange("m (q p e) -> m e p q", q=PACK, e=2),
+            )
+            quantize(mx, column_halves[u], dest[:, column_halves[u], :], fmt)
+
+        def turn_w(u, turned):
+            turn(w_grouped, w_slots, w_slots_mx, u, 0, turned, E4M3)
 
         h_rows = [grouped_tile(f"h_rows{g}") for g in range(HALVES)]
         h_rows_mx = [mx_tiles(f"h_rows{g}") for g in range(HALVES)]
         h_cols = [grouped_tile(f"h_cols{g}") for g in range(HALVES)]
         h_cols_mx = [mx_tiles(f"h_cols{g}") for g in range(HALVES)]
+        xm_grouped = [[grouped_tile(f"xm_grouped{a}{g}", HALF) for g in range(HALVES)] for a in range(2)]
+        xm_mx = [mx_tiles(f"xm{g}") for g in range(HALVES)]
         units = [(g, t) for g in range(HALVES) for t in range(BLOCKS)]
-        probs = {}
         diffs = {}
 
         def score(n):
             g, t = units[n]
-            scores = banks[n % SCORE_BANKS]
+            scores = banks[SCORE_BANK + n % 3]
             matmul(scores[:], w_mx, slice(t * P, (t + 1) * P), E4M3, x_mx[g], E4M3, True, True)
-            probs[n] = ring.tile([P, K_PASS], F32, name="prob", bufs=SCORE_BANKS + 1)
+            prob = ring.tile([P, PACK, P], F32, name="prob")
             nc.scalar.activation(
-                out=probs[n][:].rearrange("m (u p e) -> m u p e", u=2, e=2),
-                in_=scores[:].rearrange("m (p u e) -> m u p e", u=2, e=2),
+                out=prob[:],
+                in_=scores[:].rearrange("m (p j) -> m j p", j=PACK),
                 func=ACT.Sigmoid,
                 bias=kb_slot[:, t : t + 1],
                 scale=ts_slot[:, t : t + 1],
             )
-
-        def label_bank(n):
-            return banks[SCORE_BANKS + n % LABEL_BANKS]
-
-        def turn_labels(n):
-            g, t = units[n]
+            turned = banks[TURN_BANK + n % 3]
             for j in range(PACK):
-                nc.tensor.transpose(label_bank(n)[:, j * P : (j + 1) * P], y_raw[g][:, j, t * P : (t + 1) * P], ident[:])
-
-        def difference(n):
-            diffs[n] = ring.tile([P, K_PASS], F32, name="diff")
+                nc.tensor.transpose(turned[:, j * P : (j + 1) * P], prob[:, j, :], ident[:])
+            diffs[n] = ring.tile([P, PACK, P], F32, name="diff")
             nc.vector.tensor_tensor(
-                out=diffs[n][:].rearrange("m (u p e) -> m u p e", u=2, e=2),
-                in0=probs[n][:].rearrange("m (u p e) -> m u p e", u=2, e=2),
-                in1=label_bank(n)[:].rearrange("m (u e p) -> m u p e", u=2, e=2),
+                out=diffs[n][:].rearrange("p j (b m) -> p j b m", m=RUN),
+                in0=turned[:].rearrange("p (j b m) -> p j b m", j=PACK, m=RUN),
+                in1=y_raw[g][:].rearrange("p j (b q m) -> p q j b m", q=PACK, m=RUN)[:, t],
                 op=ALU.subtract,
             )
 
         def weigh(n):
             g, t = units[n]
-            if n == len(units) - 1:
-                first = 2 * K_PASS - 3 * K_PASS // 4
-                h_unit = flat(h_cols[0][:])[:, first : first + K_PASS]
-            else:
-                h_unit = ring.tile([P, K_PASS], BF16, name="h_unit")[:]
-            nc.vector.scalar_tensor_tensor(
-                out=h_unit,
-                in0=diffs[n][:],
-                scalar=ts_slot[:, t : t + 1],
-                in1=wt_free[g][:],
-                op0=ALU.mult,
-                op1=ALU.mult,
+            slots = slice(t * P, (t + 1) * P)
+            nc.vector.tensor_tensor(
+                out=h_rows[g][:, slots, :].rearrange("p (c i) j -> p c j i", i=2),
+                in0=diffs[n][:].rearrange("p j (c i) -> p c j i", i=2),
+                in1=factor[g][:, :, slots].rearrange("p j (c i) -> p c j i", i=2),
+                op=ALU.mult,
             )
-            turned = banks[PAIR_BANK + t // 2]
-            pairs = h_unit.bitcast(F32)
-            for u in range(2):
-                place = u * 2 * P + (t % 2) * P
-                nc.tensor.transpose(turned[:, place : place + P], pairs[:, u * P : (u + 1) * P], ident[:])
-            if t % 2 == 1:
-                by_q = flat(h_rows[g][:]).bitcast(F32).rearrange("p (q m u) -> p q m u", q=PACK, u=2)
-                nc.scalar.copy(
-                    out=by_q[:, :, (t - 1) * P // PACK : (t + 1) * P // PACK, :],
-                    in_=turned[:].rearrange("p (u m q) -> p q m u", u=2, q=PACK),
-                )
 
-        for n in range(SCORE_BANKS):
-            score(n)
-        turn_labels(0)
-        difference(0)
-        turn_labels(1)
+        def turn_h(g, u, turned):
+            turn(h_rows[g], h_cols[g], h_cols_mx[g], u, 0, turned, E5M2)
+
+        def prepare_xm(copy, a, g):
+            group(copy, xm_grouped[a][g][:], xm_raw[a][g][:])
+            quantize(xm_mx[g], column_halves[a], xm_grouped[a][g][:], E4M3)
+
+        score(0)
         for n in range(len(units)):
-            if n == 0:
-                prepare_x(1)
-            if n + SCORE_BANKS < len(units):
-                score(n + SCORE_BANKS)
-            if n + 2 < len(units):
-                turn_labels(n + 2)
             if n + 1 < len(units):
-                difference(n + 1)
+                score(n + 1)
+            if n == 1:
+                make_factor(1, "x0_raw1")
             weigh(n)
             if n == BLOCKS:
-                quantize(h_rows_mx[0], h_rows[0], whole, E5M2)
-        late_window(nc.gpsimd, K_PASS, "y_raw0")
-        quantize(h_rows_mx[1], h_rows[1], whole, E5M2)
-
-        xm_grouped = [grouped_tile(f"xm_grouped{g}") for g in range(HALVES)]
-        xm_mx = [mx_tiles(f"xm{g}") for g in range(HALVES)]
-        xm_pieces = [(g, cols) for g in range(HALVES) for cols in column_halves]
-        for n, (g, cols) in enumerate(xm_pieces):
-            copy = nc.scalar.copy if n < XM_PIECES_ON_SCALAR else nc.vector.tensor_copy
-            group(copy, xm_grouped[g], xm_raw[g], cols)
-        for g, cols in xm_pieces:
-            quantize(xm_mx[g], xm_grouped[g], cols, E4M3)
+                quantize(h_rows_mx[0], whole, h_rows[0][:], E5M2)
+            if n > BLOCKS and n - BLOCKS - 1 < HALVES:
+                prepare_xm(nc.scalar.copy, 0, n - BLOCKS - 1)
+        for cols in column_halves:
+            quantize(h_rows_mx[1], cols, h_rows[1][:, cols, :], E5M2)
 
         out_1_hbm = out_1[0].rearrange("(g p u e) d -> g u p e d", g=HALVES, u=2, e=2)
 
@@ -281,23 +252,15 @@ def tile_attend_gnce_wx_ts_kb_kernel(tc, xT, wT, y, wt, ts, kb, xm, offs, out_0,
                 matmul(acc[:], xm_mx[g], features, E4M3, h_rows_mx[g], E5M2, g == 0, g == HALVES - 1)
             dense = ring.tile([P, N], F32, name="dense", bufs=BLOCKS)
             nc.scalar.copy(
-                out=dense[:].rearrange("d (m q) -> d m q", q=PACK),
-                in_=acc[:].rearrange("d (q m) -> d m q", q=PACK),
+                out=dense[:].rearrange("d (b q m) -> d b q m", q=PACK, m=RUN),
+                in_=acc[:].rearrange("d (q b m) -> d b q m", q=PACK, m=RUN),
             )
-            nc.vector.tensor_copy(windows[c][:].indirect(offsets[:]), dense[:])
-            nc.sync.dma_start(out=out_0[features, :], in_=windows[c][:])
-
-        def turn_h(g, u, turned):
-            pairs = flat(h_rows[g][:]).bitcast(F32)
-            for q in range(PACK):
-                nc.tensor.transpose(turned[:, q * P : (q + 1) * P], pairs[:, 2 * q * P + u : 2 * (q + 1) * P : 2], ident[:])
-            nc.scalar.copy(
-                out=h_cols[g][:, column_halves[u], :].rearrange("m (e p) q -> m e p q", e=2),
-                in_=turned[:].bitcast(BF16).rearrange("m (q p e) -> m e p q", q=PACK, e=2),
-            )
+            window = windows[c % WINDOWS]
+            nc.vector.tensor_copy(window[:].indirect(offsets[:]), dense[:])
+            nc.sync.dma_start(out=out_0[features, :], in_=window[:])
 
         def row_gradient(g, u, accs):
-            staged = ring.tile([P, 2, D], F32, name="staged", bufs=2 * HALVES)
+            staged = keep.tile([P, 2, D], F32, name=f"staged{g}{u}", tag=f"w_table{2 * g + u}")
             for e in range(2):
                 first = (2 * u + e) * P
                 matmul(accs[e][:], h_cols_mx[g], slice(first, first + P), E5M2, w_slots_mx, E4M3, True, True)
@@ -308,18 +271,18 @@ def tile_attend_gnce_wx_ts_kb_kernel(tc, xT, wT, y, wt, ts, kb, xm, offs, out_0,
             nc.scalar.dma_start(out=out_1_hbm[g, u], in_=staged[:])
 
         table_gradient(0, banks[0])
-        for u in range(2):
-            turn_h(0, u, banks[2 + u])
-        for cols in column_halves:
-            quantize(h_cols_mx[0], h_cols[0], cols, E5M2)
-        table_gradient(1, banks[1])
+        turn_w(0, banks[7])
+        turn_w(1, banks[7])
+        turn_h(0, 0, banks[3])
+        turn_h(0, 1, banks[7])
+        for g in range(HALVES):
+            prepare_xm(nc.scalar.copy, 1, g)
         row_gradient(0, 0, banks[2:4])
         row_gradient(0, 1, banks[4:6])
-        for u in range(2):
-            turn_h(1, u, banks[2 + u])
-        for cols in column_halves:
-            quantize(h_cols_mx[1], h_cols[1], cols, E5M2)
-        table_gradient(2, banks[2])
-        row_gradient(1, 0, banks[0:2])
-        table_gradient(3, banks[3])
-        row_gradient(1, 1, banks[4:6])
+        turn_h(1, 0, banks[0])
+        table_gradient(1, banks[1])
+        turn_h(1, 1, banks[2])
+        table_gradient(2, banks[6])
+        row_gradient(1, 0, banks[3:5])
+        table_gradient(3, banks[7])
+        row_gradient(1, 1, banks[0:2])

@@ -106,9 +106,10 @@ def tile_attend_gnce_wx_ts_kb_kernel(tc, xT, wT, y, wt, ts, kb, xm, offs, out_0,
         warm = keep.tile([P, HALVES * PACK], F32, name="warm")
         nc.scalar.activation(out=warm[:], in_=wt_rows[:].rearrange("p g j -> p (g j)"), func=ACT.Sigmoid)
 
-        windows = [keep.tile([P, T], F32, name=f"window{c}") for c in range(WINDOWS - 1)]
+        windows = [keep.tile([P, T], F32, name=f"window{c}") for c in range(WINDOWS)]
         for window in windows:
-            nc.vector.memset(window[:], 0.0)
+            for first in range(0, T, K_PASS):
+                nc.gpsimd.memset(window[:, first : first + K_PASS], 0.0)
 
         per_slot = []
         for n, (name, table) in enumerate((("ts", ts_table), ("kb", kb_table))):
@@ -162,8 +163,6 @@ def tile_attend_gnce_wx_ts_kb_kernel(tc, xT, wT, y, wt, ts, kb, xm, offs, out_0,
 
         group(nc.vector.tensor_copy, x_grouped[1][:], x1_raw[:])
         quantize(x_mx[1], whole, x_grouped[1][:], E4M3)
-        windows.append(keep.tile([P, T], F32, name="window2", tag="x_grouped0", align_bytes=64))
-        nc.vector.memset(windows[-1][:], 0.0)
 
         w_slots = grouped_tile("w_slots")
         w_slots_mx = mx_tiles("w_slots")

@@ -23,7 +23,7 @@ HALVES = R // K_PASS
 BLOCKS = N // P
 LIST_ROWS = 16
 SCORE_BANK = 0
-TURN_BANK = 4
+TURN_BANK = 3
 WINDOWS = 3
 RUN = 8
 
@@ -40,8 +40,8 @@ def tile_attend_gnce_wx_ts_kb_kernel(tc, xT, wT, y, wt, ts, kb, xm, offs, out_0,
         HALF = K_PASS // 2
         column_halves = [slice(0, HALF), slice(HALF, K_PASS)]
 
-        def mx_tiles(name):
-            codes = keep.tile([P, K_PASS], U32, name=name + "_codes", align_bytes=64)
+        def mx_tiles(name, tag=None):
+            codes = keep.tile([P, K_PASS], U32, name=name + "_codes", tag=tag or name + "_codes", align_bytes=64)
             scales = keep.tile([P, K_PASS], U8, name=name + "_scales", align_bytes=64)
             return codes, scales
 
@@ -81,7 +81,9 @@ def tile_attend_gnce_wx_ts_kb_kernel(tc, xT, wT, y, wt, ts, kb, xm, offs, out_0,
         wt_rows = keep.tile([P, HALVES, PACK], F32, name="wt_rows")
         nc.scalar.dma_start(out=wt_rows[:], in_=wt[0].rearrange("(g p j) o -> p g (j o)", g=HALVES, j=PACK))
 
-        x0_raw = [keep.tile([P, PACK, HALF], F32, name=f"x0_raw{a}", tag=f"x0_raw{a}") for a in range(2)]
+        factor = [keep.tile([P, PACK, N], F32, name=f"factor{g}") for g in range(HALVES)]
+        x0_second = keep.tile([P, PACK, HALF], F32, name="x0_second", tag="w_slots", align_bytes=64)
+        x0_raw = [factor[1][:, :, 0:HALF], x0_second[:]]
         x1_raw = keep.tile([P, PACK, K_PASS], F32, name="x1_raw")
         y_raw = [keep.tile([P, PACK, N], F32, name=f"y_raw{g}") for g in range(HALVES)]
         xm_raw = [[keep.tile([P, PACK, HALF], F32, name=f"xm_raw{a}{g}") for g in range(HALVES)] for a in range(2)]
@@ -93,7 +95,7 @@ def tile_attend_gnce_wx_ts_kb_kernel(tc, xT, wT, y, wt, ts, kb, xm, offs, out_0,
         loads = [(w_table[j][:], w_hbm[j]) for j in range(PACK)]
         loads.insert(1, (ts_table[0:1, :], ts[0:1, :]))
         loads.insert(3, (kb_table[0:1, :], kb[0:1, :]))
-        loads.extend((x0_raw[a][:], x_hbm[0][:, :, column_halves[a]]) for a in range(2))
+        loads.extend((x0_raw[a], x_hbm[0][:, :, column_halves[a]]) for a in range(2))
         loads.append((x1_raw[:], x_hbm[1]))
         loads.extend((y_raw[g][:], y_hbm[g]) for g in range(HALVES))
         loads.extend((xm_raw[a][g][:], xm_hbm[g][:, :, column_halves[a]]) for a in range(2) for g in range(HALVES))
@@ -111,40 +113,39 @@ def tile_attend_gnce_wx_ts_kb_kernel(tc, xT, wT, y, wt, ts, kb, xm, offs, out_0,
             for first in range(0, T, K_PASS):
                 nc.gpsimd.memset(window[:, first : first + K_PASS], 0.0)
 
+        w_picked = keep.tile([P, PACK, N], F32, name="w_picked", tag="w_picked")
+
         per_slot = []
         for n, (name, table) in enumerate((("ts", ts_table), ("kb", kb_table))):
             picked = keep.tile([P, N], F32, name=name + "_picked")
             nc.vector.tensor_copy(picked[:], table[:].indirect(offsets[:]))
             dealt = keep.tile([P, N], F32, name=name + "_dealt")
-            nc.scalar.copy(
+            nc.vector.tensor_copy(
                 out=dealt[:].rearrange("p (q b m) -> p b q m", q=PACK, m=RUN),
                 in_=picked[:].rearrange("p (b q m) -> p b q m", q=PACK, m=RUN),
             )
-            turned = banks[SCORE_BANK + n]
+            turned = banks[TURN_BANK + n]
             for t in range(BLOCKS):
                 nc.tensor.transpose(turned[:, t * P : (t + 1) * P], dealt[:, t * P : (t + 1) * P], ident[:])
             column = keep.tile([P, BLOCKS], F32, name=name + "_slot")
             nc.scalar.copy(out=column[:], in_=turned[:, 0:N:P])
             per_slot.append(column)
         ts_slot, kb_slot = per_slot
-
-        ts_free = banks[TURN_BANK + 3]
+        ts_free = banks[7]
         for t in range(BLOCKS):
-            nc.tensor.transpose(ts_free[:, t * P : (t + 1) * P], ts_slot[:, t : t + 1].to_broadcast([P, P]), ident[:])
-        factor = {}
+            repeated = ts_slot[:, t : t + 1].to_broadcast([P, P])
+            nc.tensor.transpose(ts_free[:, t * P : (t + 1) * P], repeated, ident[:])
 
-        def make_factor(g, tag):
-            factor[g] = keep.tile([P, PACK, N], F32, name=f"factor{g}", tag=tag)
-            for j in range(PACK):
-                nc.scalar.activation(out=factor[g][:, j, :], in_=ts_free[:], func=ACT.Copy, scale=wt_rows[:, g, j : j + 1])
+        def make_factor(g, j):
+            nc.scalar.activation(out=factor[g][:, j, :], in_=ts_free[:], func=ACT.Copy, scale=wt_rows[:, g, j : j + 1])
 
-        make_factor(0, "factor0")
+        for j in range(PACK):
+            make_factor(0, j)
 
-        w_picked = keep.tile([P, PACK, N], F32, name="w_picked")
-        w_grouped = grouped_tile("w_grouped")
         w_mx = mx_tiles("w")
         for j in range(PACK):
             nc.vector.tensor_copy(w_picked[:, j, :], w_table[j][:].indirect(offsets[:]))
+        w_grouped = grouped_tile("w_grouped")
         for q in range(PACK):
             nc.vector.tensor_copy(
                 out=w_grouped[:, q * P : (q + 1) * P, :].rearrange("p (b c i) j -> p b c j i", c=2, i=4),
@@ -155,37 +156,35 @@ def tile_attend_gnce_wx_ts_kb_kernel(tc, xT, wT, y, wt, ts, kb, xm, offs, out_0,
 
         x_grouped = [grouped_tile(f"x_grouped{g}") for g in range(HALVES)]
         x_mx = [mx_tiles(f"x{g}") for g in range(HALVES)]
-        group(nc.scalar.copy, x_grouped[0][:, 0:HALF, :], x0_raw[0][:])
+        group(nc.scalar.copy, x_grouped[0][:, 0:HALF, :], x0_raw[0])
         quantize(x_mx[0], column_halves[0], x_grouped[0][:, 0:HALF, :], E4M3)
         group(nc.scalar.copy, x_grouped[0][:, HALF : HALF + P, :], x0_raw[1][:, :, 0:P])
         group(nc.vector.tensor_copy, x_grouped[0][:, HALF + P :, :], x0_raw[1][:, :, P:])
         quantize(x_mx[0], column_halves[1], x_grouped[0][:, HALF:, :], E4M3)
-
         group(nc.vector.tensor_copy, x_grouped[1][:], x1_raw[:])
         quantize(x_mx[1], whole, x_grouped[1][:], E4M3)
 
         w_slots = grouped_tile("w_slots")
-        w_slots_mx = mx_tiles("w_slots")
 
-        def turn(source, dest, mx, u, step, turned, fmt):
-            pairs = flat(source[:]).bitcast(F32)
+        def turn(blocks, dest, u, turned):
             for q in range(PACK):
-                nc.tensor.transpose(turned[:, q * P : (q + 1) * P], pairs[:, 2 * q * P + u : 2 * (q + 1) * P : 2], ident[:])
+                pairs = flat(blocks[q]).bitcast(F32)
+                nc.tensor.transpose(turned[:, q * P : (q + 1) * P], pairs[:, u : 2 * P : 2], ident[:])
             nc.scalar.copy(
-                out=dest[:, column_halves[u], :].rearrange("m (e p) q -> m e p q", e=2),
+                out=dest.rearrange("m (e p) q -> m e p q", e=2),
                 in_=turned[:].bitcast(BF16).rearrange("m (q p e) -> m e p q", q=PACK, e=2),
             )
-            quantize(mx, column_halves[u], dest[:, column_halves[u], :], fmt)
 
         def turn_w(u, turned):
-            turn(w_grouped, w_slots, w_slots_mx, u, 0, turned, E4M3)
+            blocks = [w_grouped[:, q * P : (q + 1) * P, :] for q in range(PACK)]
+            turn(blocks, w_slots[:, column_halves[u], :], u, turned)
 
         h_rows = [grouped_tile(f"h_rows{g}") for g in range(HALVES)]
         h_rows_mx = [mx_tiles(f"h_rows{g}") for g in range(HALVES)]
-        h_cols = [grouped_tile(f"h_cols{g}") for g in range(HALVES)]
+        h_cols0 = grouped_tile("h_cols0")
         h_cols_mx = [mx_tiles(f"h_cols{g}") for g in range(HALVES)]
         xm_grouped = [[grouped_tile(f"xm_grouped{a}{g}", HALF) for g in range(HALVES)] for a in range(2)]
-        xm_mx = [mx_tiles(f"xm{g}") for g in range(HALVES)]
+        xm_mx = {}
         units = [(g, t) for g in range(HALVES) for t in range(BLOCKS)]
         diffs = {}
 
@@ -201,7 +200,7 @@ def tile_attend_gnce_wx_ts_kb_kernel(tc, xT, wT, y, wt, ts, kb, xm, offs, out_0,
                 bias=kb_slot[:, t : t + 1],
                 scale=ts_slot[:, t : t + 1],
             )
-            turned = banks[TURN_BANK + n % 3]
+            turned = banks[TURN_BANK + n % 4]
             for j in range(PACK):
                 nc.tensor.transpose(turned[:, j * P : (j + 1) * P], prob[:, j, :], ident[:])
             diffs[n] = ring.tile([P, PACK, P], F32, name="diff")
@@ -223,18 +222,35 @@ def tile_attend_gnce_wx_ts_kb_kernel(tc, xT, wT, y, wt, ts, kb, xm, offs, out_0,
             )
 
         def turn_h(g, u, turned):
-            turn(h_rows[g], h_cols[g], h_cols_mx[g], u, 0, turned, E5M2)
+            blocks = [h_rows[g][:, q * P : (q + 1) * P, :] for q in range(PACK)]
+            if g == 0:
+                turn(blocks, h_cols0[:, column_halves[u], :], u, turned)
+            else:
+                dest = grouped_tile(f"h_cols1{u}", HALF)
+                turn(blocks, dest[:], u, turned)
+                quantize(h_cols_mx[1], column_halves[u], dest[:], E5M2)
 
         def prepare_xm(copy, a, g):
             group(copy, xm_grouped[a][g][:], xm_raw[a][g][:])
-            quantize(xm_mx[g], column_halves[a], xm_grouped[a][g][:], E4M3)
+            pieces = [(0, P), (P, P)] if (a, g) == (0, 1) else [(0, HALF)]
+            for first, width in pieces:
+                name = f"xm{a}{g}{first}"
+                tag = f"h_cols1{first // P}" if (a, g) == (0, 1) else name
+                codes = keep.tile([P, width], U32, name=name, tag=tag, align_bytes=64)
+                scales = keep.tile([P, width], U8, name=name + "_scales", align_bytes=64)
+                quantize((codes, scales), slice(0, width), xm_grouped[a][g][:, first : first + width, :], E4M3)
+                for c in range(width // P):
+                    xm_mx[g, 2 * a + first // P + c] = ((codes, scales), slice(c * P, (c + 1) * P))
 
         score(0)
         for n in range(len(units)):
             if n + 1 < len(units):
                 score(n + 1)
-            if n == 1:
-                make_factor(1, "x0_raw1")
+            if n < 2:
+                turn_w(n, banks[6])
+            if n == BLOCKS:
+                for j in range(PACK):
+                    make_factor(1, j)
             weigh(n)
             if n == BLOCKS:
                 quantize(h_rows_mx[0], whole, h_rows[0][:], E5M2)
@@ -248,8 +264,9 @@ def tile_attend_gnce_wx_ts_kb_kernel(tc, xT, wT, y, wt, ts, kb, xm, offs, out_0,
         def table_gradient(c, acc):
             features = slice(c * P, (c + 1) * P)
             for g in range(HALVES):
-                matmul(acc[:], xm_mx[g], features, E4M3, h_rows_mx[g], E5M2, g == 0, g == HALVES - 1)
-            dense = ring.tile([P, N], F32, name="dense", bufs=BLOCKS)
+                matmul(acc[:], xm_mx[g, c][0], xm_mx[g, c][1], E4M3, h_rows_mx[g], E5M2, g == 0, g == HALVES - 1)
+            tag = f"dense{c}"
+            dense = keep.tile([P, N], F32, name=f"dense{c}", tag=tag, align_bytes=64)
             nc.scalar.copy(
                 out=dense[:].rearrange("d (b q m) -> d b q m", q=PACK, m=RUN),
                 in_=acc[:].rearrange("d (q b m) -> d b q m", q=PACK, m=RUN),
@@ -270,18 +287,19 @@ def tile_attend_gnce_wx_ts_kb_kernel(tc, xT, wT, y, wt, ts, kb, xm, offs, out_0,
             nc.scalar.dma_start(out=out_1_hbm[g, u], in_=staged[:])
 
         table_gradient(0, banks[0])
-        turn_w(0, banks[7])
-        turn_w(1, banks[7])
-        turn_h(0, 0, banks[3])
-        turn_h(0, 1, banks[7])
-        for g in range(HALVES):
-            prepare_xm(nc.scalar.copy, 1, g)
-        row_gradient(0, 0, banks[2:4])
-        row_gradient(0, 1, banks[4:6])
-        turn_h(1, 0, banks[0])
+        turn_h(0, 0, banks[7])
+        turn_h(0, 1, banks[2])
+        w_slots_mx = mx_tiles("w_slots", tag="x1_codes")
+        quantize(w_slots_mx, whole, w_slots[:], E4M3)
+        quantize(h_cols_mx[0], whole, h_cols0[:], E5M2)
+        prepare_xm(nc.scalar.copy, 1, 0)
+        prepare_xm(nc.scalar.copy, 1, 1)
+        turn_h(1, 0, banks[5])
+        row_gradient(0, 0, banks[3:5])
         table_gradient(1, banks[1])
-        turn_h(1, 1, banks[2])
-        table_gradient(2, banks[6])
+        row_gradient(0, 1, [banks[7], banks[2]])
+        turn_h(1, 1, banks[6])
+        table_gradient(2, banks[0])
         row_gradient(1, 0, banks[3:5])
-        table_gradient(3, banks[7])
-        row_gradient(1, 1, banks[0:2])
+        table_gradient(3, banks[1])
+        row_gradient(1, 1, [banks[7], banks[2]])

@@ -9,6 +9,7 @@ FLOPS = 3 * 2 * R * D * N
 F32 = mybir.dt.float32
 BF16 = mybir.dt.bfloat16
 U32 = mybir.dt.uint32
+I32 = mybir.dt.int32
 U16 = mybir.dt.uint16
 U8 = mybir.dt.uint8
 E4M3 = mybir.dt.float8_e4m3fn_x4
@@ -23,7 +24,7 @@ HALVES = R // K_PASS
 BLOCKS = N // P
 LIST_ROWS = 16
 SCORE_BANK = 0
-TURN_BANK = 3
+TURN_BANK = 4
 WINDOWS = 3
 RUN = 8
 
@@ -81,9 +82,7 @@ def tile_attend_gnce_wx_ts_kb_kernel(tc, xT, wT, y, wt, ts, kb, xm, offs, out_0,
         wt_rows = keep.tile([P, HALVES, PACK], F32, name="wt_rows")
         nc.scalar.dma_start(out=wt_rows[:], in_=wt[0].rearrange("(g p j) o -> p g (j o)", g=HALVES, j=PACK))
 
-        factor = [keep.tile([P, PACK, N], F32, name=f"factor{g}") for g in range(HALVES)]
-        x0_second = keep.tile([P, PACK, HALF], F32, name="x0_second", tag="w_slots", align_bytes=64)
-        x0_raw = [factor[1][:, :, 0:HALF], x0_second[:]]
+        x0_raw = [keep.tile([P, PACK, HALF], F32, name=f"x0_raw{a}")[:] for a in range(2)]
         x1_raw = keep.tile([P, PACK, K_PASS], F32, name="x1_raw")
         y_raw = [keep.tile([P, PACK, N], F32, name=f"y_raw{g}") for g in range(HALVES)]
         xm_raw = [[keep.tile([P, PACK, HALF], F32, name=f"xm_raw{a}{g}") for g in range(HALVES)] for a in range(2)]
@@ -105,8 +104,6 @@ def tile_attend_gnce_wx_ts_kb_kernel(tc, xT, wT, y, wt, ts, kb, xm, offs, out_0,
         ident = keep.tile([P, P], F32, name="ident")
         make_identity(nc, ident[:])
 
-        warm = keep.tile([P, HALVES * PACK], F32, name="warm")
-        nc.scalar.activation(out=warm[:], in_=wt_rows[:].rearrange("p g j -> p (g j)"), func=ACT.Sigmoid)
 
         windows = [keep.tile([P, T], F32, name=f"window{c}") for c in range(WINDOWS)]
         for window in windows:
@@ -128,19 +125,24 @@ def tile_attend_gnce_wx_ts_kb_kernel(tc, xT, wT, y, wt, ts, kb, xm, offs, out_0,
             for t in range(BLOCKS):
                 nc.tensor.transpose(turned[:, t * P : (t + 1) * P], dealt[:, t * P : (t + 1) * P], ident[:])
             column = keep.tile([P, BLOCKS], F32, name=name + "_slot")
-            nc.scalar.copy(out=column[:], in_=turned[:, 0:N:P])
+            nc.scalar.activation(out=column[:], in_=turned[:, 0:N:P], func=ACT.Copy)
             per_slot.append(column)
         ts_slot, kb_slot = per_slot
-        ts_free = banks[7]
+        ts_free = banks[0]
         for t in range(BLOCKS):
             repeated = ts_slot[:, t : t + 1].to_broadcast([P, P])
             nc.tensor.transpose(ts_free[:, t * P : (t + 1) * P], repeated, ident[:])
 
-        def make_factor(g, j):
-            nc.scalar.activation(out=factor[g][:, j, :], in_=ts_free[:], func=ACT.Copy, scale=wt_rows[:, g, j : j + 1])
+        factor = {}
 
-        for j in range(PACK):
-            make_factor(0, j)
+        def make_factor(g, source, tag):
+            factor[g] = keep.tile([P, PACK, N], F32, name=f"factor{g}", tag=tag, align_bytes=64)
+            for j in range(PACK):
+                nc.scalar.activation(out=factor[g][:, j, :], in_=source[:], func=ACT.Copy, scale=wt_rows[:, g, j : j + 1])
+
+        make_factor(0, ts_free, "factor0")
+        ts_kept = keep.tile([P, N], F32, name="ts_kept")
+        nc.scalar.copy(out=ts_kept[:], in_=ts_free[:])
 
         w_mx = mx_tiles("w")
         for j in range(PACK):
@@ -161,36 +163,45 @@ def tile_attend_gnce_wx_ts_kb_kernel(tc, xT, wT, y, wt, ts, kb, xm, offs, out_0,
         group(nc.scalar.copy, x_grouped[0][:, HALF : HALF + P, :], x0_raw[1][:, :, 0:P])
         group(nc.vector.tensor_copy, x_grouped[0][:, HALF + P :, :], x0_raw[1][:, :, P:])
         quantize(x_mx[0], column_halves[1], x_grouped[0][:, HALF:, :], E4M3)
+
+        def split_pairs(name, grouped, tag):
+            pairs = keep.tile([P, 2, K_PASS], F32, name=name, tag=tag, align_bytes=64)
+            nc.vector.tensor_copy(
+                out=pairs[:].bitcast(I32).rearrange("p u (c i) -> p c u i", i=4),
+                in_=flat(grouped[:]).bitcast(I32).rearrange("p (c i u) -> p c u i", u=2, i=4),
+            )
+            return pairs
+
+        w_pairs = split_pairs("w_pairs", w_grouped, "x_grouped0")
         group(nc.vector.tensor_copy, x_grouped[1][:], x1_raw[:])
         quantize(x_mx[1], whole, x_grouped[1][:], E4M3)
 
-        w_slots = grouped_tile("w_slots")
-
-        def turn(blocks, dest, u, turned):
+        def turn(blocks, dest, turned):
             for q in range(PACK):
-                pairs = flat(blocks[q]).bitcast(F32)
-                nc.tensor.transpose(turned[:, q * P : (q + 1) * P], pairs[:, u : 2 * P : 2], ident[:])
+                nc.tensor.transpose(turned[:, q * P : (q + 1) * P], blocks[q], ident[:])
             nc.scalar.copy(
                 out=dest.rearrange("m (e p) q -> m e p q", e=2),
                 in_=turned[:].bitcast(BF16).rearrange("m (q p e) -> m e p q", q=PACK, e=2),
             )
 
+        w_slots = grouped_tile("w_slots")
+        w_slots_mx = mx_tiles("w_slots")
+
         def turn_w(u, turned):
-            blocks = [w_grouped[:, q * P : (q + 1) * P, :] for q in range(PACK)]
-            turn(blocks, w_slots[:, column_halves[u], :], u, turned)
+            turn([w_pairs[:, u, q * P : (q + 1) * P] for q in range(PACK)], w_slots[:, column_halves[u], :], turned)
 
         h_rows = [grouped_tile(f"h_rows{g}") for g in range(HALVES)]
         h_rows_mx = [mx_tiles(f"h_rows{g}") for g in range(HALVES)]
-        h_cols0 = grouped_tile("h_cols0")
+        h_cols = [grouped_tile(f"h_cols{g}") for g in range(HALVES)]
+        h_pairs = {}
         h_cols_mx = [mx_tiles(f"h_cols{g}") for g in range(HALVES)]
-        xm_grouped = [[grouped_tile(f"xm_grouped{a}{g}", HALF) for g in range(HALVES)] for a in range(2)]
         xm_mx = {}
         units = [(g, t) for g in range(HALVES) for t in range(BLOCKS)]
         diffs = {}
 
         def score(n):
             g, t = units[n]
-            scores = banks[SCORE_BANK + n % 3]
+            scores = banks[SCORE_BANK + t]
             matmul(scores[:], w_mx, slice(t * P, (t + 1) * P), E4M3, x_mx[g], E4M3, True, True)
             prob = ring.tile([P, PACK, P], F32, name="prob")
             nc.scalar.activation(
@@ -200,9 +211,13 @@ def tile_attend_gnce_wx_ts_kb_kernel(tc, xT, wT, y, wt, ts, kb, xm, offs, out_0,
                 bias=kb_slot[:, t : t + 1],
                 scale=ts_slot[:, t : t + 1],
             )
-            turned = banks[TURN_BANK + n % 4]
+            turned = banks[TURN_BANK + t]
             for j in range(PACK):
                 nc.tensor.transpose(turned[:, j * P : (j + 1) * P], prob[:, j, :], ident[:])
+
+        def difference(n):
+            g, t = units[n]
+            turned = banks[TURN_BANK + t]
             diffs[n] = ring.tile([P, PACK, P], F32, name="diff")
             nc.vector.tensor_tensor(
                 out=diffs[n][:].rearrange("p j (b m) -> p j b m", m=RUN),
@@ -222,50 +237,62 @@ def tile_attend_gnce_wx_ts_kb_kernel(tc, xT, wT, y, wt, ts, kb, xm, offs, out_0,
             )
 
         def turn_h(g, u, turned):
-            blocks = [h_rows[g][:, q * P : (q + 1) * P, :] for q in range(PACK)]
-            if g == 0:
-                turn(blocks, h_cols0[:, column_halves[u], :], u, turned)
+            if g in h_pairs:
+                blocks = [h_pairs[g][:, u, q * P : (q + 1) * P] for q in range(PACK)]
             else:
-                dest = grouped_tile(f"h_cols1{u}", HALF)
-                turn(blocks, dest[:], u, turned)
-                quantize(h_cols_mx[1], column_halves[u], dest[:], E5M2)
+                pairs = flat(h_rows[g][:]).bitcast(F32)
+                blocks = [pairs[:, 2 * q * P + u : 2 * (q + 1) * P : 2] for q in range(PACK)]
+            turn(blocks, h_cols[g][:, column_halves[u], :], turned)
 
-        def prepare_xm(copy, a, g):
-            group(copy, xm_grouped[a][g][:], xm_raw[a][g][:])
-            pieces = [(0, P), (P, P)] if (a, g) == (0, 1) else [(0, HALF)]
-            for first, width in pieces:
-                name = f"xm{a}{g}{first}"
-                tag = f"h_cols1{first // P}" if (a, g) == (0, 1) else name
-                codes = keep.tile([P, width], U32, name=name, tag=tag, align_bytes=64)
-                scales = keep.tile([P, width], U8, name=name + "_scales", align_bytes=64)
-                quantize((codes, scales), slice(0, width), xm_grouped[a][g][:, first : first + width, :], E4M3)
-                for c in range(width // P):
-                    xm_mx[g, 2 * a + first // P + c] = ((codes, scales), slice(c * P, (c + 1) * P))
+        def quantize_h_cols(g, cols):
+            quantize(h_cols_mx[g], cols, h_cols[g][:, cols, :], E5M2)
+
+        def prepare_xm(a, g, tag, copy=nc.scalar.copy):
+            name = f"xm{a}{g}"
+            grouped = keep.tile([P, HALF, PACK], BF16, name=name + "_grouped", tag=tag, align_bytes=64)
+            group(copy, grouped[:], xm_raw[a][g][:])
+            codes = keep.tile([P, HALF], U32, name=name + "_codes", tag=name + "_codes", align_bytes=64)
+            scales = keep.tile([P, HALF], U8, name=name + "_scales", align_bytes=64)
+            quantize((codes, scales), slice(0, HALF), grouped[:], E4M3)
+            for c in range(2):
+                xm_mx[g, 2 * a + c] = ((codes, scales), slice(c * P, (c + 1) * P))
 
         score(0)
+        difference(0)
         for n in range(len(units)):
             if n + 1 < len(units):
                 score(n + 1)
-            if n < 2:
-                turn_w(n, banks[6])
-            if n == BLOCKS:
-                for j in range(PACK):
-                    make_factor(1, j)
+            if n + 1 < len(units) and n + 1 != BLOCKS:
+                difference(n + 1)
+            if n == BLOCKS - 1:
+                make_factor(1, ts_kept, "x0_codes")
             weigh(n)
-            if n == BLOCKS:
-                quantize(h_rows_mx[0], whole, h_rows[0][:], E5M2)
+            if n == BLOCKS - 1:
+                for cols in column_halves:
+                    quantize(h_rows_mx[0], cols, h_rows[0][:, cols, :], E5M2)
+                h_pairs[0] = split_pairs("h_pairs0", h_rows[0], "x_grouped1")
+                difference(BLOCKS)
             if n > BLOCKS and n - BLOCKS - 1 < HALVES:
-                prepare_xm(nc.scalar.copy, 0, n - BLOCKS - 1)
+                prepare_xm(0, n - BLOCKS - 1, f"xm0{n - BLOCKS - 1}_grouped")
         for cols in column_halves:
             quantize(h_rows_mx[1], cols, h_rows[1][:, cols, :], E5M2)
 
         out_1_hbm = out_1[0].rearrange("(g p u e) d -> g u p e d", g=HALVES, u=2, e=2)
 
+        def table_first_half(c, acc):
+            matmul(acc[:], xm_mx[0, c][0], xm_mx[0, c][1], E4M3, h_rows_mx[0], E5M2, True, False)
+
+        def table_second_half(c, acc):
+            matmul(acc[:], xm_mx[1, c][0], xm_mx[1, c][1], E4M3, h_rows_mx[1], E5M2, False, True)
+
         def table_gradient(c, acc):
+            table_first_half(c, acc)
+            table_second_half(c, acc)
+            table_out(c, acc)
+
+        def table_out(c, acc):
             features = slice(c * P, (c + 1) * P)
-            for g in range(HALVES):
-                matmul(acc[:], xm_mx[g, c][0], xm_mx[g, c][1], E4M3, h_rows_mx[g], E5M2, g == 0, g == HALVES - 1)
-            tag = f"dense{c}"
+            tag = "w_grouped" if c == 1 else f"dense{c}"
             dense = keep.tile([P, N], F32, name=f"dense{c}", tag=tag, align_bytes=64)
             nc.scalar.copy(
                 out=dense[:].rearrange("d (b q m) -> d b q m", q=PACK, m=RUN),
@@ -287,19 +314,25 @@ def tile_attend_gnce_wx_ts_kb_kernel(tc, xT, wT, y, wt, ts, kb, xm, offs, out_0,
             nc.scalar.dma_start(out=out_1_hbm[g, u], in_=staged[:])
 
         table_gradient(0, banks[0])
-        turn_h(0, 0, banks[7])
+        h_pairs[1] = split_pairs("h_pairs1", h_rows[1], "w_grouped")
+        turn_w(0, banks[3])
+        turn_w(1, banks[4])
+        turn_h(0, 0, banks[5])
         turn_h(0, 1, banks[2])
-        w_slots_mx = mx_tiles("w_slots", tag="x1_codes")
         quantize(w_slots_mx, whole, w_slots[:], E4M3)
-        quantize(h_cols_mx[0], whole, h_cols0[:], E5M2)
-        prepare_xm(nc.scalar.copy, 1, 0)
-        prepare_xm(nc.scalar.copy, 1, 1)
-        turn_h(1, 0, banks[5])
+        quantize_h_cols(0, whole)
+        prepare_xm(1, 0, "xm10_grouped", nc.vector.tensor_copy)
+        table_first_half(1, banks[1])
+        table_second_half(1, banks[1])
+        prepare_xm(1, 1, "xm01_codes")
+        turn_h(1, 0, banks[6])
+        quantize_h_cols(1, column_halves[0])
         row_gradient(0, 0, banks[3:5])
-        table_gradient(1, banks[1])
-        row_gradient(0, 1, [banks[7], banks[2]])
-        turn_h(1, 1, banks[6])
-        table_gradient(2, banks[0])
+        table_out(1, banks[1])
+        row_gradient(0, 1, [banks[5], banks[2]])
+        turn_h(1, 1, banks[0])
+        quantize_h_cols(1, column_halves[1])
+        table_gradient(2, banks[7])
         row_gradient(1, 0, banks[3:5])
-        table_gradient(3, banks[1])
-        row_gradient(1, 1, [banks[7], banks[2]])
+        table_gradient(3, banks[6])
+        row_gradient(1, 1, [banks[5], banks[2]])

@@ -9,7 +9,6 @@ FLOPS = 3 * 2 * R * D * N
 F32 = mybir.dt.float32
 BF16 = mybir.dt.bfloat16
 U32 = mybir.dt.uint32
-I32 = mybir.dt.int32
 U16 = mybir.dt.uint16
 U8 = mybir.dt.uint8
 E4M3 = mybir.dt.float8_e4m3fn_x4
@@ -19,35 +18,37 @@ ALU = mybir.AluOpType
 
 P = 128
 PACK = 4
+RUN = 8
 K_PASS = P * PACK
+SIDE = K_PASS // 2
 HALVES = R // K_PASS
-BLOCKS = N // P
+PANELS = D // P
 LIST_ROWS = 16
 SCORE_BANK = 0
 TURN_BANK = 4
 WINDOWS = 3
-RUN = 8
+RING = 3
+ALIGN = 64
 
 
 def tile_attend_gnce_wx_ts_kb_kernel(tc, xT, wT, y, wt, ts, kb, xm, offs, out_0, out_1):
     nc = tc.nc
     with ExitStack() as ctx:
         keep = ctx.enter_context(tc.tile_pool(name="keep", bufs=1))
-        ring = ctx.enter_context(tc.tile_pool(name="ring", bufs=3))
+        ring = ctx.enter_context(tc.tile_pool(name="ring", bufs=RING))
         psum = ctx.enter_context(tc.psum_pool(name="psum", bufs=1))
 
         banks = [psum.tile([P, K_PASS], F32, name=f"bank{b}") for b in range(8)]
         whole = slice(0, K_PASS)
-        HALF = K_PASS // 2
-        column_halves = [slice(0, HALF), slice(HALF, K_PASS)]
+        sides = [slice(0, SIDE), slice(SIDE, K_PASS)]
 
-        def mx_tiles(name, tag=None):
-            codes = keep.tile([P, K_PASS], U32, name=name + "_codes", tag=tag or name + "_codes", align_bytes=64)
-            scales = keep.tile([P, K_PASS], U8, name=name + "_scales", align_bytes=64)
+        def mx_tiles(name, columns=K_PASS):
+            codes = keep.tile([P, columns], U32, name=name + "_codes", tag=name + "_codes", align_bytes=ALIGN)
+            scales = keep.tile([P, columns], U8, name=name + "_scales", align_bytes=ALIGN)
             return codes, scales
 
-        def grouped_tile(name, columns=K_PASS):
-            return keep.tile([P, columns, PACK], BF16, name=name, tag=name, align_bytes=64)
+        def grouped_tile(name, columns=K_PASS, tag=None):
+            return keep.tile([P, columns, PACK], BF16, name=name, tag=tag or name, align_bytes=ALIGN)
 
         def flat(grouped):
             return grouped.rearrange("p c j -> p (c j)")
@@ -82,61 +83,65 @@ def tile_attend_gnce_wx_ts_kb_kernel(tc, xT, wT, y, wt, ts, kb, xm, offs, out_0,
         wt_rows = keep.tile([P, HALVES, PACK], F32, name="wt_rows")
         nc.scalar.dma_start(out=wt_rows[:], in_=wt[0].rearrange("(g p j) o -> p g (j o)", g=HALVES, j=PACK))
 
-        x0_raw = [keep.tile([P, PACK, HALF], F32, name=f"x0_raw{a}")[:] for a in range(2)]
+        x0_raw = [keep.tile([P, PACK, SIDE], F32, name=f"x0_raw{a}") for a in range(2)]
         x1_raw = keep.tile([P, PACK, K_PASS], F32, name="x1_raw")
         y_raw = [keep.tile([P, PACK, N], F32, name=f"y_raw{g}") for g in range(HALVES)]
-        xm_raw = [[keep.tile([P, PACK, HALF], F32, name=f"xm_raw{a}{g}") for g in range(HALVES)] for a in range(2)]
+        xm_raw = [[keep.tile([P, PACK, SIDE], F32, name=f"xm_raw{a}{g}") for g in range(HALVES)] for a in range(2)]
         w_table = [keep.tile([P, T], F32, name=f"w_table{j}", tag=f"w_table{j}") for j in range(PACK)]
         x_hbm = xT[0].rearrange("(p j) (g r) -> g p j r", j=PACK, g=HALVES)
         y_hbm = y[0].rearrange("(g p j) i -> g p j i", j=PACK, g=HALVES)
         xm_hbm = xm[0].rearrange("(g p j) d -> g p j d", j=PACK, g=HALVES)
         w_hbm = wT.rearrange("(p j) t -> j p t", j=PACK)
-        loads = [(w_table[j][:], w_hbm[j]) for j in range(PACK)]
-        loads.insert(1, (ts_table[0:1, :], ts[0:1, :]))
-        loads.insert(3, (kb_table[0:1, :], kb[0:1, :]))
-        loads.extend((x0_raw[a], x_hbm[0][:, :, column_halves[a]]) for a in range(2))
+        loads = [
+            (w_table[0][:], w_hbm[0]),
+            (ts_table[0:1, :], ts[0:1, :]),
+            (w_table[1][:], w_hbm[1]),
+            (kb_table[0:1, :], kb[0:1, :]),
+            (w_table[2][:], w_hbm[2]),
+            (w_table[3][:], w_hbm[3]),
+        ]
+        loads.extend((x0_raw[a][:], x_hbm[0][:, :, sides[a]]) for a in range(2))
         loads.append((x1_raw[:], x_hbm[1]))
         loads.extend((y_raw[g][:], y_hbm[g]) for g in range(HALVES))
-        loads.extend((xm_raw[a][g][:], xm_hbm[g][:, :, column_halves[a]]) for a in range(2) for g in range(HALVES))
+        loads.extend((xm_raw[a][g][:], xm_hbm[g][:, :, sides[a]]) for a in range(2) for g in range(HALVES))
         for dest, source in loads:
             nc.sync.dma_start(out=dest, in_=source)
 
         ident = keep.tile([P, P], F32, name="ident")
         make_identity(nc, ident[:])
 
-
         windows = [keep.tile([P, T], F32, name=f"window{c}") for c in range(WINDOWS)]
         for window in windows:
             for first in range(0, T, K_PASS):
                 nc.gpsimd.memset(window[:, first : first + K_PASS], 0.0)
 
-        w_picked = keep.tile([P, PACK, N], F32, name="w_picked", tag="w_picked")
+        w_picked = keep.tile([P, PACK, N], F32, name="w_picked")
 
         per_slot = []
         for n, (name, table) in enumerate((("ts", ts_table), ("kb", kb_table))):
-            picked = keep.tile([P, N], F32, name=name + "_picked")
+            picked = keep.tile([P, N], F32, name=name + "_picked", tag=name + "_picked")
             nc.vector.tensor_copy(picked[:], table[:].indirect(offsets[:]))
-            dealt = keep.tile([P, N], F32, name=name + "_dealt")
+            dealt = keep.tile([P, N], F32, name=name + "_dealt", tag=name + "_dealt")
             nc.vector.tensor_copy(
                 out=dealt[:].rearrange("p (q b m) -> p b q m", q=PACK, m=RUN),
                 in_=picked[:].rearrange("p (b q m) -> p b q m", q=PACK, m=RUN),
             )
             turned = banks[TURN_BANK + n]
-            for t in range(BLOCKS):
-                nc.tensor.transpose(turned[:, t * P : (t + 1) * P], dealt[:, t * P : (t + 1) * P], ident[:])
-            column = keep.tile([P, BLOCKS], F32, name=name + "_slot")
+            for q in range(PACK):
+                nc.tensor.transpose(turned[:, q * P : (q + 1) * P], dealt[:, q * P : (q + 1) * P], ident[:])
+            column = keep.tile([P, PACK], F32, name=name + "_slot")
             nc.scalar.activation(out=column[:], in_=turned[:, 0:N:P], func=ACT.Copy)
             per_slot.append(column)
         ts_slot, kb_slot = per_slot
-        ts_free = banks[0]
-        for t in range(BLOCKS):
-            repeated = ts_slot[:, t : t + 1].to_broadcast([P, P])
-            nc.tensor.transpose(ts_free[:, t * P : (t + 1) * P], repeated, ident[:])
 
+        ts_free = banks[SCORE_BANK]
+        for q in range(PACK):
+            repeated = ts_slot[:, q : q + 1].to_broadcast([P, P])
+            nc.tensor.transpose(ts_free[:, q * P : (q + 1) * P], repeated, ident[:])
         factor = {}
 
         def make_factor(g, source, tag):
-            factor[g] = keep.tile([P, PACK, N], F32, name=f"factor{g}", tag=tag, align_bytes=64)
+            factor[g] = keep.tile([P, PACK, N], F32, name=f"factor{g}", tag=tag, align_bytes=ALIGN)
             for j in range(PACK):
                 nc.scalar.activation(out=factor[g][:, j, :], in_=source[:], func=ACT.Copy, scale=wt_rows[:, g, j : j + 1])
 
@@ -153,186 +158,185 @@ def tile_attend_gnce_wx_ts_kb_kernel(tc, xT, wT, y, wt, ts, kb, xm, offs, out_0,
                 out=w_grouped[:, q * P : (q + 1) * P, :].rearrange("p (b c i) j -> p b c j i", c=2, i=4),
                 in_=w_picked[:].rearrange("p j (b q c i) -> p q b c j i", q=PACK, c=2, i=4)[:, q],
             )
-        for slots in column_halves:
-            quantize(w_mx, slots, w_grouped[:, slots, :], E4M3)
+        for side in sides:
+            quantize(w_mx, side, w_grouped[:, side, :], E4M3)
 
         x_grouped = [grouped_tile(f"x_grouped{g}") for g in range(HALVES)]
         x_mx = [mx_tiles(f"x{g}") for g in range(HALVES)]
-        group(nc.scalar.copy, x_grouped[0][:, 0:HALF, :], x0_raw[0])
-        quantize(x_mx[0], column_halves[0], x_grouped[0][:, 0:HALF, :], E4M3)
-        group(nc.scalar.copy, x_grouped[0][:, HALF : HALF + P, :], x0_raw[1][:, :, 0:P])
-        group(nc.vector.tensor_copy, x_grouped[0][:, HALF + P :, :], x0_raw[1][:, :, P:])
-        quantize(x_mx[0], column_halves[1], x_grouped[0][:, HALF:, :], E4M3)
+        group(nc.scalar.copy, x_grouped[0][:, 0:SIDE, :], x0_raw[0][:])
+        quantize(x_mx[0], sides[0], x_grouped[0][:, 0:SIDE, :], E4M3)
+        group(nc.scalar.copy, x_grouped[0][:, SIDE : SIDE + P, :], x0_raw[1][:, :, 0:P])
+        group(nc.vector.tensor_copy, x_grouped[0][:, SIDE + P :, :], x0_raw[1][:, :, P:])
+        quantize(x_mx[0], sides[1], x_grouped[0][:, SIDE:, :], E4M3)
 
-        def split_pairs(name, grouped, tag):
-            pairs = keep.tile([P, 2, K_PASS], F32, name=name, tag=tag, align_bytes=64)
+        w_pairs = keep.tile([P, PACK, 2, P, 2], BF16, name="w_pairs", tag="x_grouped0", align_bytes=ALIGN)
+        for u in range(2):
             nc.vector.tensor_copy(
-                out=pairs[:].bitcast(I32).rearrange("p u (c i) -> p c u i", i=4),
-                in_=flat(grouped[:]).bitcast(I32).rearrange("p (c i u) -> p c u i", u=2, i=4),
+                out=w_pairs[:, :, u].rearrange("p j (b m) e -> p j b m e", m=RUN),
+                in_=w_picked[:].rearrange("p j (b u e m) -> p u j b m e", u=2, e=2, m=RUN)[:, u],
             )
-            return pairs
-
-        w_pairs = split_pairs("w_pairs", w_grouped, "x_grouped0")
         group(nc.vector.tensor_copy, x_grouped[1][:], x1_raw[:])
         quantize(x_mx[1], whole, x_grouped[1][:], E4M3)
-
-        def turn(blocks, dest, turned):
-            for q in range(PACK):
-                nc.tensor.transpose(turned[:, q * P : (q + 1) * P], blocks[q], ident[:])
-            nc.scalar.copy(
-                out=dest.rearrange("m (e p) q -> m e p q", e=2),
-                in_=turned[:].bitcast(BF16).rearrange("m (q p e) -> m e p q", q=PACK, e=2),
-            )
 
         w_slots = grouped_tile("w_slots")
         w_slots_mx = mx_tiles("w_slots")
 
-        def turn_w(u, turned):
-            turn([w_pairs[:, u, q * P : (q + 1) * P] for q in range(PACK)], w_slots[:, column_halves[u], :], turned)
+        def turn_w(a, turned):
+            pairs = w_pairs[:].rearrange("p j u m e -> p (j u) (m e)").bitcast(F32)
+            for place in range(PACK):
+                nc.tensor.transpose(turned[:, place * P : (place + 1) * P], pairs[:, PACK * a + place, :], ident[:])
+            nc.scalar.copy(
+                out=flat(w_slots[:, sides[a], :]).bitcast(F32).rearrange("m (j p u) -> m j p u", j=2, u=2),
+                in_=turned[:].rearrange("m (j u p) -> m j p u", j=2, u=2),
+            )
 
         h_rows = [grouped_tile(f"h_rows{g}") for g in range(HALVES)]
         h_rows_mx = [mx_tiles(f"h_rows{g}") for g in range(HALVES)]
-        h_cols = [grouped_tile(f"h_cols{g}") for g in range(HALVES)]
-        h_pairs = {}
-        h_cols_mx = [mx_tiles(f"h_cols{g}") for g in range(HALVES)]
+        h_slots_mx = [mx_tiles(f"h_slots{g}") for g in range(HALVES)]
         xm_mx = {}
-        units = [(g, t) for g in range(HALVES) for t in range(BLOCKS)]
+        h_pairs = {}
+        units = [(g, q) for g in range(HALVES) for q in range(PACK)]
         diffs = {}
 
         def score(n):
-            g, t = units[n]
-            scores = banks[SCORE_BANK + t]
-            matmul(scores[:], w_mx, slice(t * P, (t + 1) * P), E4M3, x_mx[g], E4M3, True, True)
+            g, q = units[n]
+            scores = banks[SCORE_BANK + q]
+            matmul(scores[:], w_mx, slice(q * P, (q + 1) * P), E4M3, x_mx[g], E4M3, True, True)
             prob = ring.tile([P, PACK, P], F32, name="prob")
             nc.scalar.activation(
                 out=prob[:],
                 in_=scores[:].rearrange("m (p j) -> m j p", j=PACK),
                 func=ACT.Sigmoid,
-                bias=kb_slot[:, t : t + 1],
-                scale=ts_slot[:, t : t + 1],
+                bias=kb_slot[:, q : q + 1],
+                scale=ts_slot[:, q : q + 1],
             )
-            turned = banks[TURN_BANK + t]
             for j in range(PACK):
-                nc.tensor.transpose(turned[:, j * P : (j + 1) * P], prob[:, j, :], ident[:])
+                nc.tensor.transpose(banks[TURN_BANK + q][:, j * P : (j + 1) * P], prob[:, j, :], ident[:])
 
         def difference(n):
-            g, t = units[n]
-            turned = banks[TURN_BANK + t]
+            g, q = units[n]
             diffs[n] = ring.tile([P, PACK, P], F32, name="diff")
             nc.vector.tensor_tensor(
                 out=diffs[n][:].rearrange("p j (b m) -> p j b m", m=RUN),
-                in0=turned[:].rearrange("p (j b m) -> p j b m", j=PACK, m=RUN),
-                in1=y_raw[g][:].rearrange("p j (b q m) -> p q j b m", q=PACK, m=RUN)[:, t],
+                in0=banks[TURN_BANK + q][:].rearrange("p (j b m) -> p j b m", j=PACK, m=RUN),
+                in1=y_raw[g][:].rearrange("p j (b q m) -> p q j b m", q=PACK, m=RUN)[:, q],
                 op=ALU.subtract,
             )
 
         def weigh(n):
-            g, t = units[n]
-            slots = slice(t * P, (t + 1) * P)
+            g, q = units[n]
+            cols = slice(q * P, (q + 1) * P)
             nc.vector.tensor_tensor(
-                out=h_rows[g][:, slots, :].rearrange("p (c i) j -> p c j i", i=2),
+                out=h_rows[g][:, cols, :].rearrange("p (c i) j -> p c j i", i=2),
                 in0=diffs[n][:].rearrange("p j (c i) -> p c j i", i=2),
-                in1=factor[g][:, :, slots].rearrange("p j (c i) -> p c j i", i=2),
+                in1=factor[g][:, :, cols].rearrange("p j (c i) -> p c j i", i=2),
                 op=ALU.mult,
             )
 
-        def turn_h(g, u, turned):
-            if g in h_pairs:
-                blocks = [h_pairs[g][:, u, q * P : (q + 1) * P] for q in range(PACK)]
-            else:
-                pairs = flat(h_rows[g][:]).bitcast(F32)
-                blocks = [pairs[:, 2 * q * P + u : 2 * (q + 1) * P : 2] for q in range(PACK)]
-            turn(blocks, h_cols[g][:, column_halves[u], :], turned)
+        def turn_h(g, u, turned, tag):
+            pairs = flat(h_rows[g][:]).bitcast(F32)
+            for q in range(PACK):
+                nc.tensor.transpose(turned[:, q * P : (q + 1) * P], pairs[:, 2 * q * P + u : 2 * (q + 1) * P : 2], ident[:])
+            h_pairs[g, u] = keep.tile([P, P, PACK], F32, name=f"h_pairs{g}{u}", tag=tag)
+            nc.scalar.copy(out=h_pairs[g, u][:], in_=turned[:].rearrange("m (q p) -> m p q", q=PACK))
 
-        def quantize_h_cols(g, cols):
-            quantize(h_cols_mx[g], cols, h_cols[g][:, cols, :], E5M2)
+        def split_h(g, u, grouped):
+            nc.scalar.copy(
+                out=grouped.rearrange("m (e p) q -> m e (p q)", e=2),
+                in_=h_pairs[g, u][:].rearrange("m p q -> m (p q)").bitcast(BF16).rearrange("m (c e) -> m e c", e=2),
+            )
 
-        def prepare_xm(a, g, tag, copy=nc.scalar.copy):
-            name = f"xm{a}{g}"
-            grouped = keep.tile([P, HALF, PACK], BF16, name=name + "_grouped", tag=tag, align_bytes=64)
+        def prepare_xm(a, g, copy, panels_a_tile, tag=None):
+            grouped = grouped_tile(f"xm{a}{g}_grouped", SIDE, tag)
             group(copy, grouped[:], xm_raw[a][g][:])
-            codes = keep.tile([P, HALF], U32, name=name + "_codes", tag=name + "_codes", align_bytes=64)
-            scales = keep.tile([P, HALF], U8, name=name + "_scales", align_bytes=64)
-            quantize((codes, scales), slice(0, HALF), grouped[:], E4M3)
-            for c in range(2):
-                xm_mx[g, 2 * a + c] = ((codes, scales), slice(c * P, (c + 1) * P))
+            width = panels_a_tile * P
+            for first in range(0, SIDE, width):
+                mx = mx_tiles(f"xm_half{g}_panel{2 * a + first // P}", width)
+                quantize(mx, slice(0, width), grouped[:, first : first + width, :], E4M3)
+                for c in range(panels_a_tile):
+                    xm_mx[g, 2 * a + first // P + c] = (mx, slice(c * P, (c + 1) * P))
 
+        last_of_first_half = PACK - 1
         score(0)
         difference(0)
         for n in range(len(units)):
             if n + 1 < len(units):
                 score(n + 1)
-            if n + 1 < len(units) and n + 1 != BLOCKS:
-                difference(n + 1)
-            if n == BLOCKS - 1:
+            if n == last_of_first_half:
                 make_factor(1, ts_kept, "x0_codes")
+                weigh(n)
+                for side in sides:
+                    quantize(h_rows_mx[0], side, h_rows[0][:, side, :], E5M2)
+                difference(n + 1)
+                continue
+            if n + 1 < len(units):
+                difference(n + 1)
             weigh(n)
-            if n == BLOCKS - 1:
-                for cols in column_halves:
-                    quantize(h_rows_mx[0], cols, h_rows[0][:, cols, :], E5M2)
-                h_pairs[0] = split_pairs("h_pairs0", h_rows[0], "x_grouped1")
-                difference(BLOCKS)
-            if n > BLOCKS and n - BLOCKS - 1 < HALVES:
-                prepare_xm(0, n - BLOCKS - 1, f"xm0{n - BLOCKS - 1}_grouped")
-        for cols in column_halves:
-            quantize(h_rows_mx[1], cols, h_rows[1][:, cols, :], E5M2)
+            if n == len(units) - 3:
+                prepare_xm(0, 0, nc.scalar.copy, 2)
+            if n == len(units) - 2:
+                prepare_xm(0, 1, nc.scalar.copy, 1)
+        for side in sides:
+            quantize(h_rows_mx[1], side, h_rows[1][:, side, :], E5M2)
 
         out_1_hbm = out_1[0].rearrange("(g p u e) d -> g u p e d", g=HALVES, u=2, e=2)
 
-        def table_first_half(c, acc):
-            matmul(acc[:], xm_mx[0, c][0], xm_mx[0, c][1], E4M3, h_rows_mx[0], E5M2, True, False)
+        def multiply_panel(c, acc):
+            for g in range(HALVES):
+                mx, cols = xm_mx[g, c]
+                matmul(acc[:], mx, cols, E4M3, h_rows_mx[g], E5M2, g == 0, g == HALVES - 1)
 
-        def table_second_half(c, acc):
-            matmul(acc[:], xm_mx[1, c][0], xm_mx[1, c][1], E4M3, h_rows_mx[1], E5M2, False, True)
-
-        def table_gradient(c, acc):
-            table_first_half(c, acc)
-            table_second_half(c, acc)
-            table_out(c, acc)
-
-        def table_out(c, acc):
-            features = slice(c * P, (c + 1) * P)
-            tag = "w_grouped" if c == 1 else f"dense{c}"
-            dense = keep.tile([P, N], F32, name=f"dense{c}", tag=tag, align_bytes=64)
+        def store_panel(c, acc):
+            dense = keep.tile([P, N], F32, name=f"dense{c}")
             nc.scalar.copy(
                 out=dense[:].rearrange("d (b q m) -> d b q m", q=PACK, m=RUN),
                 in_=acc[:].rearrange("d (q b m) -> d b q m", q=PACK, m=RUN),
             )
             window = windows[c % WINDOWS]
             nc.vector.tensor_copy(window[:].indirect(offsets[:]), dense[:])
-            nc.sync.dma_start(out=out_0[features, :], in_=window[:])
+            nc.sync.dma_start(out=out_0[c * P : (c + 1) * P, :], in_=window[:])
 
         def row_gradient(g, u, accs):
             staged = keep.tile([P, 2, D], F32, name=f"staged{g}{u}", tag=f"w_table{2 * g + u}")
             for e in range(2):
                 first = (2 * u + e) * P
-                matmul(accs[e][:], h_cols_mx[g], slice(first, first + P), E5M2, w_slots_mx, E4M3, True, True)
+                matmul(accs[e][:], h_slots_mx[g], slice(first, first + P), E5M2, w_slots_mx, E4M3, True, True)
                 nc.scalar.copy(
                     out=staged[:, e, :].rearrange("r (p j) -> r p j", j=PACK),
                     in_=accs[e][:].rearrange("r (j p) -> r p j", j=PACK),
                 )
             nc.scalar.dma_start(out=out_1_hbm[g, u], in_=staged[:])
 
-        table_gradient(0, banks[0])
-        h_pairs[1] = split_pairs("h_pairs1", h_rows[1], "w_grouped")
+        multiply_panel(0, banks[0])
+        store_panel(0, banks[0])
         turn_w(0, banks[3])
         turn_w(1, banks[4])
-        turn_h(0, 0, banks[5])
-        turn_h(0, 1, banks[2])
+        turn_h(0, 0, banks[5], "ts_picked")
+        turn_h(0, 1, banks[2], "kb_picked")
+        h_slots = grouped_tile("h_slots0")
+        for u in range(2):
+            split_h(0, u, h_slots[:, sides[u], :])
         quantize(w_slots_mx, whole, w_slots[:], E4M3)
-        quantize_h_cols(0, whole)
-        prepare_xm(1, 0, "xm10_grouped", nc.vector.tensor_copy)
-        table_first_half(1, banks[1])
-        table_second_half(1, banks[1])
-        prepare_xm(1, 1, "xm01_codes")
-        turn_h(1, 0, banks[6])
-        quantize_h_cols(1, column_halves[0])
+        quantize(h_slots_mx[0], whole, h_slots[:], E5M2)
+        prepare_xm(1, 0, nc.vector.tensor_copy, 2)
+
+        multiply_panel(1, banks[1])
+        turn_h(1, 0, banks[6], "ts_dealt")
         row_gradient(0, 0, banks[3:5])
-        table_out(1, banks[1])
+        h_slots_left = grouped_tile("h_slots1_left", SIDE, "xm_half1_panel0_codes")
+        split_h(1, 0, h_slots_left[:])
+        quantize(h_slots_mx[1], sides[0], h_slots_left[:], E5M2)
+        prepare_xm(1, 1, nc.scalar.copy, 2, "xm_half1_panel1_codes")
+        store_panel(1, banks[1])
+
+        turn_h(1, 1, banks[0], "kb_dealt")
         row_gradient(0, 1, [banks[5], banks[2]])
-        turn_h(1, 1, banks[0])
-        quantize_h_cols(1, column_halves[1])
-        table_gradient(2, banks[7])
+        h_slots_right = grouped_tile("h_slots1_right", SIDE)
+        split_h(1, 1, h_slots_right[:])
+        quantize(h_slots_mx[1], sides[1], h_slots_right[:], E5M2)
+        multiply_panel(2, banks[7])
+        store_panel(2, banks[7])
         row_gradient(1, 0, banks[3:5])
-        table_gradient(3, banks[6])
+        multiply_panel(PANELS - 1, banks[6])
+        store_panel(PANELS - 1, banks[6])
         row_gradient(1, 1, [banks[5], banks[2]])

@@ -75,16 +75,14 @@ def tile_attend_gnce_wx_ts_kb_kernel(tc, xT, wT, y, wt, ts, kb, xm, offs, out_0,
             )
 
         offsets = keep.tile([P, N // LIST_ROWS], U16, name="offsets")
-        nc.sync.dma_start(offsets[:], offs)
-        ts_table = keep.tile([P, T], F32, name="ts_table")
-        kb_table = keep.tile([P, T], F32, name="kb_table")
+        ts_table = keep.tile([P, T], F32, name="ts_table", tag="ts_table", align_bytes=ALIGN)
+        kb_table = keep.tile([P, T], F32, name="kb_table", tag="kb_table", align_bytes=ALIGN)
         for table in (ts_table, kb_table):
             nc.vector.memset(table[:], 0.0)
         wt_rows = keep.tile([P, HALVES, PACK], F32, name="wt_rows")
         nc.scalar.dma_start(out=wt_rows[:], in_=wt[0].rearrange("(g p j) o -> p g (j o)", g=HALVES, j=PACK))
 
-        x0_raw = [keep.tile([P, PACK, SIDE], F32, name=f"x0_raw{a}") for a in range(2)]
-        x1_raw = keep.tile([P, PACK, K_PASS], F32, name="x1_raw")
+        x_raw = [[keep.tile([P, PACK, SIDE], F32, name=f"x_raw{g}{a}", tag=f"x_raw{g}{a}", align_bytes=ALIGN) for a in range(2)] for g in range(HALVES)]
         y_raw = [keep.tile([P, PACK, N], F32, name=f"y_raw{g}") for g in range(HALVES)]
         xm_raw = [[keep.tile([P, PACK, SIDE], F32, name=f"xm_raw{a}{g}") for g in range(HALVES)] for a in range(2)]
         w_table = [keep.tile([P, T], F32, name=f"w_table{j}", tag=f"w_table{j}") for j in range(PACK)]
@@ -92,17 +90,21 @@ def tile_attend_gnce_wx_ts_kb_kernel(tc, xT, wT, y, wt, ts, kb, xm, offs, out_0,
         y_hbm = y[0].rearrange("(g p j) i -> g p j i", j=PACK, g=HALVES)
         xm_hbm = xm[0].rearrange("(g p j) d -> g p j d", j=PACK, g=HALVES)
         w_hbm = wT.rearrange("(p j) t -> j p t", j=PACK)
+        nc.sync.dma_start(out=w_table[0][:], in_=w_hbm[0])
+        nc.sync.dma_start(offsets[:], offs)
         loads = [
-            (w_table[0][:], w_hbm[0]),
             (ts_table[0:1, :], ts[0:1, :]),
             (w_table[1][:], w_hbm[1]),
             (kb_table[0:1, :], kb[0:1, :]),
             (w_table[2][:], w_hbm[2]),
             (w_table[3][:], w_hbm[3]),
+            (x_raw[0][0][:], x_hbm[0][:, :, sides[0]]),
+            (x_raw[0][1][:], x_hbm[0][:, :, sides[1]]),
+            (x_raw[1][0][:], x_hbm[1][:, :, sides[0]]),
+            (x_raw[1][1][:], x_hbm[1][:, :, sides[1]]),
+            (y_raw[0][:], y_hbm[0]),
+            (y_raw[1][:], y_hbm[1]),
         ]
-        loads.extend((x0_raw[a][:], x_hbm[0][:, :, sides[a]]) for a in range(2))
-        loads.append((x1_raw[:], x_hbm[1]))
-        loads.extend((y_raw[g][:], y_hbm[g]) for g in range(HALVES))
         loads.extend((xm_raw[a][g][:], xm_hbm[g][:, :, sides[a]]) for a in range(2) for g in range(HALVES))
         for dest, source in loads:
             nc.sync.dma_start(out=dest, in_=source)
@@ -110,21 +112,20 @@ def tile_attend_gnce_wx_ts_kb_kernel(tc, xT, wT, y, wt, ts, kb, xm, offs, out_0,
         ident = keep.tile([P, P], F32, name="ident")
         make_identity(nc, ident[:])
 
+        warm = keep.tile([P, 1], F32, name="warm")
+        nc.scalar.activation(out=warm[:], in_=ident[:, 0:1], func=ACT.Sigmoid)
+
         windows = [keep.tile([P, T], F32, name=f"window{c}") for c in range(WINDOWS)]
         for window in windows:
             for first in range(0, T, K_PASS):
                 nc.gpsimd.memset(window[:, first : first + K_PASS], 0.0)
 
-        w_picked = keep.tile([P, PACK, N], F32, name="w_picked")
-
         per_slot = []
         for n, (name, table) in enumerate((("ts", ts_table), ("kb", kb_table))):
-            picked = keep.tile([P, N], F32, name=name + "_picked", tag=name + "_picked")
-            nc.vector.tensor_copy(picked[:], table[:].indirect(offsets[:]))
             dealt = keep.tile([P, N], F32, name=name + "_dealt", tag=name + "_dealt")
             nc.vector.tensor_copy(
-                out=dealt[:].rearrange("p (q b m) -> p b q m", q=PACK, m=RUN),
-                in_=picked[:].rearrange("p (b q m) -> p b q m", q=PACK, m=RUN),
+                dealt[:].bitcast(U32).rearrange("p (q b m) -> p b q m", q=PACK, m=RUN),
+                table[:].bitcast(U32).indirect(offsets[:]),
             )
             turned = banks[TURN_BANK + n]
             for q in range(PACK):
@@ -132,51 +133,67 @@ def tile_attend_gnce_wx_ts_kb_kernel(tc, xT, wT, y, wt, ts, kb, xm, offs, out_0,
             column = keep.tile([P, PACK], F32, name=name + "_slot")
             nc.scalar.activation(out=column[:], in_=turned[:, 0:N:P], func=ACT.Copy)
             per_slot.append(column)
+            if n == 0:
+                ts_free = banks[TURN_BANK + 3]
+                for q in range(PACK):
+                    repeated = column[:, q : q + 1].to_broadcast([P, P])
+                    nc.tensor.transpose(ts_free[:, q * P : (q + 1) * P], repeated, ident[:])
         ts_slot, kb_slot = per_slot
 
-        ts_free = banks[SCORE_BANK]
-        for q in range(PACK):
-            repeated = ts_slot[:, q : q + 1].to_broadcast([P, P])
-            nc.tensor.transpose(ts_free[:, q * P : (q + 1) * P], repeated, ident[:])
         factor = {}
 
-        def make_factor(g, source, tag):
-            factor[g] = keep.tile([P, PACK, N], F32, name=f"factor{g}", tag=tag, align_bytes=ALIGN)
+        def make_factor(g, first, width, tag):
+            tile = keep.tile([P, PACK, width], F32, name=f"factor{g}_{first}", tag=tag, align_bytes=ALIGN)
             for j in range(PACK):
-                nc.scalar.activation(out=factor[g][:, j, :], in_=source[:], func=ACT.Copy, scale=wt_rows[:, g, j : j + 1])
+                nc.scalar.activation(out=tile[:, j, :], in_=ts_free[:, first : first + width], func=ACT.Copy, scale=wt_rows[:, g, j : j + 1])
+            for q in range(first // P, (first + width) // P):
+                factor[g, q] = tile[:, :, q * P - first : (q + 1) * P - first]
 
-        make_factor(0, ts_free, "factor0")
-        ts_kept = keep.tile([P, N], F32, name="ts_kept")
-        nc.scalar.copy(out=ts_kept[:], in_=ts_free[:])
+        make_factor(0, 0, K_PASS, "factor0")
+        make_factor(1, 0, SIDE, "factor1")
 
+        w_picked = keep.tile([P, PACK, N], F32, name="w_picked", tag="ts_table", align_bytes=ALIGN)
         w_mx = mx_tiles("w")
         for j in range(PACK):
             nc.vector.tensor_copy(w_picked[:, j, :], w_table[j][:].indirect(offsets[:]))
-        w_grouped = grouped_tile("w_grouped")
-        for q in range(PACK):
+        w_grouped = {}
+
+        def deal_w(q):
             nc.vector.tensor_copy(
-                out=w_grouped[:, q * P : (q + 1) * P, :].rearrange("p (b c i) j -> p b c j i", c=2, i=4),
+                out=w_grouped[q // 2][:, q % 2 * P : (q % 2 + 1) * P, :].rearrange("p (b c i) j -> p b c j i", c=2, i=4),
                 in_=w_picked[:].rearrange("p j (b q c i) -> p q b c j i", q=PACK, c=2, i=4)[:, q],
             )
-        for side in sides:
-            quantize(w_mx, side, w_grouped[:, side, :], E4M3)
 
-        x_grouped = [grouped_tile(f"x_grouped{g}") for g in range(HALVES)]
+        x_grouped = [[grouped_tile(f"x_grouped{g}{a}", SIDE) for a in range(2)] for g in range(HALVES)]
         x_mx = [mx_tiles(f"x{g}") for g in range(HALVES)]
-        group(nc.scalar.copy, x_grouped[0][:, 0:SIDE, :], x0_raw[0][:])
-        quantize(x_mx[0], sides[0], x_grouped[0][:, 0:SIDE, :], E4M3)
-        group(nc.scalar.copy, x_grouped[0][:, SIDE : SIDE + P, :], x0_raw[1][:, :, 0:P])
-        group(nc.vector.tensor_copy, x_grouped[0][:, SIDE + P :, :], x0_raw[1][:, :, P:])
-        quantize(x_mx[0], sides[1], x_grouped[0][:, SIDE:, :], E4M3)
+        group(nc.scalar.copy, x_grouped[0][0][:], x_raw[0][0][:])
+        make_factor(1, SIDE, SIDE, "x_raw00")
+        w_grouped[0] = grouped_tile("w_grouped0", SIDE)
+        deal_w(0)
+        deal_w(1)
+        quantize(w_mx, sides[0], w_grouped[0][:], E4M3)
+        group(nc.vector.tensor_copy, x_grouped[0][1][:], x_raw[0][1][:])
+        quantize(x_mx[0], sides[0], x_grouped[0][0][:], E4M3)
+        quantize(x_mx[0], sides[1], x_grouped[0][1][:], E4M3)
+        w_grouped[1] = grouped_tile("w_grouped1", SIDE, "x_raw01")
+        deal_w(2)
+        deal_w(3)
+        group(nc.scalar.copy, x_grouped[1][0][:], x_raw[1][0][:])
 
-        w_pairs = keep.tile([P, PACK, 2, P, 2], BF16, name="w_pairs", tag="x_grouped0", align_bytes=ALIGN)
-        for u in range(2):
+        w_pairs = keep.tile([P, PACK, 2, P, 2], BF16, name="w_pairs", tag="x_grouped01", align_bytes=ALIGN)
+
+        def pair_w(u):
             nc.vector.tensor_copy(
                 out=w_pairs[:, :, u].rearrange("p j (b m) e -> p j b m e", m=RUN),
                 in_=w_picked[:].rearrange("p j (b u e m) -> p u j b m e", u=2, e=2, m=RUN)[:, u],
             )
-        group(nc.vector.tensor_copy, x_grouped[1][:], x1_raw[:])
-        quantize(x_mx[1], whole, x_grouped[1][:], E4M3)
+
+        pair_w(0)
+        quantize(w_mx, sides[1], w_grouped[1][:], E4M3)
+        group(nc.vector.tensor_copy, x_grouped[1][1][:], x_raw[1][1][:])
+        quantize(x_mx[1], sides[0], x_grouped[1][0][:], E4M3)
+        quantize(x_mx[1], sides[1], x_grouped[1][1][:], E4M3)
+        pair_w(1)
 
         w_slots = grouped_tile("w_slots")
         w_slots_mx = mx_tiles("w_slots")
@@ -193,16 +210,17 @@ def tile_attend_gnce_wx_ts_kb_kernel(tc, xT, wT, y, wt, ts, kb, xm, offs, out_0,
         h_rows = [grouped_tile(f"h_rows{g}") for g in range(HALVES)]
         h_rows_mx = [mx_tiles(f"h_rows{g}") for g in range(HALVES)]
         h_slots_mx = [mx_tiles(f"h_slots{g}") for g in range(HALVES)]
+        h_slots = {}
         xm_mx = {}
-        h_pairs = {}
         units = [(g, q) for g in range(HALVES) for q in range(PACK)]
         diffs = {}
+        probs = {}
 
         def score(n):
             g, q = units[n]
-            scores = banks[SCORE_BANK + q]
+            scores = banks[q]
             matmul(scores[:], w_mx, slice(q * P, (q + 1) * P), E4M3, x_mx[g], E4M3, True, True)
-            prob = ring.tile([P, PACK, P], F32, name="prob")
+            prob = ring.tile([P, PACK, P], F32, name="prob", bufs=6)
             nc.scalar.activation(
                 out=prob[:],
                 in_=scores[:].rearrange("m (p j) -> m j p", j=PACK),
@@ -210,8 +228,11 @@ def tile_attend_gnce_wx_ts_kb_kernel(tc, xT, wT, y, wt, ts, kb, xm, offs, out_0,
                 bias=kb_slot[:, q : q + 1],
                 scale=ts_slot[:, q : q + 1],
             )
+            probs[n] = prob
+
+        def turn(n):
             for j in range(PACK):
-                nc.tensor.transpose(banks[TURN_BANK + q][:, j * P : (j + 1) * P], prob[:, j, :], ident[:])
+                nc.tensor.transpose(banks[TURN_BANK + n % PACK][:, j * P : (j + 1) * P], probs[n][:, j, :], ident[:])
 
         def difference(n):
             g, q = units[n]
@@ -229,53 +250,66 @@ def tile_attend_gnce_wx_ts_kb_kernel(tc, xT, wT, y, wt, ts, kb, xm, offs, out_0,
             nc.vector.tensor_tensor(
                 out=h_rows[g][:, cols, :].rearrange("p (c i) j -> p c j i", i=2),
                 in0=diffs[n][:].rearrange("p j (c i) -> p c j i", i=2),
-                in1=factor[g][:, :, cols].rearrange("p j (c i) -> p c j i", i=2),
+                in1=factor[g, q].rearrange("p j (c i) -> p c j i", i=2),
                 op=ALU.mult,
             )
 
-        def turn_h(g, u, turned, tag):
+        def turn_h(g, u, turned):
+            turn_pairs(g, u, turned)
+            part_pairs(g, u, turned)
+
+        def turn_pairs(g, u, turned):
             pairs = flat(h_rows[g][:]).bitcast(F32)
             for q in range(PACK):
                 nc.tensor.transpose(turned[:, q * P : (q + 1) * P], pairs[:, 2 * q * P + u : 2 * (q + 1) * P : 2], ident[:])
-            h_pairs[g, u] = keep.tile([P, P, PACK], F32, name=f"h_pairs{g}{u}", tag=tag)
-            nc.scalar.copy(out=h_pairs[g, u][:], in_=turned[:].rearrange("m (q p) -> m p q", q=PACK))
 
-        def split_h(g, u, grouped):
+        def part_pairs(g, u, turned):
+            h_slots[g, u] = grouped_tile(f"h_slots{g}{u}", SIDE)
             nc.scalar.copy(
-                out=grouped.rearrange("m (e p) q -> m e (p q)", e=2),
-                in_=h_pairs[g, u][:].rearrange("m p q -> m (p q)").bitcast(BF16).rearrange("m (c e) -> m e c", e=2),
+                out=h_slots[g, u][:].rearrange("m (e p) q -> m e p q", e=2),
+                in_=turned[:].bitcast(BF16).rearrange("m (q p e) -> m e p q", q=PACK, e=2),
             )
 
-        def prepare_xm(a, g, copy, panels_a_tile, tag=None):
-            grouped = grouped_tile(f"xm{a}{g}_grouped", SIDE, tag)
-            group(copy, grouped[:], xm_raw[a][g][:])
-            width = panels_a_tile * P
-            for first in range(0, SIDE, width):
-                mx = mx_tiles(f"xm_half{g}_panel{2 * a + first // P}", width)
-                quantize(mx, slice(0, width), grouped[:, first : first + width, :], E4M3)
-                for c in range(panels_a_tile):
-                    xm_mx[g, 2 * a + first // P + c] = (mx, slice(c * P, (c + 1) * P))
+        def group_xm(a, g, copy, first, width, tag=None):
+            grouped = grouped_tile(f"xm{a}{g}_{first}_grouped", width, tag)
+            group(copy, grouped[:], xm_raw[a][g][:, :, first : first + width])
+            return grouped
 
-        last_of_first_half = PACK - 1
-        score(0)
+        def quantize_xm(a, g, grouped, first, width):
+            mx = mx_tiles(f"xm_half{g}_panel{2 * a + first // P}", width)
+            quantize(mx, slice(0, width), grouped[:], E4M3)
+            for c in range(width // P):
+                xm_mx[g, 2 * a + first // P + c] = (mx, slice(c * P, (c + 1) * P))
+
+        for n in range(PACK):
+            score(n)
+        for n in range(PACK):
+            turn(n)
+            score(n + PACK)
+        turn_w(0, banks[0])
+        turn_w(1, banks[1])
+        xm_left = [group_xm(0, g, nc.scalar.copy, 0, SIDE) for g in range(HALVES)]
         difference(0)
-        for n in range(len(units)):
-            if n + 1 < len(units):
-                score(n + 1)
-            if n == last_of_first_half:
-                make_factor(1, ts_kept, "x0_codes")
-                weigh(n)
-                for side in sides:
-                    quantize(h_rows_mx[0], side, h_rows[0][:, side, :], E5M2)
-                difference(n + 1)
-                continue
-            if n + 1 < len(units):
+        for n in range(PACK):
+            turn(n + PACK)
+            if n + 1 < PACK:
                 difference(n + 1)
             weigh(n)
-            if n == len(units) - 3:
-                prepare_xm(0, 0, nc.scalar.copy, 2)
-            if n == len(units) - 2:
-                prepare_xm(0, 1, nc.scalar.copy, 1)
+        quantize(h_rows_mx[0], sides[0], h_rows[0][:, sides[0], :], E5M2)
+        difference(4)
+        quantize(h_rows_mx[0], sides[1], h_rows[0][:, sides[1], :], E5M2)
+        turn_h(0, 0, banks[2])
+        turn_h(0, 1, banks[3])
+        xm_right = [group_xm(1, g, nc.scalar.copy, 0, SIDE) for g in range(HALVES)]
+        difference(5)
+        weigh(4)
+        difference(6)
+        weigh(5)
+        difference(7)
+        quantize_xm(0, 0, xm_left[0], 0, SIDE)
+        weigh(6)
+        weigh(7)
+        quantize_xm(0, 1, xm_left[1], 0, SIDE)
         for side in sides:
             quantize(h_rows_mx[1], side, h_rows[1][:, side, :], E5M2)
 
@@ -286,14 +320,18 @@ def tile_attend_gnce_wx_ts_kb_kernel(tc, xT, wT, y, wt, ts, kb, xm, offs, out_0,
                 mx, cols = xm_mx[g, c]
                 matmul(acc[:], mx, cols, E4M3, h_rows_mx[g], E5M2, g == 0, g == HALVES - 1)
 
-        def store_panel(c, acc):
-            dense = keep.tile([P, N], F32, name=f"dense{c}")
+        dense = {}
+
+        def empty_panel(c, acc, tag=None):
+            dense[c] = keep.tile([P, N], F32, name=f"dense{c}", tag=tag or f"dense{c}", align_bytes=ALIGN)
             nc.scalar.copy(
-                out=dense[:].rearrange("d (b q m) -> d b q m", q=PACK, m=RUN),
+                out=dense[c][:].rearrange("d (b q m) -> d b q m", q=PACK, m=RUN),
                 in_=acc[:].rearrange("d (q b m) -> d b q m", q=PACK, m=RUN),
             )
+
+        def store_panel(c):
             window = windows[c % WINDOWS]
-            nc.vector.tensor_copy(window[:].indirect(offsets[:]), dense[:])
+            nc.vector.tensor_copy(window[:].indirect(offsets[:]), dense[c][:])
             nc.sync.dma_start(out=out_0[c * P : (c + 1) * P, :], in_=window[:])
 
         def row_gradient(g, u, accs):
@@ -308,35 +346,28 @@ def tile_attend_gnce_wx_ts_kb_kernel(tc, xT, wT, y, wt, ts, kb, xm, offs, out_0,
             nc.scalar.dma_start(out=out_1_hbm[g, u], in_=staged[:])
 
         multiply_panel(0, banks[0])
-        store_panel(0, banks[0])
-        turn_w(0, banks[3])
-        turn_w(1, banks[4])
-        turn_h(0, 0, banks[5], "ts_picked")
-        turn_h(0, 1, banks[2], "kb_picked")
-        h_slots = grouped_tile("h_slots0")
+        empty_panel(0, banks[0])
         for u in range(2):
-            split_h(0, u, h_slots[:, sides[u], :])
+            quantize(h_slots_mx[0], sides[u], h_slots[0, u][:], E5M2)
         quantize(w_slots_mx, whole, w_slots[:], E4M3)
-        quantize(h_slots_mx[0], whole, h_slots[:], E5M2)
-        prepare_xm(1, 0, nc.vector.tensor_copy, 2)
-
+        for g in range(HALVES):
+            quantize_xm(1, g, xm_right[g], 0, SIDE)
+        store_panel(0)
         multiply_panel(1, banks[1])
-        turn_h(1, 0, banks[6], "ts_dealt")
-        row_gradient(0, 0, banks[3:5])
-        h_slots_left = grouped_tile("h_slots1_left", SIDE, "xm_half1_panel0_codes")
-        split_h(1, 0, h_slots_left[:])
-        quantize(h_slots_mx[1], sides[0], h_slots_left[:], E5M2)
-        prepare_xm(1, 1, nc.scalar.copy, 2, "xm_half1_panel1_codes")
-        store_panel(1, banks[1])
-
-        turn_h(1, 1, banks[0], "kb_dealt")
-        row_gradient(0, 1, [banks[5], banks[2]])
-        h_slots_right = grouped_tile("h_slots1_right", SIDE)
-        split_h(1, 1, h_slots_right[:])
-        quantize(h_slots_mx[1], sides[1], h_slots_right[:], E5M2)
-        multiply_panel(2, banks[7])
-        store_panel(2, banks[7])
-        row_gradient(1, 0, banks[3:5])
-        multiply_panel(PANELS - 1, banks[6])
-        store_panel(PANELS - 1, banks[6])
-        row_gradient(1, 1, [banks[5], banks[2]])
+        row_gradient(0, 0, banks[4:6])
+        turn_h(1, 0, banks[0])
+        quantize(h_slots_mx[1], sides[0], h_slots[1, 0][:], E5M2)
+        turn_pairs(1, 1, banks[4])
+        empty_panel(1, banks[1], "h_rows1")
+        store_panel(1)
+        row_gradient(0, 1, banks[6:8])
+        part_pairs(1, 1, banks[4])
+        multiply_panel(2, banks[2])
+        row_gradient(1, 0, [banks[5], banks[0]])
+        empty_panel(2, banks[2])
+        quantize(h_slots_mx[1], sides[1], h_slots[1, 1][:], E5M2)
+        store_panel(2)
+        multiply_panel(3, banks[3])
+        empty_panel(3, banks[3])
+        row_gradient(1, 1, banks[6:8])
+        store_panel(3)

@@ -18,7 +18,8 @@ ALU = mybir.AluOpType
 
 P = 128
 PACK = 4
-RUN = 8
+HELPED = 3
+RUN = 4
 K_PASS = P * PACK
 SIDE = K_PASS // 2
 HALVES = R // K_PASS
@@ -42,8 +43,8 @@ def tile_attend_gnce_wx_ts_kb_kernel(tc, xT, wT, y, wt, ts, kb, xm, offs, out_0,
         whole = slice(0, K_PASS)
         sides = [slice(0, SIDE), slice(SIDE, K_PASS)]
 
-        def mx_tiles(name, columns=K_PASS):
-            codes = keep.tile([P, columns], U32, name=name + "_codes", tag=name + "_codes", align_bytes=ALIGN)
+        def mx_tiles(name, columns=K_PASS, tag=None):
+            codes = keep.tile([P, columns], U32, name=name + "_codes", tag=tag or name + "_codes", align_bytes=ALIGN)
             scales = keep.tile([P, columns], U8, name=name + "_scales", align_bytes=ALIGN)
             return codes, scales
 
@@ -83,7 +84,7 @@ def tile_attend_gnce_wx_ts_kb_kernel(tc, xT, wT, y, wt, ts, kb, xm, offs, out_0,
         nc.scalar.dma_start(out=wt_rows[:], in_=wt[0].rearrange("(g p j) o -> p g (j o)", g=HALVES, j=PACK))
 
         x_raw = [[keep.tile([P, PACK, SIDE], F32, name=f"x_raw{g}{a}", tag=f"x_raw{g}{a}", align_bytes=ALIGN) for a in range(2)] for g in range(HALVES)]
-        y_raw = [keep.tile([P, PACK, N], F32, name=f"y_raw{g}") for g in range(HALVES)]
+        y_raw = [keep.tile([P, PACK, N], F32, name=f"y_raw{g}", tag=f"y_raw{g}", align_bytes=ALIGN) for g in range(HALVES)]
         xm_raw = [[keep.tile([P, PACK, SIDE], F32, name=f"xm_raw{a}{g}") for g in range(HALVES)] for a in range(2)]
         w_table = [keep.tile([P, T], F32, name=f"w_table{j}", tag=f"w_table{j}") for j in range(PACK)]
         x_hbm = xT[0].rearrange("(p j) (g r) -> g p j r", j=PACK, g=HALVES)
@@ -115,16 +116,22 @@ def tile_attend_gnce_wx_ts_kb_kernel(tc, xT, wT, y, wt, ts, kb, xm, offs, out_0,
         warm = keep.tile([P, 1], F32, name="warm")
         nc.scalar.activation(out=warm[:], in_=ident[:, 0:1], func=ACT.Sigmoid)
 
-        windows = [keep.tile([P, T], F32, name=f"window{c}") for c in range(WINDOWS)]
-        for window in windows:
-            for first in range(0, T, K_PASS):
-                nc.gpsimd.memset(window[:, first : first + K_PASS], 0.0)
+        windows = []
+
+        def zeroed_window(piece, tag=None):
+            name = f"window{len(windows)}"
+            windows.append(keep.tile([P, T], F32, name=name, tag=tag or name, align_bytes=ALIGN))
+            for first in range(0, T, piece):
+                nc.gpsimd.memset(windows[-1][:, first : first + piece], 0.0)
+
+        for c in range(WINDOWS - 1):
+            zeroed_window(K_PASS)
 
         per_slot = []
         for n, (name, table) in enumerate((("ts", ts_table), ("kb", kb_table))):
             dealt = keep.tile([P, N], F32, name=name + "_dealt", tag=name + "_dealt")
             nc.vector.tensor_copy(
-                dealt[:].bitcast(U32).rearrange("p (q b m) -> p b q m", q=PACK, m=RUN),
+                dealt[:].bitcast(U32).rearrange("p (q c i) -> p c q i", q=PACK, i=RUN),
                 table[:].bitcast(U32).indirect(offsets[:]),
             )
             turned = banks[TURN_BANK + n]
@@ -149,7 +156,17 @@ def tile_attend_gnce_wx_ts_kb_kernel(tc, xT, wT, y, wt, ts, kb, xm, offs, out_0,
             for q in range(first // P, (first + width) // P):
                 factor[g, q] = tile[:, :, q * P - first : (q + 1) * P - first]
 
-        make_factor(0, 0, K_PASS, "factor0")
+        ts_kept = keep.tile([P, HELPED * P], F32, name="ts_kept")
+        nc.scalar.copy(out=ts_kept[:], in_=ts_free[:, 0 : HELPED * P])
+        for q in range(HELPED):
+            factor[0, q] = keep.tile([P, P, PACK], F32, name=f"woven_factor{q}", tag=f"woven_factor{q}", align_bytes=ALIGN)
+            nc.gpsimd.tensor_tensor(
+                out=factor[0, q][:],
+                in0=ts_kept[:, q * P : (q + 1) * P].unsqueeze(2).to_broadcast([P, P, PACK]),
+                in1=wt_rows[:, 0, :].unsqueeze(1).to_broadcast([P, P, PACK]),
+                op=ALU.mult,
+            )
+        make_factor(0, HELPED * P, K_PASS - HELPED * P, "factor0")
         make_factor(1, 0, SIDE, "factor1")
 
         w_picked = keep.tile([P, PACK, N], F32, name="w_picked", tag="ts_table", align_bytes=ALIGN)
@@ -160,8 +177,8 @@ def tile_attend_gnce_wx_ts_kb_kernel(tc, xT, wT, y, wt, ts, kb, xm, offs, out_0,
 
         def deal_w(q):
             nc.vector.tensor_copy(
-                out=w_grouped[q // 2][:, q % 2 * P : (q % 2 + 1) * P, :].rearrange("p (b c i) j -> p b c j i", c=2, i=4),
-                in_=w_picked[:].rearrange("p j (b q c i) -> p q b c j i", q=PACK, c=2, i=4)[:, q],
+                out=w_grouped[q // 2][:, q % 2 * P : (q % 2 + 1) * P, :].rearrange("p (c i) j -> p c j i", i=RUN),
+                in_=w_picked[:].rearrange("p j (c q i) -> p q c j i", q=PACK, i=RUN)[:, q],
             )
 
         x_grouped = [[grouped_tile(f"x_grouped{g}{a}", SIDE) for a in range(2)] for g in range(HALVES)]
@@ -184,8 +201,8 @@ def tile_attend_gnce_wx_ts_kb_kernel(tc, xT, wT, y, wt, ts, kb, xm, offs, out_0,
 
         def pair_w(u):
             nc.vector.tensor_copy(
-                out=w_pairs[:, :, u].rearrange("p j (b m) e -> p j b m e", m=RUN),
-                in_=w_picked[:].rearrange("p j (b u e m) -> p u j b m e", u=2, e=2, m=RUN)[:, u],
+                out=w_pairs[:, :, u].rearrange("p j (c i) e -> p j c i e", i=RUN),
+                in_=w_picked[:].rearrange("p j (c u e i) -> p u j c i e", u=2, e=2, i=RUN)[:, u],
             )
 
         pair_w(0)
@@ -207,8 +224,8 @@ def tile_attend_gnce_wx_ts_kb_kernel(tc, xT, wT, y, wt, ts, kb, xm, offs, out_0,
                 in_=turned[:].rearrange("m (j u p) -> m j p u", j=2, u=2),
             )
 
-        h_rows = [grouped_tile(f"h_rows{g}") for g in range(HALVES)]
-        h_rows_mx = [mx_tiles(f"h_rows{g}") for g in range(HALVES)]
+        h_rows = {}
+        h_rows_mx = {1: mx_tiles("h_rows1")}
         h_slots_mx = [mx_tiles(f"h_slots{g}") for g in range(HALVES)]
         h_slots = {}
         xm_mx = {}
@@ -236,19 +253,40 @@ def tile_attend_gnce_wx_ts_kb_kernel(tc, xT, wT, y, wt, ts, kb, xm, offs, out_0,
 
         def difference(n):
             g, q = units[n]
-            diffs[n] = ring.tile([P, PACK, P], F32, name="diff")
+            if n < HELPED:
+                diffs[n] = keep.tile([P, P, PACK], F32, name=f"diff{n}", tag=f"diff{n}", align_bytes=ALIGN)
+                nc.vector.tensor_tensor(
+                    out=diffs[n][:].rearrange("p (c i) j -> p c j i", i=RUN),
+                    in0=banks[TURN_BANK + q][:].rearrange("p (j c i) -> p c j i", j=PACK, i=RUN),
+                    in1=y_raw[g][:].rearrange("p j (c q i) -> p q c j i", q=PACK, i=RUN)[:, q],
+                    op=ALU.subtract,
+                )
+                return
+            diffs[n] = keep.tile([P, PACK, P], F32, name=f"diff{n}", tag=f"diff{n}", align_bytes=ALIGN)
             nc.vector.tensor_tensor(
-                out=diffs[n][:].rearrange("p j (b m) -> p j b m", m=RUN),
-                in0=banks[TURN_BANK + q][:].rearrange("p (j b m) -> p j b m", j=PACK, m=RUN),
-                in1=y_raw[g][:].rearrange("p j (b q m) -> p q j b m", q=PACK, m=RUN)[:, q],
+                out=diffs[n][:].rearrange("p j (c i) -> p j c i", i=RUN),
+                in0=banks[TURN_BANK + q][:].rearrange("p (j c i) -> p j c i", j=PACK, i=RUN),
+                in1=y_raw[g][:].rearrange("p j (c q i) -> p q j c i", q=PACK, i=RUN)[:, q],
                 op=ALU.subtract,
             )
 
         def weigh(n):
             g, q = units[n]
-            cols = slice(q * P, (q + 1) * P)
+            if n == 0:
+                h_rows["early"] = grouped_tile("h_early", HELPED * P)
+                for c in range(HELPED):
+                    h_rows[units[c]] = h_rows["early"][:, c * P : (c + 1) * P, :]
+            if n == HELPED:
+                h_rows[g, q] = grouped_tile("h_late", P, "y_raw1")[:]
+            if n == PACK:
+                h_rows[1] = grouped_tile("h_rows1", K_PASS, "factor0")
+                for c in range(PACK):
+                    h_rows[1, c] = h_rows[1][:, c * P : (c + 1) * P, :]
+            if n < HELPED:
+                nc.gpsimd.tensor_tensor(out=h_rows[g, q], in0=diffs[n][:], in1=factor[g, q][:], op=ALU.mult)
+                return
             nc.vector.tensor_tensor(
-                out=h_rows[g][:, cols, :].rearrange("p (c i) j -> p c j i", i=2),
+                out=h_rows[g, q].rearrange("p (c i) j -> p c j i", i=2),
                 in0=diffs[n][:].rearrange("p j (c i) -> p c j i", i=2),
                 in1=factor[g, q].rearrange("p j (c i) -> p c j i", i=2),
                 op=ALU.mult,
@@ -259,9 +297,9 @@ def tile_attend_gnce_wx_ts_kb_kernel(tc, xT, wT, y, wt, ts, kb, xm, offs, out_0,
             part_pairs(g, u, turned)
 
         def turn_pairs(g, u, turned):
-            pairs = flat(h_rows[g][:]).bitcast(F32)
             for q in range(PACK):
-                nc.tensor.transpose(turned[:, q * P : (q + 1) * P], pairs[:, 2 * q * P + u : 2 * (q + 1) * P : 2], ident[:])
+                pairs = flat(h_rows[g, q]).bitcast(F32)
+                nc.tensor.transpose(turned[:, q * P : (q + 1) * P], pairs[:, u : 2 * P : 2], ident[:])
 
         def part_pairs(g, u, turned):
             h_slots[g, u] = grouped_tile(f"h_slots{g}{u}", SIDE)
@@ -283,29 +321,31 @@ def tile_attend_gnce_wx_ts_kb_kernel(tc, xT, wT, y, wt, ts, kb, xm, offs, out_0,
 
         for n in range(PACK):
             score(n)
+        for a in range(2):
+            turn(2 * a)
+            turn(2 * a + 1)
+            score(PACK + 2 * a)
+            score(PACK + 2 * a + 1)
         for n in range(PACK):
-            turn(n)
-            score(n + PACK)
+            difference(n)
+            turn(n + PACK)
         turn_w(0, banks[0])
         turn_w(1, banks[1])
         xm_left = [group_xm(0, g, nc.scalar.copy, 0, SIDE) for g in range(HALVES)]
-        difference(0)
         for n in range(PACK):
-            turn(n + PACK)
-            if n + 1 < PACK:
-                difference(n + 1)
-            weigh(n)
-        quantize(h_rows_mx[0], sides[0], h_rows[0][:, sides[0], :], E5M2)
-        difference(4)
-        quantize(h_rows_mx[0], sides[1], h_rows[0][:, sides[1], :], E5M2)
+            if n < HELPED:
+                weigh(n)
+            difference(n + PACK)
+        weigh(3)
+        h_rows_mx[0] = mx_tiles("h_rows0", K_PASS, f"diff{HELPED}")
+        quantize(h_rows_mx[0], sides[0], h_rows["early"][:, sides[0], :], E5M2)
+        weigh(4)
+        for q in range(2, PACK):
+            quantize(h_rows_mx[0], slice(q * P, (q + 1) * P), h_rows[0, q], E5M2)
         turn_h(0, 0, banks[2])
         turn_h(0, 1, banks[3])
-        xm_right = [group_xm(1, g, nc.scalar.copy, 0, SIDE) for g in range(HALVES)]
-        difference(5)
-        weigh(4)
-        difference(6)
+        xm_right = [group_xm(1, 0, nc.scalar.copy, 0, SIDE, "xm_right")]
         weigh(5)
-        difference(7)
         quantize_xm(0, 0, xm_left[0], 0, SIDE)
         weigh(6)
         weigh(7)
@@ -325,8 +365,8 @@ def tile_attend_gnce_wx_ts_kb_kernel(tc, xT, wT, y, wt, ts, kb, xm, offs, out_0,
         def empty_panel(c, acc, tag=None):
             dense[c] = keep.tile([P, N], F32, name=f"dense{c}", tag=tag or f"dense{c}", align_bytes=ALIGN)
             nc.scalar.copy(
-                out=dense[c][:].rearrange("d (b q m) -> d b q m", q=PACK, m=RUN),
-                in_=acc[:].rearrange("d (q b m) -> d b q m", q=PACK, m=RUN),
+                out=dense[c][:].rearrange("d (c q i) -> d c q i", q=PACK, i=RUN),
+                in_=acc[:].rearrange("d (q c i) -> d c q i", q=PACK, i=RUN),
             )
 
         def store_panel(c):
@@ -350,21 +390,31 @@ def tile_attend_gnce_wx_ts_kb_kernel(tc, xT, wT, y, wt, ts, kb, xm, offs, out_0,
         for u in range(2):
             quantize(h_slots_mx[0], sides[u], h_slots[0, u][:], E5M2)
         quantize(w_slots_mx, whole, w_slots[:], E4M3)
-        for g in range(HALVES):
-            quantize_xm(1, g, xm_right[g], 0, SIDE)
+        quantize_xm(1, 0, xm_right[0], 0, SIDE)
+        xm_right.append(grouped_tile("xm11_grouped", SIDE, "xm_right"))
+        nc.gpsimd.tensor_scalar(
+            out=xm_right[1][:],
+            in0=xm_raw[1][1][:].rearrange("p j c -> p c j"),
+            scalar1=1.0,
+            scalar2=0.0,
+            op0=ALU.mult,
+            op1=ALU.add,
+        )
         store_panel(0)
         multiply_panel(1, banks[1])
         row_gradient(0, 0, banks[4:6])
         turn_h(1, 0, banks[0])
         quantize(h_slots_mx[1], sides[0], h_slots[1, 0][:], E5M2)
+        quantize_xm(1, 1, xm_right[1], 0, SIDE)
+        zeroed_window(2 * K_PASS, "xm_right")
         turn_pairs(1, 1, banks[4])
-        empty_panel(1, banks[1], "h_rows1")
+        empty_panel(1, banks[1], "factor0")
         store_panel(1)
         row_gradient(0, 1, banks[6:8])
         part_pairs(1, 1, banks[4])
         multiply_panel(2, banks[2])
-        row_gradient(1, 0, [banks[5], banks[0]])
         empty_panel(2, banks[2])
+        row_gradient(1, 0, [banks[5], banks[0]])
         quantize(h_slots_mx[1], sides[1], h_slots[1, 1][:], E5M2)
         store_panel(2)
         multiply_panel(3, banks[3])

@@ -80,8 +80,8 @@ def tile_attend_gnce_wx_ts_kb_kernel(tc, xT, wT, y, wt, ts, kb, xm, offs, out_0,
         kb_table = keep.tile([P, T], F32, name="kb_table", tag="kb_table", align_bytes=ALIGN)
         for table in (ts_table, kb_table):
             nc.vector.memset(table[:], 0.0)
-        wt_rows = keep.tile([P, HALVES, PACK], F32, name="wt_rows")
-        nc.scalar.dma_start(out=wt_rows[:], in_=wt[0].rearrange("(g p j) o -> p g (j o)", g=HALVES, j=PACK))
+        wt_rows = keep.tile([P, HALVES, 2 * PACK], F32, name="wt_rows")[:, :, 0:PACK]
+        nc.scalar.dma_start(out=wt_rows, in_=wt[0].rearrange("(g p j) o -> p g (j o)", g=HALVES, j=PACK))
 
         x_raw = [[keep.tile([P, PACK, SIDE], F32, name=f"x_raw{g}{a}", tag=f"x_raw{g}{a}", align_bytes=ALIGN) for a in range(2)] for g in range(HALVES)]
         y_raw = [keep.tile([P, PACK, N], F32, name=f"y_raw{g}", tag=f"y_raw{g}", align_bytes=ALIGN) for g in range(HALVES)]
@@ -129,7 +129,7 @@ def tile_attend_gnce_wx_ts_kb_kernel(tc, xT, wT, y, wt, ts, kb, xm, offs, out_0,
 
         per_slot = []
         for n, (name, table) in enumerate((("ts", ts_table), ("kb", kb_table))):
-            dealt = keep.tile([P, N], F32, name=name + "_dealt", tag=name + "_dealt")
+            dealt = keep.tile([P, N], F32, name=name + "_dealt", tag=name + "_dealt", align_bytes=ALIGN)
             nc.vector.tensor_copy(
                 dealt[:].bitcast(U32).rearrange("p (q c i) -> p c q i", q=PACK, i=RUN),
                 table[:].bitcast(U32).indirect(offsets[:]),
@@ -137,27 +137,27 @@ def tile_attend_gnce_wx_ts_kb_kernel(tc, xT, wT, y, wt, ts, kb, xm, offs, out_0,
             turned = banks[TURN_BANK + n]
             for q in range(PACK):
                 nc.tensor.transpose(turned[:, q * P : (q + 1) * P], dealt[:, q * P : (q + 1) * P], ident[:])
-            column = keep.tile([P, PACK], F32, name=name + "_slot")
-            nc.scalar.activation(out=column[:], in_=turned[:, 0:N:P], func=ACT.Copy)
-            per_slot.append(column)
             if n == 0:
+                ts_slot = keep.tile([P, PACK], F32, name="ts_slot")
+                nc.scalar.activation(out=ts_slot[:], in_=turned[:, 0:N:P], func=ACT.Copy)
+                spread = keep.tile([P, PACK], F32, name="ts_spread", tag="ts_spread", align_bytes=ALIGN)
+                nc.scalar.activation(out=spread[:], in_=turned[:, 0:N:P], func=ACT.Copy)
                 ts_free = banks[TURN_BANK + 3]
                 for q in range(PACK):
-                    repeated = column[:, q : q + 1].to_broadcast([P, P])
+                    repeated = spread[:, q : q + 1].to_broadcast([P, P])
                     nc.tensor.transpose(ts_free[:, q * P : (q + 1) * P], repeated, ident[:])
-        ts_slot, kb_slot = per_slot
 
         factor = {}
 
-        def make_factor(g, first, width, tag):
-            tile = keep.tile([P, PACK, width], F32, name=f"factor{g}_{first}", tag=tag, align_bytes=ALIGN)
+        def make_factor(g, first, width, tile):
             for j in range(PACK):
                 nc.scalar.activation(out=tile[:, j, :], in_=ts_free[:, first : first + width], func=ACT.Copy, scale=wt_rows[:, g, j : j + 1])
             for q in range(first // P, (first + width) // P):
                 factor[g, q] = tile[:, :, q * P - first : (q + 1) * P - first]
 
         ts_kept = keep.tile([P, HELPED * P], F32, name="ts_kept")
-        nc.scalar.copy(out=ts_kept[:], in_=ts_free[:, 0 : HELPED * P])
+        nc.scalar.copy(out=ts_kept[:, 0:P], in_=ts_free[:, 0:P])
+        nc.scalar.copy(out=ts_kept[:, P:], in_=ts_free[:, P : HELPED * P])
         for q in range(HELPED):
             factor[0, q] = keep.tile([P, P, PACK], F32, name=f"woven_factor{q}", tag=f"woven_factor{q}", align_bytes=ALIGN)
             nc.gpsimd.tensor_tensor(
@@ -166,13 +166,41 @@ def tile_attend_gnce_wx_ts_kb_kernel(tc, xT, wT, y, wt, ts, kb, xm, offs, out_0,
                 in1=wt_rows[:, 0, :].unsqueeze(1).to_broadcast([P, P, PACK]),
                 op=ALU.mult,
             )
-        make_factor(0, HELPED * P, K_PASS - HELPED * P, "factor0")
-        make_factor(1, 0, SIDE, "factor1")
 
         w_picked = keep.tile([P, PACK, N], F32, name="w_picked", tag="ts_table", align_bytes=ALIGN)
         w_mx = mx_tiles("w")
+        w_pairs = [keep.tile([P, 2, P, 2], BF16, name=f"w_pairs{j}", tag=tag, align_bytes=ALIGN) for j, tag in enumerate(("ts_dealt", "ts_spread", "w_pairs2", "w_pairs3"))]
+        w_slots = [grouped_tile("w_slots0", SIDE)]
+
+        def pair_w(j, copy):
+            copy(
+                out=w_pairs[j][:].rearrange("p u (c i) e -> p u c i e", i=RUN),
+                in_=w_picked[:, j, :].rearrange("p (c u e i) -> p u c i e", u=2, e=2, i=RUN),
+            )
+
+        def turn_w(a, turned):
+            turn_w_pairs(a, turned)
+            keep_w(a, turned, nc.scalar.copy)
+
+        def turn_w_pairs(a, turned):
+            for place in range(PACK):
+                pairs = w_pairs[2 * a + place // 2][:].rearrange("p u m e -> p u (m e)").bitcast(F32)
+                nc.tensor.transpose(turned[:, place * P : (place + 1) * P], pairs[:, place % 2, :], ident[:])
+
+        def keep_w(a, turned, copy):
+            copy(
+                out=flat(w_slots[a][:]).bitcast(F32).rearrange("m (j p u) -> m j p u", j=2, u=2),
+                in_=turned[:].rearrange("m (j u p) -> m j p u", j=2, u=2),
+            )
+
         for j in range(PACK):
             nc.vector.tensor_copy(w_picked[:, j, :], w_table[j][:].indirect(offsets[:]))
+        pair_w(0, nc.scalar.copy)
+        pair_w(1, nc.scalar.copy)
+        make_factor(0, HELPED * P, P, keep.tile([P, PACK, P], F32, name="factor0", tag="factor0", align_bytes=ALIGN))
+        make_factor(1, 0, SIDE, keep.tile([P, PACK, SIDE], F32, name="factor1"))
+        turn_w(0, banks[0])
+        pair_w(2, nc.scalar.copy)
         w_grouped = {}
 
         def deal_w(q):
@@ -184,45 +212,32 @@ def tile_attend_gnce_wx_ts_kb_kernel(tc, xT, wT, y, wt, ts, kb, xm, offs, out_0,
         x_grouped = [[grouped_tile(f"x_grouped{g}{a}", SIDE) for a in range(2)] for g in range(HALVES)]
         x_mx = [mx_tiles(f"x{g}") for g in range(HALVES)]
         group(nc.scalar.copy, x_grouped[0][0][:], x_raw[0][0][:])
-        make_factor(1, SIDE, SIDE, "x_raw00")
+        late = keep.tile([P, PACK * SIDE + PACK], F32, name="late", tag="x_raw00", align_bytes=ALIGN)
+        kb_slot = late[:, PACK * SIDE :]
+        nc.scalar.activation(out=kb_slot, in_=banks[TURN_BANK + 1][:, 0:N:P], func=ACT.Copy)
+        make_factor(1, SIDE, SIDE, late[:, 0 : PACK * SIDE].rearrange("p (j c) -> p j c", j=PACK))
         w_grouped[0] = grouped_tile("w_grouped0", SIDE)
         deal_w(0)
         deal_w(1)
+        pair_w(PACK - 1, nc.vector.tensor_copy)
         quantize(w_mx, sides[0], w_grouped[0][:], E4M3)
+        turn_w_pairs(1, banks[6])
         group(nc.vector.tensor_copy, x_grouped[0][1][:], x_raw[0][1][:])
         quantize(x_mx[0], sides[0], x_grouped[0][0][:], E4M3)
         quantize(x_mx[0], sides[1], x_grouped[0][1][:], E4M3)
         w_grouped[1] = grouped_tile("w_grouped1", SIDE, "x_raw01")
         deal_w(2)
         deal_w(3)
-        group(nc.scalar.copy, x_grouped[1][0][:], x_raw[1][0][:])
-
-        w_pairs = keep.tile([P, PACK, 2, P, 2], BF16, name="w_pairs", tag="x_grouped01", align_bytes=ALIGN)
-
-        def pair_w(u):
-            nc.vector.tensor_copy(
-                out=w_pairs[:, :, u].rearrange("p j (c i) e -> p j c i e", i=RUN),
-                in_=w_picked[:].rearrange("p j (c u e i) -> p u j c i e", u=2, e=2, i=RUN)[:, u],
-            )
-
-        pair_w(0)
+        w_slots_mx = mx_tiles("w_slots", K_PASS, "x_grouped00")
+        quantize(w_slots_mx, sides[0], w_slots[0][:], E4M3)
         quantize(w_mx, sides[1], w_grouped[1][:], E4M3)
+        w_slots.append(grouped_tile("w_slots1", SIDE, "x_grouped01"))
+        keep_w(1, banks[6], nc.vector.tensor_copy)
+        group(nc.scalar.copy, x_grouped[1][0][:], x_raw[1][0][:])
         group(nc.vector.tensor_copy, x_grouped[1][1][:], x_raw[1][1][:])
-        quantize(x_mx[1], sides[0], x_grouped[1][0][:], E4M3)
-        quantize(x_mx[1], sides[1], x_grouped[1][1][:], E4M3)
-        pair_w(1)
-
-        w_slots = grouped_tile("w_slots")
-        w_slots_mx = mx_tiles("w_slots")
-
-        def turn_w(a, turned):
-            pairs = w_pairs[:].rearrange("p j u m e -> p (j u) (m e)").bitcast(F32)
-            for place in range(PACK):
-                nc.tensor.transpose(turned[:, place * P : (place + 1) * P], pairs[:, PACK * a + place, :], ident[:])
-            nc.scalar.copy(
-                out=flat(w_slots[:, sides[a], :]).bitcast(F32).rearrange("m (j p u) -> m j p u", j=2, u=2),
-                in_=turned[:].rearrange("m (j u p) -> m j p u", j=2, u=2),
-            )
+        for a in range(2):
+            quantize(x_mx[1], sides[a], x_grouped[1][a][:], E4M3)
+        quantize(w_slots_mx, sides[1], w_slots[1][:], E4M3)
 
         h_rows = {}
         h_rows_mx = {1: mx_tiles("h_rows1")}
@@ -237,7 +252,10 @@ def tile_attend_gnce_wx_ts_kb_kernel(tc, xT, wT, y, wt, ts, kb, xm, offs, out_0,
             g, q = units[n]
             scores = banks[q]
             matmul(scores[:], w_mx, slice(q * P, (q + 1) * P), E4M3, x_mx[g], E4M3, True, True)
-            prob = ring.tile([P, PACK, P], F32, name="prob", bufs=6)
+            if n == len(units) - 1:
+                prob = keep.tile([P, PACK, P], F32, name="last_prob", tag="last_prob", align_bytes=ALIGN)
+            else:
+                prob = ring.tile([P, PACK, P], F32, name="prob", bufs=6)
             nc.scalar.activation(
                 out=prob[:],
                 in_=scores[:].rearrange("m (p j) -> m j p", j=PACK),
@@ -277,7 +295,7 @@ def tile_attend_gnce_wx_ts_kb_kernel(tc, xT, wT, y, wt, ts, kb, xm, offs, out_0,
                 for c in range(HELPED):
                     h_rows[units[c]] = h_rows["early"][:, c * P : (c + 1) * P, :]
             if n == HELPED:
-                h_rows[g, q] = grouped_tile("h_late", P, "y_raw1")[:]
+                h_rows[g, q] = grouped_tile("h_late", P, "last_prob")[:]
             if n == PACK:
                 h_rows[1] = grouped_tile("h_rows1", K_PASS, "factor0")
                 for c in range(PACK):
@@ -329,8 +347,6 @@ def tile_attend_gnce_wx_ts_kb_kernel(tc, xT, wT, y, wt, ts, kb, xm, offs, out_0,
         for n in range(PACK):
             difference(n)
             turn(n + PACK)
-        turn_w(0, banks[0])
-        turn_w(1, banks[1])
         xm_left = [group_xm(0, g, nc.scalar.copy, 0, SIDE) for g in range(HALVES)]
         for n in range(PACK):
             if n < HELPED:
@@ -344,7 +360,7 @@ def tile_attend_gnce_wx_ts_kb_kernel(tc, xT, wT, y, wt, ts, kb, xm, offs, out_0,
             quantize(h_rows_mx[0], slice(q * P, (q + 1) * P), h_rows[0, q], E5M2)
         turn_h(0, 0, banks[2])
         turn_h(0, 1, banks[3])
-        xm_right = [group_xm(1, 0, nc.scalar.copy, 0, SIDE, "xm_right")]
+        xm_right = [group_xm(1, 0, nc.scalar.copy, 0, SIDE)]
         weigh(5)
         quantize_xm(0, 0, xm_left[0], 0, SIDE)
         weigh(6)
@@ -362,17 +378,21 @@ def tile_attend_gnce_wx_ts_kb_kernel(tc, xT, wT, y, wt, ts, kb, xm, offs, out_0,
 
         dense = {}
 
-        def empty_panel(c, acc, tag=None):
-            dense[c] = keep.tile([P, N], F32, name=f"dense{c}", tag=tag or f"dense{c}", align_bytes=ALIGN)
+        def empty_panel(c, acc, a=0, parts=1, tag=None):
+            share = P // RUN // parts
+            name = f"dense{c}_{a}"
+            dense[c, a] = keep.tile([P, N // parts], F32, name=name, tag=tag or name, align_bytes=ALIGN)
             nc.scalar.copy(
-                out=dense[c][:].rearrange("d (c q i) -> d c q i", q=PACK, i=RUN),
-                in_=acc[:].rearrange("d (q c i) -> d c q i", q=PACK, i=RUN),
+                out=dense[c, a][:].rearrange("d (c q i) -> d c q i", q=PACK, i=RUN),
+                in_=acc[:].rearrange("d (q c i) -> d c q i", q=PACK, i=RUN)[:, a * share : (a + 1) * share],
             )
 
-        def store_panel(c):
+        def scatter(c, a=0, parts=1):
+            share = N // LIST_ROWS // parts
             window = windows[c % WINDOWS]
-            nc.vector.tensor_copy(window[:].indirect(offsets[:]), dense[c][:])
-            nc.sync.dma_start(out=out_0[c * P : (c + 1) * P, :], in_=window[:])
+            nc.vector.tensor_copy(window[:].indirect(offsets[:, a * share : (a + 1) * share]), dense[c, a][:])
+            if a == parts - 1:
+                nc.sync.dma_start(out=out_0[c * P : (c + 1) * P, :], in_=window[:])
 
         def row_gradient(g, u, accs):
             staged = keep.tile([P, 2, D], F32, name=f"staged{g}{u}", tag=f"w_table{2 * g + u}")
@@ -389,35 +409,26 @@ def tile_attend_gnce_wx_ts_kb_kernel(tc, xT, wT, y, wt, ts, kb, xm, offs, out_0,
         empty_panel(0, banks[0])
         for u in range(2):
             quantize(h_slots_mx[0], sides[u], h_slots[0, u][:], E5M2)
-        quantize(w_slots_mx, whole, w_slots[:], E4M3)
-        quantize_xm(1, 0, xm_right[0], 0, SIDE)
-        xm_right.append(grouped_tile("xm11_grouped", SIDE, "xm_right"))
-        nc.gpsimd.tensor_scalar(
-            out=xm_right[1][:],
-            in0=xm_raw[1][1][:].rearrange("p j c -> p c j"),
-            scalar1=1.0,
-            scalar2=0.0,
-            op0=ALU.mult,
-            op1=ALU.add,
-        )
-        store_panel(0)
+        xm_right.append(group_xm(1, 1, nc.vector.tensor_copy, 0, SIDE))
+        for g in range(HALVES):
+            quantize_xm(1, g, xm_right[g], 0, SIDE)
+        scatter(0)
         multiply_panel(1, banks[1])
         row_gradient(0, 0, banks[4:6])
         turn_h(1, 0, banks[0])
         quantize(h_slots_mx[1], sides[0], h_slots[1, 0][:], E5M2)
-        quantize_xm(1, 1, xm_right[1], 0, SIDE)
-        zeroed_window(2 * K_PASS, "xm_right")
+        zeroed_window(2 * K_PASS, "h_slots10")
         turn_pairs(1, 1, banks[4])
-        empty_panel(1, banks[1], "factor0")
-        store_panel(1)
+        empty_panel(1, banks[1], tag="factor0")
+        scatter(1)
         row_gradient(0, 1, banks[6:8])
         part_pairs(1, 1, banks[4])
         multiply_panel(2, banks[2])
         empty_panel(2, banks[2])
         row_gradient(1, 0, [banks[5], banks[0]])
         quantize(h_slots_mx[1], sides[1], h_slots[1, 1][:], E5M2)
-        store_panel(2)
+        scatter(2)
         multiply_panel(3, banks[3])
         empty_panel(3, banks[3])
         row_gradient(1, 1, banks[6:8])
-        store_panel(3)
+        scatter(3)

@@ -83,7 +83,8 @@ def tile_attend_gnce_wx_ts_kb_kernel(tc, xT, wT, y, wt, ts, kb, xm, offs, out_0,
         wt_rows = keep.tile([P, HALVES, 2 * PACK], F32, name="wt_rows")[:, :, 0:PACK]
         nc.scalar.dma_start(out=wt_rows, in_=wt[0].rearrange("(g p j) o -> p g (j o)", g=HALVES, j=PACK))
 
-        x_raw = [[keep.tile([P, PACK, SIDE], F32, name=f"x_raw{g}{a}", tag=f"x_raw{g}{a}", align_bytes=ALIGN) for a in range(2)] for g in range(HALVES)]
+        x_raw = [[keep.tile([P, PACK, SIDE], F32, name=f"x_raw0{a}", tag=f"x_raw0{a}", align_bytes=ALIGN) for a in range(2)]]
+        x_raw.append(keep.tile([P, PACK, K_PASS], F32, name="x_raw1"))
         y_raw = [keep.tile([P, PACK, N], F32, name=f"y_raw{g}", tag=f"y_raw{g}", align_bytes=ALIGN) for g in range(HALVES)]
         xm_raw = [[keep.tile([P, PACK, SIDE], F32, name=f"xm_raw{a}{g}") for g in range(HALVES)] for a in range(2)]
         w_table = [keep.tile([P, T], F32, name=f"w_table{j}", tag=f"w_table{j}") for j in range(PACK)]
@@ -101,8 +102,7 @@ def tile_attend_gnce_wx_ts_kb_kernel(tc, xT, wT, y, wt, ts, kb, xm, offs, out_0,
             (w_table[3][:], w_hbm[3]),
             (x_raw[0][0][:], x_hbm[0][:, :, sides[0]]),
             (x_raw[0][1][:], x_hbm[0][:, :, sides[1]]),
-            (x_raw[1][0][:], x_hbm[1][:, :, sides[0]]),
-            (x_raw[1][1][:], x_hbm[1][:, :, sides[1]]),
+            (x_raw[1][:], x_hbm[1]),
             (y_raw[0][:], y_hbm[0]),
             (y_raw[1][:], y_hbm[1]),
         ]
@@ -232,9 +232,9 @@ def tile_attend_gnce_wx_ts_kb_kernel(tc, xT, wT, y, wt, ts, kb, xm, offs, out_0,
         quantize(w_slots_mx, sides[0], w_slots[0][:], E4M3)
         quantize(w_mx, sides[1], w_grouped[1][:], E4M3)
         w_slots.append(grouped_tile("w_slots1", SIDE, "x_grouped01"))
-        keep_w(1, banks[6], nc.vector.tensor_copy)
-        group(nc.scalar.copy, x_grouped[1][0][:], x_raw[1][0][:])
-        group(nc.vector.tensor_copy, x_grouped[1][1][:], x_raw[1][1][:])
+        keep_w(1, banks[6], nc.scalar.copy)
+        for a in range(2):
+            group(nc.vector.tensor_copy, x_grouped[1][a][:], x_raw[1][:, :, sides[a]])
         for a in range(2):
             quantize(x_mx[1], sides[a], x_grouped[1][a][:], E4M3)
         quantize(w_slots_mx, sides[1], w_slots[1][:], E4M3)

@@ -27,7 +27,18 @@ PANELS = D // P
 LIST_ROWS = 16
 SCORE_BANK = 0
 TURN_BANK = 4
-WINDOWS = 3
+KB = 1024
+PLACES = {
+    "dense0": 0,
+    "h_slots11": 0,
+    "h_slots10": 3 * KB,
+    "dense2": 4 * KB,
+    "h_slots1_codes": 5 * KB,
+    "h_slots0_codes": 10 * KB,
+    "dense1": 10 * KB,
+    "dense3": 10 * KB,
+    "staged10": 8 * KB,
+}
 RING = 3
 ALIGN = 64
 
@@ -37,19 +48,24 @@ def tile_attend_gnce_wx_ts_kb_kernel(tc, xT, wT, y, wt, ts, kb, xm, offs, out_0,
     with ExitStack() as ctx:
         keep = ctx.enter_context(tc.tile_pool(name="keep", bufs=1))
         ring = ctx.enter_context(tc.tile_pool(name="ring", bufs=RING))
+        placed = ctx.enter_context(tc.tile_pool(name="placed", bufs=1))
         psum = ctx.enter_context(tc.psum_pool(name="psum", bufs=1))
 
         banks = [psum.tile([P, K_PASS], F32, name=f"bank{b}") for b in range(8)]
         whole = slice(0, K_PASS)
         sides = [slice(0, SIDE), slice(SIDE, K_PASS)]
 
+        def tile(name, shape, dtype, tag=None):
+            tag = tag or name
+            if tag in PLACES:
+                return placed.tile([P] + shape, dtype, name=name, tag=tag, align_bytes=ALIGN, offset=PLACES[tag])
+            return keep.tile([P] + shape, dtype, name=name, tag=tag, align_bytes=ALIGN)
+
         def mx_tiles(name, columns=K_PASS, tag=None):
-            codes = keep.tile([P, columns], U32, name=name + "_codes", tag=tag or name + "_codes", align_bytes=ALIGN)
-            scales = keep.tile([P, columns], U8, name=name + "_scales", align_bytes=ALIGN)
-            return codes, scales
+            return tile(name + "_codes", [columns], U32, tag), tile(name + "_scales", [columns], U8)
 
         def grouped_tile(name, columns=K_PASS, tag=None):
-            return keep.tile([P, columns, PACK], BF16, name=name, tag=tag or name, align_bytes=ALIGN)
+            return tile(name, [columns, PACK], BF16, tag)
 
         def flat(grouped):
             return grouped.rearrange("p c j -> p (c j)")
@@ -87,7 +103,7 @@ def tile_attend_gnce_wx_ts_kb_kernel(tc, xT, wT, y, wt, ts, kb, xm, offs, out_0,
         x_raw.append(keep.tile([P, PACK, K_PASS], F32, name="x_raw1"))
         y_raw = [keep.tile([P, PACK, N], F32, name=f"y_raw{g}", tag=f"y_raw{g}", align_bytes=ALIGN) for g in range(HALVES)]
         xm_raw = [[keep.tile([P, PACK, SIDE], F32, name=f"xm_raw{a}{g}") for g in range(HALVES)] for a in range(2)]
-        w_table = [keep.tile([P, T], F32, name=f"w_table{j}", tag=f"w_table{j}") for j in range(PACK)]
+        w_table = [tile(f"w_table{j}", [T], F32) for j in range(PACK)]
         x_hbm = xT[0].rearrange("(p j) (g r) -> g p j r", j=PACK, g=HALVES)
         y_hbm = y[0].rearrange("(g p j) i -> g p j i", j=PACK, g=HALVES)
         xm_hbm = xm[0].rearrange("(g p j) d -> g p j d", j=PACK, g=HALVES)
@@ -120,11 +136,11 @@ def tile_attend_gnce_wx_ts_kb_kernel(tc, xT, wT, y, wt, ts, kb, xm, offs, out_0,
 
         def zeroed_window(piece, tag=None):
             name = f"window{len(windows)}"
-            windows.append(keep.tile([P, T], F32, name=name, tag=tag or name, align_bytes=ALIGN))
+            windows.append(tile(name, [T], F32, tag))
             for first in range(0, T, piece):
                 nc.gpsimd.memset(windows[-1][:, first : first + piece], 0.0)
 
-        for c in range(WINDOWS - 1):
+        for c in range(2):
             zeroed_window(K_PASS)
 
         per_slot = []
@@ -198,7 +214,7 @@ def tile_attend_gnce_wx_ts_kb_kernel(tc, xT, wT, y, wt, ts, kb, xm, offs, out_0,
         pair_w(0, nc.scalar.copy)
         pair_w(1, nc.scalar.copy)
         make_factor(0, HELPED * P, P, keep.tile([P, PACK, P], F32, name="factor0", tag="factor0", align_bytes=ALIGN))
-        make_factor(1, 0, SIDE, keep.tile([P, PACK, SIDE], F32, name="factor1"))
+        make_factor(1, 0, SIDE, keep.tile([P, PACK, SIDE], F32, name="factor1", align_bytes=ALIGN))
         turn_w(0, banks[0])
         pair_w(2, nc.scalar.copy)
         w_grouped = {}
@@ -241,7 +257,7 @@ def tile_attend_gnce_wx_ts_kb_kernel(tc, xT, wT, y, wt, ts, kb, xm, offs, out_0,
 
         h_rows = {}
         h_rows_mx = {1: mx_tiles("h_rows1")}
-        h_slots_mx = [mx_tiles(f"h_slots{g}") for g in range(HALVES)]
+        h_slots_mx = [mx_tiles("h_slots0")]
         h_slots = {}
         xm_mx = {}
         units = [(g, q) for g in range(HALVES) for q in range(PACK)]
@@ -319,9 +335,9 @@ def tile_attend_gnce_wx_ts_kb_kernel(tc, xT, wT, y, wt, ts, kb, xm, offs, out_0,
                 pairs = flat(h_rows[g, q]).bitcast(F32)
                 nc.tensor.transpose(turned[:, q * P : (q + 1) * P], pairs[:, u : 2 * P : 2], ident[:])
 
-        def part_pairs(g, u, turned):
-            h_slots[g, u] = grouped_tile(f"h_slots{g}{u}", SIDE)
-            nc.scalar.copy(
+        def part_pairs(g, u, turned, copy=nc.scalar.copy, tag=None):
+            h_slots[g, u] = grouped_tile(f"h_slots{g}{u}", SIDE, tag)
+            copy(
                 out=h_slots[g, u][:].rearrange("m (e p) q -> m e p q", e=2),
                 in_=turned[:].bitcast(BF16).rearrange("m (q p e) -> m e p q", q=PACK, e=2),
             )
@@ -363,6 +379,7 @@ def tile_attend_gnce_wx_ts_kb_kernel(tc, xT, wT, y, wt, ts, kb, xm, offs, out_0,
         xm_right = [group_xm(1, 0, nc.scalar.copy, 0, SIDE)]
         weigh(5)
         quantize_xm(0, 0, xm_left[0], 0, SIDE)
+        quantize(h_slots_mx[0], sides[0], h_slots[0, 0][:], E5M2)
         weigh(6)
         weigh(7)
         quantize_xm(0, 1, xm_left[1], 0, SIDE)
@@ -378,57 +395,76 @@ def tile_attend_gnce_wx_ts_kb_kernel(tc, xT, wT, y, wt, ts, kb, xm, offs, out_0,
 
         dense = {}
 
-        def empty_panel(c, acc, a=0, parts=1, tag=None):
-            share = P // RUN // parts
-            name = f"dense{c}_{a}"
-            dense[c, a] = keep.tile([P, N // parts], F32, name=name, tag=tag or name, align_bytes=ALIGN)
-            nc.scalar.copy(
-                out=dense[c, a][:].rearrange("d (c q i) -> d c q i", q=PACK, i=RUN),
-                in_=acc[:].rearrange("d (q c i) -> d c q i", q=PACK, i=RUN)[:, a * share : (a + 1) * share],
+        def empty_panel(c, acc, copy, tag=None):
+            dense[c] = tile(f"dense{c}", [N], F32, tag)
+            copy(
+                out=dense[c][:].rearrange("d (c q i) -> d c q i", q=PACK, i=RUN),
+                in_=acc[:].rearrange("d (q c i) -> d c q i", q=PACK, i=RUN),
             )
 
-        def scatter(c, a=0, parts=1):
-            share = N // LIST_ROWS // parts
-            window = windows[c % WINDOWS]
-            nc.vector.tensor_copy(window[:].indirect(offsets[:, a * share : (a + 1) * share]), dense[c, a][:])
-            if a == parts - 1:
-                nc.sync.dma_start(out=out_0[c * P : (c + 1) * P, :], in_=window[:])
+        def store_window(c, queue):
+            queue.dma_start(out=out_0[c * P : (c + 1) * P, :], in_=windows[c][:])
 
-        def row_gradient(g, u, accs):
-            staged = keep.tile([P, 2, D], F32, name=f"staged{g}{u}", tag=f"w_table{2 * g + u}")
+        def vector_scatter(c):
+            nc.vector.tensor_copy(windows[c][:].indirect(offsets[:]), dense[c][:])
+            store_window(c, nc.sync)
+
+        def scalar_scatter(c):
+            share = N // LIST_ROWS // 2
+            for a in range(2):
+                listed = windows[c][:].indirect(offsets[:, a * share : (a + 1) * share])
+                nc.scalar.activation(out=listed, in_=dense[c][:, sides[a]], func=ACT.Copy)
+            store_window(c, nc.scalar)
+
+        def multiply_rows(g, u, accs):
             for e in range(2):
                 first = (2 * u + e) * P
                 matmul(accs[e][:], h_slots_mx[g], slice(first, first + P), E5M2, w_slots_mx, E4M3, True, True)
-                nc.scalar.copy(
+
+        def empty_rows(g, u, accs, copy, tag=None):
+            staged = tile(f"staged{g}{u}", [2, D], F32, tag)
+            for e in range(2):
+                copy(
                     out=staged[:, e, :].rearrange("r (p j) -> r p j", j=PACK),
                     in_=accs[e][:].rearrange("r (j p) -> r p j", j=PACK),
                 )
-            nc.scalar.dma_start(out=out_1_hbm[g, u], in_=staged[:])
+            return staged
 
+        def store_rows(g, u, staged, queue):
+            queue.dma_start(out=out_1_hbm[g, u], in_=staged[:])
+
+        on_vector, on_scalar = nc.vector.tensor_copy, nc.scalar.copy
+        multiply_rows(0, 0, banks[4:6])
+        rows = empty_rows(0, 0, banks[4:6], on_scalar, "w_table0")
         multiply_panel(0, banks[0])
-        empty_panel(0, banks[0])
-        for u in range(2):
-            quantize(h_slots_mx[0], sides[u], h_slots[0, u][:], E5M2)
-        xm_right.append(group_xm(1, 1, nc.vector.tensor_copy, 0, SIDE))
+        store_rows(0, 0, rows, nc.scalar)
+        empty_panel(0, banks[0], on_scalar)
+        xm_right.append(group_xm(1, 1, on_vector, 0, SIDE, "factor1"))
+        quantize(h_slots_mx[0], sides[1], h_slots[0, 1][:], E5M2)
         for g in range(HALVES):
             quantize_xm(1, g, xm_right[g], 0, SIDE)
-        scatter(0)
+        multiply_rows(0, 1, banks[6:8])
         multiply_panel(1, banks[1])
-        row_gradient(0, 0, banks[4:6])
-        turn_h(1, 0, banks[0])
-        quantize(h_slots_mx[1], sides[0], h_slots[1, 0][:], E5M2)
-        zeroed_window(2 * K_PASS, "h_slots10")
-        turn_pairs(1, 1, banks[4])
-        empty_panel(1, banks[1], tag="factor0")
-        scatter(1)
-        row_gradient(0, 1, banks[6:8])
-        part_pairs(1, 1, banks[4])
+        vector_scatter(0)
+        zeroed_window(2 * K_PASS, "factor1")
+        windows.append(windows[0])
         multiply_panel(2, banks[2])
-        empty_panel(2, banks[2])
-        row_gradient(1, 0, [banks[5], banks[0]])
-        quantize(h_slots_mx[1], sides[1], h_slots[1, 1][:], E5M2)
-        scatter(2)
         multiply_panel(3, banks[3])
-        empty_panel(3, banks[3])
-        row_gradient(1, 1, banks[6:8])
-        scatter(3)
+        turn_pairs(1, 1, banks[0])
+        store_rows(0, 1, empty_rows(0, 1, banks[6:8], on_scalar, "w_table1"), nc.scalar)
+        empty_panel(1, banks[1], on_scalar)
+        turn_pairs(1, 0, banks[1])
+        empty_panel(2, banks[2], on_scalar)
+        scalar_scatter(1)
+        part_pairs(1, 1, banks[0], on_vector)
+        vector_scatter(2)
+        empty_panel(3, banks[3], on_scalar)
+        scalar_scatter(3)
+        h_slots_mx.append(mx_tiles("h_slots1"))
+        quantize(h_slots_mx[1], sides[1], h_slots[1, 1][:], E5M2)
+        part_pairs(1, 0, banks[1], on_vector)
+        multiply_rows(1, 1, banks[6:8])
+        quantize(h_slots_mx[1], sides[0], h_slots[1, 0][:], E5M2)
+        multiply_rows(1, 0, banks[4:6])
+        store_rows(1, 1, empty_rows(1, 1, banks[6:8], on_vector, "w_table2"), nc.sync)
+        store_rows(1, 0, empty_rows(1, 0, banks[4:6], on_scalar), nc.scalar)

@@ -38,6 +38,9 @@ PLACES = {
     "dense1": 10 * KB,
     "dense3": 10 * KB,
     "staged10": 8 * KB,
+    "window2": 12 * KB,
+    "factor1": 19 * KB,
+    "window3": 20 * KB,
 }
 RING = 3
 ALIGN = 64
@@ -214,7 +217,7 @@ def tile_attend_gnce_wx_ts_kb_kernel(tc, xT, wT, y, wt, ts, kb, xm, offs, out_0,
         pair_w(0, nc.scalar.copy)
         pair_w(1, nc.scalar.copy)
         make_factor(0, HELPED * P, P, keep.tile([P, PACK, P], F32, name="factor0", tag="factor0", align_bytes=ALIGN))
-        make_factor(1, 0, SIDE, keep.tile([P, PACK, SIDE], F32, name="factor1", align_bytes=ALIGN))
+        make_factor(1, 0, SIDE, tile("factor1", [PACK, SIDE], F32))
         turn_w(0, banks[0])
         pair_w(2, nc.scalar.copy)
         w_grouped = {}
@@ -409,12 +412,12 @@ def tile_attend_gnce_wx_ts_kb_kernel(tc, xT, wT, y, wt, ts, kb, xm, offs, out_0,
             nc.vector.tensor_copy(windows[c][:].indirect(offsets[:]), dense[c][:])
             store_window(c, nc.sync)
 
-        def scalar_scatter(c):
+        def scalar_scatter(c, a):
             share = N // LIST_ROWS // 2
-            for a in range(2):
-                listed = windows[c][:].indirect(offsets[:, a * share : (a + 1) * share])
-                nc.scalar.activation(out=listed, in_=dense[c][:, sides[a]], func=ACT.Copy)
-            store_window(c, nc.scalar)
+            listed = windows[c][:].indirect(offsets[:, a * share : (a + 1) * share])
+            nc.scalar.activation(out=listed, in_=dense[c][:, sides[a]], func=ACT.Copy)
+            if a == 1:
+                store_window(c, nc.scalar)
 
         def multiply_rows(g, u, accs):
             for e in range(2):
@@ -439,27 +442,29 @@ def tile_attend_gnce_wx_ts_kb_kernel(tc, xT, wT, y, wt, ts, kb, xm, offs, out_0,
         multiply_panel(0, banks[0])
         store_rows(0, 0, rows, nc.scalar)
         empty_panel(0, banks[0], on_scalar)
-        xm_right.append(group_xm(1, 1, on_vector, 0, SIDE, "factor1"))
         quantize(h_slots_mx[0], sides[1], h_slots[0, 1][:], E5M2)
+        xm_right.append(group_xm(1, 1, on_vector, 0, SIDE, "factor1"))
         for g in range(HALVES):
             quantize_xm(1, g, xm_right[g], 0, SIDE)
         multiply_rows(0, 1, banks[6:8])
         multiply_panel(1, banks[1])
         vector_scatter(0)
-        zeroed_window(2 * K_PASS, "factor1")
-        windows.append(windows[0])
+        for c in range(2):
+            zeroed_window(2 * K_PASS)
         multiply_panel(2, banks[2])
         multiply_panel(3, banks[3])
         turn_pairs(1, 1, banks[0])
         store_rows(0, 1, empty_rows(0, 1, banks[6:8], on_scalar, "w_table1"), nc.scalar)
         empty_panel(1, banks[1], on_scalar)
         turn_pairs(1, 0, banks[1])
+        scalar_scatter(1, 0)
         empty_panel(2, banks[2], on_scalar)
-        scalar_scatter(1)
+        scalar_scatter(1, 1)
         part_pairs(1, 1, banks[0], on_vector)
         vector_scatter(2)
         empty_panel(3, banks[3], on_scalar)
-        scalar_scatter(3)
+        scalar_scatter(3, 0)
+        scalar_scatter(3, 1)
         h_slots_mx.append(mx_tiles("h_slots1"))
         quantize(h_slots_mx[1], sides[1], h_slots[1, 1][:], E5M2)
         part_pairs(1, 0, banks[1], on_vector)

from contextlib import ExitStack

import concourse.mybir as mybir
from concourse.masks import make_identity

N, T, D, R = 512, 2048, 512, 1024
FLOPS = 3 * 2 * R * D * N

F32 = mybir.dt.float32
BF16 = mybir.dt.bfloat16
U32 = mybir.dt.uint32
U16 = mybir.dt.uint16
U8 = mybir.dt.uint8
E4M3 = mybir.dt.float8_e4m3fn_x4
E5M2 = mybir.dt.float8_e5m2_x4
ACT = mybir.ActivationFunctionType
ALU = mybir.AluOpType

P = 128
PACK = 4
HELPED = 3
RUN = 4
K_PASS = P * PACK
SIDE = K_PASS // 2
HALVES = R // K_PASS
PANELS = D // P
LIST_ROWS = 16
SCORE_BANK = 0
TURN_BANK = 4
KB = 1024
PLACES = {
    "dense0": 0,
    "h_slots11": 0,
    "h_slots10": 3 * KB,
    "dense2": 4 * KB,
    "h_slots1_codes": 5 * KB,
    "h_slots0_codes": 10 * KB,
    "dense1": 10 * KB,
    "dense3": 10 * KB,
    "staged10": 8 * KB,
    "window2": 12 * KB,
    "factor1": 19 * KB,
    "window3": 20 * KB,
}
RING = 3
ALIGN = 64


def tile_attend_gnce_wx_ts_kb_kernel(tc, xT, wT, y, wt, ts, kb, xm, offs, out_0, out_1):
    nc = tc.nc
    with ExitStack() as ctx:
        keep = ctx.enter_context(tc.tile_pool(name="keep", bufs=1))
        ring = ctx.enter_context(tc.tile_pool(name="ring", bufs=RING))
        placed = ctx.enter_context(tc.tile_pool(name="placed", bufs=1))
        psum = ctx.enter_context(tc.psum_pool(name="psum", bufs=1))

        banks = [psum.tile([P, K_PASS], F32, name=f"bank{b}") for b in range(8)]
        whole = slice(0, K_PASS)
        sides = [slice(0, SIDE), slice(SIDE, K_PASS)]

        def tile(name, shape, dtype, tag=None):
            tag = tag or name
            if tag in PLACES:
                return placed.tile([P] + shape, dtype, name=name, tag=tag, align_bytes=ALIGN, offset=PLACES[tag])
            return keep.tile([P] + shape, dtype, name=name, tag=tag, align_bytes=ALIGN)

        def mx_tiles(name, columns=K_PASS, tag=None):
            return tile(name + "_codes", [columns], U32, tag), tile(name + "_scales", [columns], U8)

        def grouped_tile(name, columns=K_PASS, tag=None):
            return tile(name, [columns, PACK], BF16, tag)

        def flat(grouped):
            return grouped.rearrange("p c j -> p (c j)")

        def quantize(mx, cols, grouped, fmt):
            codes, scales = mx
            nc.vector.quantize_mx(out=codes[:, cols].bitcast(fmt), scales=scales[:, cols], in_=flat(grouped))

        def matmul(out, lhs, lhs_cols, lhs_fmt, rhs, rhs_fmt, start, stop):
            nc.tensor.matmul_mx(
                out=out,
                lhsT=lhs[0][:, lhs_cols].bitcast(lhs_fmt),
                lhsT_scale=lhs[1][:, lhs_cols],
                rhs=rhs[0][:].bitcast(rhs_fmt),
                rhs_scale=rhs[1][:],
                start=start,
                stop=stop,
            )

        def group(copy, grouped, raw):
            copy(
                out=grouped.rearrange("p (c i) j -> p c j i", i=4),
                in_=raw.rearrange("p j (c i) -> p c j i", i=4),
            )

        offsets = keep.tile([P, N // LIST_ROWS], U16, name="offsets")
        ts_table = keep.tile([P, T], F32, name="ts_table", tag="ts_table", align_bytes=ALIGN)
        kb_table = keep.tile([P, T], F32, name="kb_table", tag="kb_table", align_bytes=ALIGN)
        for table in (ts_table, kb_table):
            nc.vector.memset(table[:], 0.0)
        wt_rows = keep.tile([P, HALVES, 2 * PACK], F32, name="wt_rows")[:, :, 0:PACK]
        nc.scalar.dma_start(out=wt_rows, in_=wt[0].rearrange("(g p j) o -> p g (j o)", g=HALVES, j=PACK))

        x_raw = [[keep.tile([P, PACK, SIDE], F32, name=f"x_raw0{a}", tag=f"x_raw0{a}", align_bytes=ALIGN) for a in range(2)]]
        x_raw.append(keep.tile([P, PACK, K_PASS], F32, name="x_raw1"))
        y_raw = [keep.tile([P, PACK, N], F32, name=f"y_raw{g}", tag=f"y_raw{g}", align_bytes=ALIGN) for g in range(HALVES)]
        xm_raw = [[keep.tile([P, PACK, SIDE], F32, name=f"xm_raw{a}{g}") for g in range(HALVES)] for a in range(2)]
        w_table = [tile(f"w_table{j}", [T], F32) for j in range(PACK)]
        x_hbm = xT[0].rearrange("(p j) (g r) -> g p j r", j=PACK, g=HALVES)
        y_hbm = y[0].rearrange("(g p j) i -> g p j i", j=PACK, g=HALVES)
        xm_hbm = xm[0].rearrange("(g p j) d -> g p j d", j=PACK, g=HALVES)
        w_hbm = wT.rearrange("(p j) t -> j p t", j=PACK)
        nc.sync.dma_start(out=w_table[0][:], in_=w_hbm[0])
        nc.sync.dma_start(offsets[:], offs)
        loads = [
            (ts_table[0:1, :], ts[0:1, :]),
            (w_table[1][:], w_hbm[1]),
            (kb_table[0:1, :], kb[0:1, :]),
            (w_table[2][:], w_hbm[2]),
            (w_table[3][:], w_hbm[3]),
            (x_raw[0][0][:], x_hbm[0][:, :, sides[0]]),
            (x_raw[0][1][:], x_hbm[0][:, :, sides[1]]),
            (x_raw[1][:], x_hbm[1]),
            (y_raw[0][:], y_hbm[0]),
            (y_raw[1][:], y_hbm[1]),
        ]
        loads.extend((xm_raw[a][g][:], xm_hbm[g][:, :, sides[a]]) for a in range(2) for g in range(HALVES))
        for dest, source in loads:
            nc.sync.dma_start(out=dest, in_=source)

        ident = keep.tile([P, P], F32, name="ident")
        make_identity(nc, ident[:])

        warm = keep.tile([P, 1], F32, name="warm")
        nc.scalar.activation(out=warm[:], in_=ident[:, 0:1], func=ACT.Sigmoid)

        windows = []

        def zeroed_window(piece, tag=None):
            name = f"window{len(windows)}"
            windows.append(tile(name, [T], F32, tag))
            for first in range(0, T, piece):
                nc.gpsimd.memset(windows[-1][:, first : first + piece], 0.0)

        for c in range(2):
            zeroed_window(K_PASS)

        per_slot = []
        for n, (name, table) in enumerate((("ts", ts_table), ("kb", kb_table))):
            dealt = keep.tile([P, N], F32, name=name + "_dealt", tag=name + "_dealt", align_bytes=ALIGN)
            nc.vector.tensor_copy(
                dealt[:].bitcast(U32).rearrange("p (q c i) -> p c q i", q=PACK, i=RUN),
                table[:].bitcast(U32).indirect(offsets[:]),
            )
            turned = banks[TURN_BANK + n]
            for q in range(PACK):
                nc.tensor.transpose(turned[:, q * P : (q + 1) * P], dealt[:, q * P : (q + 1) * P], ident[:])
            if n == 0:
                ts_slot = keep.tile([P, PACK], F32, name="ts_slot")
                nc.scalar.activation(out=ts_slot[:], in_=turned[:, 0:N:P], func=ACT.Copy)
                spread = keep.tile([P, PACK], F32, name="ts_spread", tag="ts_spread", align_bytes=ALIGN)
                nc.scalar.activation(out=spread[:], in_=turned[:, 0:N:P], func=ACT.Copy)
                ts_free = banks[TURN_BANK + 3]
                for q in range(PACK):
                    repeated = spread[:, q : q + 1].to_broadcast([P, P])
                    nc.tensor.transpose(ts_free[:, q * P : (q + 1) * P], repeated, ident[:])

        factor = {}

        def make_factor(g, first, width, tile):
            for j in range(PACK):
                nc.scalar.activation(out=tile[:, j, :], in_=ts_free[:, first : first + width], func=ACT.Copy, scale=wt_rows[:, g, j : j + 1])
            for q in range(first // P, (first + width) // P):
                factor[g, q] = tile[:, :, q * P - first : (q + 1) * P - first]

        ts_kept = keep.tile([P, HELPED * P], F32, name="ts_kept")
        nc.scalar.copy(out=ts_kept[:, 0:P], in_=ts_free[:, 0:P])
        nc.scalar.copy(out=ts_kept[:, P:], in_=ts_free[:, P : HELPED * P])
        for q in range(HELPED):
            factor[0, q] = keep.tile([P, P, PACK], F32, name=f"woven_factor{q}", tag=f"woven_factor{q}", align_bytes=ALIGN)
            nc.gpsimd.tensor_tensor(
                out=factor[0, q][:],
                in0=ts_kept[:, q * P : (q + 1) * P].unsqueeze(2).to_broadcast([P, P, PACK]),
                in1=wt_rows[:, 0, :].unsqueeze(1).to_broadcast([P, P, PACK]),
                op=ALU.mult,
            )

        w_picked = keep.tile([P, PACK, N], F32, name="w_picked", tag="ts_table", align_bytes=ALIGN)
        w_mx = mx_tiles("w")
        w_pairs = [keep.tile([P, 2, P, 2], BF16, name=f"w_pairs{j}", tag=tag, align_bytes=ALIGN) for j, tag in enumerate(("ts_dealt", "ts_spread", "w_pairs2", "w_pairs3"))]
        w_slots = [grouped_tile("w_slots0", SIDE)]

        def pair_w(j, copy):
            copy(
                out=w_pairs[j][:].rearrange("p u (c i) e -> p u c i e", i=RUN),
                in_=w_picked[:, j, :].rearrange("p (c u e i) -> p u c i e", u=2, e=2, i=RUN),
            )

        def turn_w(a, turned):
            turn_w_pairs(a, turned)
            keep_w(a, turned, nc.scalar.copy)

        def turn_w_pairs(a, turned):
            for place in range(PACK):
                pairs = w_pairs[2 * a + place // 2][:].rearrange("p u m e -> p u (m e)").bitcast(F32)
                nc.tensor.transpose(turned[:, place * P : (place + 1) * P], pairs[:, place % 2, :], ident[:])

        def keep_w(a, turned, copy):
            copy(
                out=flat(w_slots[a][:]).bitcast(F32).rearrange("m (j p u) -> m j p u", j=2, u=2),
                in_=turned[:].rearrange("m (j u p) -> m j p u", j=2, u=2),
            )

        for j in range(PACK):
            nc.vector.tensor_copy(w_picked[:, j, :], w_table[j][:].indirect(offsets[:]))
        pair_w(0, nc.scalar.copy)
        pair_w(1, nc.scalar.copy)
        make_factor(0, HELPED * P, P, keep.tile([P, PACK, P], F32, name="factor0", tag="factor0", align_bytes=ALIGN))
        make_factor(1, 0, SIDE, tile("factor1", [PACK, SIDE], F32))
        turn_w(0, banks[0])
        pair_w(2, nc.scalar.copy)
        w_grouped = {}

        def deal_w(q):
            nc.vector.tensor_copy(
                out=w_grouped[q // 2][:, q % 2 * P : (q % 2 + 1) * P, :].rearrange("p (c i) j -> p c j i", i=RUN),
                in_=w_picked[:].rearrange("p j (c q i) -> p q c j i", q=PACK, i=RUN)[:, q],
            )

        x_grouped = [[grouped_tile(f"x_grouped{g}{a}", SIDE) for a in range(2)] for g in range(HALVES)]
        x_mx = [mx_tiles(f"x{g}") for g in range(HALVES)]
        group(nc.scalar.copy, x_grouped[0][0][:], x_raw[0][0][:])
        late = keep.tile([P, PACK * SIDE + PACK], F32, name="late", tag="x_raw00", align_bytes=ALIGN)
        kb_slot = late[:, PACK * SIDE :]
        nc.scalar.activation(out=kb_slot, in_=banks[TURN_BANK + 1][:, 0:N:P], func=ACT.Copy)
        make_factor(1, SIDE, SIDE, late[:, 0 : PACK * SIDE].rearrange("p (j c) -> p j c", j=PACK))
        w_grouped[0] = grouped_tile("w_grouped0", SIDE)
        deal_w(0)
        deal_w(1)
        pair_w(PACK - 1, nc.vector.tensor_copy)
        quantize(w_mx, sides[0], w_grouped[0][:], E4M3)
        turn_w_pairs(1, banks[6])
        group(nc.vector.tensor_copy, x_grouped[0][1][:], x_raw[0][1][:])
        quantize(x_mx[0], sides[0], x_grouped[0][0][:], E4M3)
        quantize(x_mx[0], sides[1], x_grouped[0][1][:], E4M3)
        w_grouped[1] = grouped_tile("w_grouped1", SIDE, "x_raw01")
        deal_w(2)
        deal_w(3)
        w_slots_mx = mx_tiles("w_slots", K_PASS, "x_grouped00")
        quantize(w_slots_mx, sides[0], w_slots[0][:], E4M3)
        quantize(w_mx, sides[1], w_grouped[1][:], E4M3)
        w_slots.append(grouped_tile("w_slots1", SIDE, "x_grouped01"))
        keep_w(1, banks[6], nc.scalar.copy)
        for a in range(2):
            group(nc.vector.tensor_copy, x_grouped[1][a][:], x_raw[1][:, :, sides[a]])
        for a in range(2):
            quantize(x_mx[1], sides[a], x_grouped[1][a][:], E4M3)
        quantize(w_slots_mx, sides[1], w_slots[1][:], E4M3)

        h_rows = {}
        h_rows_mx = {1: mx_tiles("h_rows1")}
        h_slots_mx = [mx_tiles("h_slots0")]
        h_slots = {}
        xm_mx = {}
        units = [(g, q) for g in range(HALVES) for q in range(PACK)]
        diffs = {}
        probs = {}

        def score(n):
            g, q = units[n]
            scores = banks[q]
            matmul(scores[:], w_mx, slice(q * P, (q + 1) * P), E4M3, x_mx[g], E4M3, True, True)
            if n == len(units) - 1:
                prob = keep.tile([P, PACK, P], F32, name="last_prob", tag="last_prob", align_bytes=ALIGN)
            else:
                prob = ring.tile([P, PACK, P], F32, name="prob", bufs=6)
            nc.scalar.activation(
                out=prob[:],
                in_=scores[:].rearrange("m (p j) -> m j p", j=PACK),
                func=ACT.Sigmoid,
                bias=kb_slot[:, q : q + 1],
                scale=ts_slot[:, q : q + 1],
            )
            probs[n] = prob

        def turn(n):
            for j in range(PACK):
                nc.tensor.transpose(banks[TURN_BANK + n % PACK][:, j * P : (j + 1) * P], probs[n][:, j, :], ident[:])

        def difference(n):
            g, q = units[n]
            if n < HELPED:
                diffs[n] = keep.tile([P, P, PACK], F32, name=f"diff{n}", tag=f"diff{n}", align_bytes=ALIGN)
                nc.vector.tensor_tensor(
                    out=diffs[n][:].rearrange("p (c i) j -> p c j i", i=RUN),
                    in0=banks[TURN_BANK + q][:].rearrange("p (j c i) -> p c j i", j=PACK, i=RUN),
                    in1=y_raw[g][:].rearrange("p j (c q i) -> p q c j i", q=PACK, i=RUN)[:, q],
                    op=ALU.subtract,
                )
                return
            diffs[n] = keep.tile([P, PACK, P], F32, name=f"diff{n}", tag=f"diff{n}", align_bytes=ALIGN)
            nc.vector.tensor_tensor(
                out=diffs[n][:].rearrange("p j (c i) -> p j c i", i=RUN),
                in0=banks[TURN_BANK + q][:].rearrange("p (j c i) -> p j c i", j=PACK, i=RUN),
                in1=y_raw[g][:].rearrange("p j (c q i) -> p q j c i", q=PACK, i=RUN)[:, q],
                op=ALU.subtract,
            )

        def weigh(n):
            g, q = units[n]
            if n == 0:
                h_rows["early"] = grouped_tile("h_early", HELPED * P)
                for c in range(HELPED):
                    h_rows[units[c]] = h_rows["early"][:, c * P : (c + 1) * P, :]
            if n == HELPED:
                h_rows[g, q] = grouped_tile("h_late", P, "last_prob")[:]
            if n == PACK:
                h_rows[1] = grouped_tile("h_rows1", K_PASS, "factor0")
                for c in range(PACK):
                    h_rows[1, c] = h_rows[1][:, c * P : (c + 1) * P, :]
            if n < HELPED:
                nc.gpsimd.tensor_tensor(out=h_rows[g, q], in0=diffs[n][:], in1=factor[g, q][:], op=ALU.mult)
                return
            nc.vector.tensor_tensor(
                out=h_rows[g, q].rearrange("p (c i) j -> p c j i", i=2),
                in0=diffs[n][:].rearrange("p j (c i) -> p c j i", i=2),
                in1=factor[g, q].rearrange("p j (c i) -> p c j i", i=2),
                op=ALU.mult,
            )

        def turn_h(g, u, turned):
            turn_pairs(g, u, turned)
            part_pairs(g, u, turned)

        def turn_pairs(g, u, turned):
            for q in range(PACK):
                pairs = flat(h_rows[g, q]).bitcast(F32)
                nc.tensor.transpose(turned[:, q * P : (q + 1) * P], pairs[:, u : 2 * P : 2], ident[:])

        def part_pairs(g, u, turned, copy=nc.scalar.copy, tag=None):
            h_slots[g, u] = grouped_tile(f"h_slots{g}{u}", SIDE, tag)
            copy(
                out=h_slots[g, u][:].rearrange("m (e p) q -> m e p q", e=2),
                in_=turned[:].bitcast(BF16).rearrange("m (q p e) -> m e p q", q=PACK, e=2),
            )

        def group_xm(a, g, copy, first, width, tag=None):
            grouped = grouped_tile(f"xm{a}{g}_{first}_grouped", width, tag)
            group(copy, grouped[:], xm_raw[a][g][:, :, first : first + width])
            return grouped

        def quantize_xm(a, g, grouped, first, width):
            mx = mx_tiles(f"xm_half{g}_panel{2 * a + first // P}", width)
            quantize(mx, slice(0, width), grouped[:], E4M3)
            for c in range(width // P):
                xm_mx[g, 2 * a + first // P + c] = (mx, slice(c * P, (c + 1) * P))

        for n in range(PACK):
            score(n)
        for a in range(2):
            turn(2 * a)
            turn(2 * a + 1)
            score(PACK + 2 * a)
            score(PACK + 2 * a + 1)
        for n in range(PACK):
            difference(n)
            turn(n + PACK)
        xm_left = [group_xm(0, g, nc.scalar.copy, 0, SIDE) for g in range(HALVES)]
        for n in range(PACK):
            if n < HELPED:
                weigh(n)
            difference(n + PACK)
        weigh(3)
        h_rows_mx[0] = mx_tiles("h_rows0", K_PASS, f"diff{HELPED}")
        quantize(h_rows_mx[0], sides[0], h_rows["early"][:, sides[0], :], E5M2)
        weigh(4)
        for q in range(2, PACK):
            quantize(h_rows_mx[0], slice(q * P, (q + 1) * P), h_rows[0, q], E5M2)
        turn_h(0, 0, banks[2])
        turn_h(0, 1, banks[3])
        xm_right = [group_xm(1, 0, nc.scalar.copy, 0, SIDE)]
        weigh(5)
        quantize_xm(0, 0, xm_left[0], 0, SIDE)
        quantize(h_slots_mx[0], sides[0], h_slots[0, 0][:], E5M2)
        weigh(6)
        weigh(7)
        quantize_xm(0, 1, xm_left[1], 0, SIDE)
        for side in sides:
            quantize(h_rows_mx[1], side, h_rows[1][:, side, :], E5M2)

        out_1_hbm = out_1[0].rearrange("(g p u e) d -> g u p e d", g=HALVES, u=2, e=2)

        def multiply_panel(c, acc):
            for g in range(HALVES):
                mx, cols = xm_mx[g, c]
                matmul(acc[:], mx, cols, E4M3, h_rows_mx[g], E5M2, g == 0, g == HALVES - 1)

        dense = {}

        def empty_panel(c, acc, copy, tag=None):
            dense[c] = tile(f"dense{c}", [N], F32, tag)
            copy(
                out=dense[c][:].rearrange("d (c q i) -> d c q i", q=PACK, i=RUN),
                in_=acc[:].rearrange("d (q c i) -> d c q i", q=PACK, i=RUN),
            )

        def store_window(c, queue):
            queue.dma_start(out=out_0[c * P : (c + 1) * P, :], in_=windows[c][:])

        def vector_scatter(c):
            nc.vector.tensor_copy(windows[c][:].indirect(offsets[:]), dense[c][:])
            store_window(c, nc.sync)

        def scalar_scatter(c, a):
            share = N // LIST_ROWS // 2
            listed = windows[c][:].indirect(offsets[:, a * share : (a + 1) * share])
            nc.scalar.activation(out=listed, in_=dense[c][:, sides[a]], func=ACT.Copy)
            if a == 1:
                store_window(c, nc.scalar)

        def multiply_rows(g, u, accs):
            for e in range(2):
                first = (2 * u + e) * P
                matmul(accs[e][:], h_slots_mx[g], slice(first, first + P), E5M2, w_slots_mx, E4M3, True, True)

        def empty_rows(g, u, accs, copy, tag=None):
            staged = tile(f"staged{g}{u}", [2, D], F32, tag)
            for e in range(2):
                copy(
                    out=staged[:, e, :].rearrange("r (p j) -> r p j", j=PACK),
                    in_=accs[e][:].rearrange("r (j p) -> r p j", j=PACK),
                )
            return staged

        def store_rows(g, u, staged, queue):
            queue.dma_start(out=out_1_hbm[g, u], in_=staged[:])

        on_vector, on_scalar = nc.vector.tensor_copy, nc.scalar.copy
        multiply_rows(0, 0, banks[4:6])
        rows = empty_rows(0, 0, banks[4:6], on_scalar, "w_table0")
        multiply_panel(0, banks[0])
        store_rows(0, 0, rows, nc.scalar)
        empty_panel(0, banks[0], on_scalar)
        quantize(h_slots_mx[0], sides[1], h_slots[0, 1][:], E5M2)
        xm_right.append(group_xm(1, 1, on_vector, 0, SIDE, "factor1"))
        for g in range(HALVES):
            quantize_xm(1, g, xm_right[g], 0, SIDE)
        multiply_rows(0, 1, banks[6:8])
        multiply_panel(1, banks[1])
        vector_scatter(0)
        for c in range(2):
            zeroed_window(2 * K_PASS)
        multiply_panel(2, banks[2])
        multiply_panel(3, banks[3])
        turn_pairs(1, 1, banks[0])
        store_rows(0, 1, empty_rows(0, 1, banks[6:8], on_scalar, "w_table1"), nc.scalar)
        empty_panel(1, banks[1], on_scalar)
        turn_pairs(1, 0, banks[1])
        scalar_scatter(1, 0)
        empty_panel(2, banks[2], on_scalar)
        scalar_scatter(1, 1)
        part_pairs(1, 1, banks[0], on_vector)
        vector_scatter(2)
        empty_panel(3, banks[3], on_scalar)
        scalar_scatter(3, 0)
        scalar_scatter(3, 1)
        h_slots_mx.append(mx_tiles("h_slots1"))
        quantize(h_slots_mx[1], sides[1], h_slots[1, 1][:], E5M2)
        part_pairs(1, 0, banks[1], on_vector)
        multiply_rows(1, 1, banks[6:8])
        quantize(h_slots_mx[1], sides[0], h_slots[1, 0][:], E5M2)
        multiply_rows(1, 0, banks[4:6])
        store_rows(1, 1, empty_rows(1, 1, banks[6:8], on_vector, "w_table2"), nc.sync)
        store_rows(1, 0, empty_rows(1, 0, banks[4:6], on_scalar), nc.scalar)
